import numpy as np
import ml_dtypes


def mxq(x, axis, fmt="e4m3"):
    dtype, down = {"e4m3": (ml_dtypes.float8_e4m3fn, 7), "e5m2": (ml_dtypes.float8_e5m2, 14)}[fmt]
    v = np.moveaxis(np.asarray(x, np.float32).astype(ml_dtypes.bfloat16).astype(np.float64), axis, -1)
    blocks = v.reshape(v.shape[:-1] + (-1, 32))
    amax = np.abs(blocks).max(-1, keepdims=True)
    byte = np.maximum(np.where(amax > 0, np.frexp(amax)[1] - 1 + 127, 0) - down, 1)
    scale = np.exp2(byte - 127.0)
    codes = (blocks / scale).astype(np.float32).astype(dtype).astype(np.float64)
    return np.moveaxis((codes * scale).reshape(v.shape), -1, axis)


WIDE = False


def mx_kscale(k):
    if not WIDE:
        return np.ones(k)
    levels = np.array([10, -10, 5, -5, 0])
    if k % 512:
        return np.exp2(np.random.permutation(np.resize(levels, k // 32))).repeat(32)
    a = np.empty((k // 512, 16))
    for p in range(k // 512):
        a[p, :8] = np.random.permutation(np.resize(levels, 8))
        for g in range(8):
            far = levels[np.abs(levels - a[p, g]) >= 10]
            a[p, g + 8] = far[np.random.randint(len(far))]
    return np.exp2(a.ravel()).repeat(32)


def f64(x):
    return np.asarray(x).astype(np.float64)


def striped(idx):
    return np.tile(idx.reshape(-1, 16).T, (8, 1)).astype(np.uint16)


def unstriped(offs):
    return offs[:16].T.reshape(-1).astype(np.int64)


def striped8(idx):
    return np.concatenate([x.reshape(-1, 16).T for x in idx]).astype(np.uint16)


def runs(offs, k):
    lists = np.stack([offs[16 * r : 16 * r + 16].T.reshape(-1) for r in range(8)]).astype(np.int64)
    return lists[np.arange(k) % 512 // 64]


def pack_weight(w):
    k, n = w.shape
    w = f64(np.asarray(w, np.float32).astype(ml_dtypes.bfloat16)).reshape(k // 32, 32, n)
    amax = np.abs(w).max(1)
    byte = np.clip(np.where(amax > 0, np.frexp(amax)[1] - 1 + 127 - 7, 1), 1, 254)
    scaled = (w * np.exp2(127.0 - byte)[:, None, :]).reshape(k, n).astype(np.float32)
    words = np.ascontiguousarray(scaled.reshape(k // 512, 128, 4, n).transpose(0, 1, 3, 2)).astype(ml_dtypes.float8_e4m3fn).view(np.uint8)
    return words, np.ascontiguousarray(byte.astype(np.uint8).reshape(k // 512, 16, n))


def unpack_weight(words, scales):
    g, p, n, _ = words.shape
    vals = np.ascontiguousarray(words).view(ml_dtypes.float8_e4m3fn).astype(np.float64) * np.repeat(np.exp2(scales.astype(np.float64) - 127.0), 8, axis=1)[..., None]
    return vals.transpose(0, 1, 3, 2).reshape(g * 512, n)


def sigmoid(v):
    return 1.0 / (1.0 + np.exp(-np.maximum(v, -700.0)))


K, T, S, N = 1024, 2048, 512, 512


def setup_inputs():
    n = np.random.standard_normal
    s = mx_kscale(K)[:, None]
    packed_xT = pack_weight(n((K, T)) * s)
    return {
        "x_words": packed_xT[0],
        "x_scales": packed_xT[1],
        "w1": (n((K, N)) / np.sqrt(K) / s).astype(np.float32),
        "res1": np.random.uniform(0, 1, (N, S)).astype(np.float32),
        "res2": np.random.uniform(0, 1, (N, S)).astype(np.float32),
        "offs": striped(np.random.permutation(T)[:S]),
        "opp1": striped8(np.stack([np.random.permutation(S) for _ in range(8)])),
        "opp2": striped8(np.stack([np.random.permutation(S) for _ in range(8)])),
    }


def reference(x_words, x_scales, w1, res1, res2, offs, opp1, opp2):
    xq = unpack_weight(x_words, x_scales)[:, unstriped(offs)]
    y = mxq(f64(w1), 0, "e4m3").T @ xq
    return y + 0.75 * (f64(res1) - (sigmoid(y - (y[np.arange(N)[:, None], runs(opp1, N)]))) + f64(res2) - (sigmoid(y - (y[np.arange(N)[:, None], runs(opp2, N)]))))

@@ -1,0 +1,229 @@
+from contextlib import ExitStack
+
+import concourse.mybir as mybir
+from concourse.masks import make_identity
+
+K, T, S, N = 1024, 2048, 512, 512
+FLOPS = 2 * K * N * S
+
+F32 = mybir.dt.float32
+BF16 = mybir.dt.bfloat16
+I32 = mybir.dt.int32
+U32 = mybir.dt.uint32
+U16 = mybir.dt.uint16
+U8 = mybir.dt.uint8
+FP8X4 = mybir.dt.float8_e4m3fn_x4
+ALU = mybir.AluOpType
+ACT = mybir.ActivationFunctionType
+
+P = 128
+PACK = 4
+PASSES = K // (P * PACK)
+BLOCKS = N // P
+CHUNKS = S // P
+STEP = 0.75
+SPLIT = 96
+
+
+def tile_picked_elo8_none_p_kernel(
+    tc, x_words, x_scales, w1, res1, res2, offs, opp1, opp2, out
+):
+    nc = tc.nc
+    with ExitStack() as ctx:
+        lists = ctx.enter_context(tc.tile_pool(name="lists", bufs=1))
+        keep = ctx.enter_context(tc.tile_pool(name="keep", bufs=1))
+        psum = ctx.enter_context(tc.psum_pool(name="psum", bufs=1))
+
+        picks = lists.tile([P, S // 16], U16, name="picks")
+        rivals = [lists.tile([P, S // 16], U16, name="rivals%d" % g) for g in range(2)]
+
+        scale_table = keep.tile([P, T], U8, name="scale_table", tag="scale_table", align_bytes=64)
+        nc.gpsimd.memset(scale_table[:].bitcast(I32), 0)
+
+        warm = keep.tile([P, 2], F32, name="warm")
+        nc.vector.memset(warm[:, 0:1], 0.0)
+        nc.scalar.activation(out=warm[:, 1:2], in_=warm[:, 0:1], func=ACT.Sigmoid)
+
+        w_raw = [keep.tile([P, PACK, N], F32, name="w_raw%d" % z) for z in range(PASSES)]
+        word_table = [keep.tile([P, T], I32, name="word_table%d" % z, tag="word_table%d" % z, align_bytes=64) for z in range(PASSES)]
+        w_rows = w1.rearrange("(z p j) m -> z p j m", z=PASSES, j=PACK)
+        nc.sync.dma_start(out=w_raw[0][:], in_=w_rows[0])
+        for q in range(4):
+            nc.sync.dma_start(
+                out=scale_table[32 * q : 32 * q + 4 * PASSES, :].bitcast(I32),
+                in_=x_scales[:, 4 * q : 4 * q + 4, :].bitcast(I32),
+            )
+        nc.sync.dma_start(picks[:], offs)
+        nc.sync.dma_start(out=w_raw[1][:], in_=w_rows[1])
+        for z in range(PASSES):
+            nc.sync.dma_start(
+                out=word_table[z][:], in_=x_words[z].rearrange("p n t -> p (n t)").bitcast(I32)
+            )
+        nc.sync.dma_start(rivals[0][:], opp1)
+        nc.sync.dma_start(rivals[1][:], opp2)
+        results = {}
+        for pair in range(BLOCKS // 2):
+            for g, res in enumerate((res1, res2)):
+                both = keep.tile([P, 2, S], F32, name="res%d_%d" % (g, pair))
+                nc.sync.dma_start(
+                    out=both[:], in_=res.rearrange("(p b) j -> p b j", b=BLOCKS)[:, 2 * pair : 2 * pair + 2, :]
+                )
+                results[g, 2 * pair] = both[:, 0, :]
+                results[g, 2 * pair + 1] = both[:, 1, :]
+
+        ident = keep.tile([P, P], F32, name="ident")
+        make_identity(nc, ident[:])
+
+        windows = [keep.tile([P, 2 * S], F32, name="window%d" % b) for b in range(BLOCKS)]
+        for b in range(BLOCKS):
+            nc.vector.memset(windows[b][:, S:], 0.0)
+
+        half = S // 2
+        grouped = [keep.tile([P, BLOCKS, P, PACK], BF16, name="grouped%d" % z, align_bytes=64) for z in range(PASSES)]
+        dst = [grouped[z][:].rearrange("p b m j -> p m b j") for z in range(PASSES)]
+        src = [w_raw[z][:].rearrange("p j (m b) -> p m b j", b=BLOCKS) for z in range(PASSES)]
+        nc.vector.tensor_copy(out=dst[0][:, P // 2 :], in_=src[0][:, P // 2 :])
+        nc.scalar.copy(out=dst[0][:, : P // 2], in_=src[0][:, : P // 2])
+        nc.scalar.copy(out=dst[1], in_=src[1])
+
+        x_scale = keep.tile([P, S], U8, name="x_scale", align_bytes=64)
+        nc.vector.tensor_copy(x_scale[:], scale_table[:].indirect(picks[:]))
+
+        def quantize(z, codes_tag, scale_tag):
+            codes = keep.tile([P, N], U32, name="w_codes%d" % z, tag=codes_tag, align_bytes=64)
+            scales = keep.tile([P, N], U8, name="w_scale%d" % z, tag=scale_tag, align_bytes=64)
+            nc.vector.quantize_mx(
+                out=codes[:].bitcast(FP8X4), scales=scales[:], in_=grouped[z][:].rearrange("p b m j -> p (b m j)")
+            )
+            return codes, scales
+
+        x_codes = [keep.tile([P, S], U32, name="x_codes%d" % z, align_bytes=64) for z in range(PASSES)]
+        weights = [quantize(0, "w_codes0", "scale_table")]
+        nc.vector.tensor_copy(x_codes[0][:], word_table[0][:].bitcast(U32).indirect(picks[:]))
+        weights.append(quantize(1, "word_table0", "w_scale1"))
+        for h in range(2):
+            nc.vector.tensor_copy(
+                x_codes[1][:, h * half : (h + 1) * half],
+                word_table[1][:].bitcast(U32).indirect(picks[:, h * half // 16 : (h + 1) * half // 16]),
+            )
+
+        def bank(name, number, width=S):
+            return psum.tile([P, width], F32, name=name, tag="bank%d" % number)
+
+        pieces = [(0, 0, half, 0), (0, half, half, 1)] + [(b, 0, S, b + 1) for b in range(1, BLOCKS)]
+        ratings = [bank("rating%d" % k, k, width) for (b, c0, width, k) in pieces]
+
+        def multiply(k, z):
+            b, c0, width, k = pieces[k]
+            cols = slice(b * P, (b + 1) * P)
+            players = slice(c0, c0 + width)
+            nc.tensor.matmul_mx(
+                out=ratings[k][:],
+                lhsT=weights[z][0][:, cols].bitcast(FP8X4),
+                lhsT_scale=weights[z][1][:, cols],
+                rhs=x_codes[z][:, players].bitcast(FP8X4),
+                rhs_scale=x_scale[4 * z :, players],
+                start=(z == 0),
+                stop=(z == PASSES - 1),
+            )
+
+        for z in range(PASSES):
+            for k in range(3):
+                multiply(k, z)
+        for k in range(3, len(pieces)):
+            for z in range(PASSES):
+                multiply(k, z)
+
+        plain = [keep.tile([P, S], F32, name="plain%d" % b) for b in range(BLOCKS)]
+        for b, c0, width, k in pieces:
+            nc.scalar.activation(
+                out=windows[b][:, c0 : c0 + width], in_=ratings[k][:], func=ACT.Copy, scale=1.0 / STEP
+            )
+            if k == 0:
+                nc.scalar.activation(out=plain[0][:, :half], in_=ratings[0][:], func=ACT.Copy, scale=1.0 / STEP)
+        nc.vector.tensor_copy(out=plain[0][:, half:], in_=windows[0][:, half:S])
+        for b in (2, 3):
+            nc.sync.dma_start(out=plain[b][:], in_=windows[b][:, :S])
+
+        last = BLOCKS - 1
+        sum_bank = {0: 5, 1: 6, 2: 0, 3: 7}
+        back_bank = {0: 2, 1: 3, 2: 4, 3: 1}
+        sums, backs, wins = {}, {}, {}
+        out_rows = out.rearrange("(p b) j -> p b j", b=BLOCKS)
+
+        def add_turned(b, values, first, final):
+            for c in range(CHUNKS):
+                cols = slice(c * P, (c + 1) * P)
+                nc.tensor.matmul(
+                    sums[b][:, cols],
+                    values[:, cols],
+                    ident[:],
+                    start=(first and c == 0),
+                    stop=(final and c == CHUNKS - 1),
+                    is_transpose=True,
+                )
+
+        def open_sum(b):
+            sums[b] = bank("sum%d" % b, sum_bank[b])
+            add_turned(b, windows[b], True, False)
+            add_turned(b, results[0, b], False, False)
+            add_turned(b, results[1, b], False, b == last)
+
+        def turn_back(b):
+            turned = keep.tile([P, S], F32, name="turned%d" % b, tag="turned%d" % b)
+            nc.scalar.activation(out=turned[:], in_=sums[b][:], func=ACT.Copy, scale=STEP, bias=-2 * STEP)
+            backs[b] = bank("back%d" % b, back_bank[b])
+            for c in range(CHUNKS):
+                cols = slice(c * P, (c + 1) * P)
+                nc.tensor.transpose(backs[b][:, cols], turned[:, cols], ident[:])
+
+        def duel(b, g, c0=0, width=S):
+            gap = keep.tile([P, width], F32, name="gap%d_%d_%d" % (b, g, c0))
+            nc.vector.tensor_tensor(
+                gap[:],
+                windows[b][:].indirect(rivals[g][:, c0 // 16 : (c0 + width) // 16]),
+                plain[b][:, c0 : c0 + width],
+                ALU.subtract,
+            )
+            if c0 == 0:
+                tag = "second" if g == 1 else ("turned%d" % (b - 2) if b >= 2 else "first%d" % b)
+                wins[b, g] = keep.tile([P, S], F32, name="win%d_%d" % (b, g), tag=tag)
+            nc.scalar.activation(out=wins[b, g][:, c0 : c0 + width], in_=gap[:], func=ACT.Sigmoid, scale=STEP)
+            if b < last:
+                add_turned(b, wins[b, g], False, g == 1)
+
+        def store(b):
+            done = keep.tile([P, S], F32, name="done%d" % b)
+            nc.scalar.copy(out=done[:], in_=backs[b][:])
+            nc.sync.dma_start(out=out_rows[:, b, :], in_=done[:])
+
+        open_sum(0)
+        open_sum(1)
+        duel(0, 0)
+        duel(0, 1)
+        nc.vector.tensor_copy(out=plain[1][:], in_=windows[1][:, :S])
+        open_sum(last)
+        duel(1, 0)
+        turn_back(0)
+        duel(1, 1)
+        store(0)
+        open_sum(2)
+        turn_back(last)
+        duel(2, 0)
+        turn_back(1)
+        duel(2, 1)
+        store(1)
+        duel(last, 0)
+        turn_back(2)
+        duel(last, 1, 0, half)
+        duel(last, 1, half, half)
+        store(2)
+
+        part = keep.tile([P, S], F32, name="part")
+        nc.vector.scalar_tensor_tensor(part[:], wins[last, 0][:], STEP, backs[last][:], ALU.mult, ALU.add)
+        for c0 in (0, half):
+            done = keep.tile([P, half], F32, name="done_last%d" % c0)
+            nc.vector.scalar_tensor_tensor(
+                done[:], wins[last, 1][:, c0 : c0 + half], STEP, part[:, c0 : c0 + half], ALU.mult, ALU.add
+            )
+            nc.sync.dma_start(out=out_rows[:, last, c0 : c0 + half], in_=done[:])

@@ -22,7 +22,6 @@ PASSES = K // (P * PACK)
 BLOCKS = N // P
 CHUNKS = S // P
 STEP = 0.75
-SPLIT = 96
 
 
 def tile_picked_elo8_none_p_kernel(
@@ -62,14 +61,17 @@ def tile_picked_elo8_none_p_kernel(
         nc.sync.dma_start(rivals[0][:], opp1)
         nc.sync.dma_start(rivals[1][:], opp2)
         results = {}
-        for pair in range(BLOCKS // 2):
-            for g, res in enumerate((res1, res2)):
-                both = keep.tile([P, 2, S], F32, name="res%d_%d" % (g, pair))
-                nc.sync.dma_start(
-                    out=both[:], in_=res.rearrange("(p b) j -> p b j", b=BLOCKS)[:, 2 * pair : 2 * pair + 2, :]
-                )
-                results[g, 2 * pair] = both[:, 0, :]
-                results[g, 2 * pair + 1] = both[:, 1, :]
+        res_rows = [res.rearrange("(p b) j -> p b j", b=BLOCKS) for res in (res1, res2)]
+        for g in range(2):
+            both = keep.tile([P, 2, S], F32, name="res%d_early" % g)
+            nc.sync.dma_start(out=both[:], in_=res_rows[g][:, 0:2, :])
+            results[g, 0] = both[:, 0, :]
+            results[g, 1] = both[:, 1, :]
+        for b in (2, 3):
+            for g in range(2):
+                one = keep.tile([P, S], F32, name="res%d_%d" % (g, b), tag="res%d_%d" % (g, b))
+                nc.sync.dma_start(out=one[:], in_=res_rows[g][:, b, :])
+                results[g, b] = one[:]
 
         ident = keep.tile([P, P], F32, name="ident")
         make_identity(nc, ident[:])
@@ -80,10 +82,10 @@ def tile_picked_elo8_none_p_kernel(
 
         half = S // 2
         grouped = [keep.tile([P, BLOCKS, P, PACK], BF16, name="grouped%d" % z, align_bytes=64) for z in range(PASSES)]
-        dst = [grouped[z][:].rearrange("p b m j -> p m b j") for z in range(PASSES)]
-        src = [w_raw[z][:].rearrange("p j (m b) -> p m b j", b=BLOCKS) for z in range(PASSES)]
-        nc.vector.tensor_copy(out=dst[0][:, P // 2 :], in_=src[0][:, P // 2 :])
-        nc.scalar.copy(out=dst[0][:, : P // 2], in_=src[0][:, : P // 2])
+        dst = [grouped[z][:].rearrange("p (u e) m j -> p u m j e", e=2) for z in range(PASSES)]
+        src = [w_raw[z][:].rearrange("p j (m u e) -> p u m j e", u=2, e=2) for z in range(PASSES)]
+        nc.vector.tensor_copy(out=dst[0][:, :, P // 2 :], in_=src[0][:, :, P // 2 :])
+        nc.scalar.copy(out=dst[0][:, :, : P // 2], in_=src[0][:, :, : P // 2])
         nc.scalar.copy(out=dst[1], in_=src[1])
 
         x_scale = keep.tile([P, S], U8, name="x_scale", align_bytes=64)
@@ -111,7 +113,7 @@ def tile_picked_elo8_none_p_kernel(
             return psum.tile([P, width], F32, name=name, tag="bank%d" % number)
 
         pieces = [(0, 0, half, 0), (0, half, half, 1)] + [(b, 0, S, b + 1) for b in range(1, BLOCKS)]
-        ratings = [bank("rating%d" % k, k, width) for (b, c0, width, k) in pieces]
+        ratings = [bank("rating%d" % k, k, width) for (b, c0, width, k) in pieces[:-1]]
 
         def multiply(k, z):
             b, c0, width, k = pieces[k]
@@ -130,25 +132,28 @@ def tile_picked_elo8_none_p_kernel(
         for z in range(PASSES):
             for k in range(3):
                 multiply(k, z)
-        for k in range(3, len(pieces)):
-            for z in range(PASSES):
-                multiply(k, z)
+        for z in range(PASSES):
+            multiply(3, z)
 
-        plain = [keep.tile([P, S], F32, name="plain%d" % b) for b in range(BLOCKS)]
-        for b, c0, width, k in pieces:
-            nc.scalar.activation(
-                out=windows[b][:, c0 : c0 + width], in_=ratings[k][:], func=ACT.Copy, scale=1.0 / STEP
-            )
-            if k == 0:
-                nc.scalar.activation(out=plain[0][:, :half], in_=ratings[0][:], func=ACT.Copy, scale=1.0 / STEP)
-        nc.vector.tensor_copy(out=plain[0][:, half:], in_=windows[0][:, half:S])
-        for b in (2, 3):
-            nc.sync.dma_start(out=plain[b][:], in_=windows[b][:, :S])
+        plain = [keep.tile([P, S], F32, name="plain%d" % b, tag="plain%d" % b) for b in range(BLOCKS)]
 
-        last = BLOCKS - 1
-        sum_bank = {0: 5, 1: 6, 2: 0, 3: 7}
-        back_bank = {0: 2, 1: 3, 2: 4, 3: 1}
-        sums, backs, wins = {}, {}, {}
+        def leave(k, tile):
+            b, c0, width, k = pieces[k]
+            nc.scalar.activation(out=tile[:, c0 : c0 + width], in_=ratings[k][:], func=ACT.Copy, scale=1.0 / STEP)
+
+        leave(0, windows[0])
+        leave(0, plain[0])
+        leave(1, windows[0])
+        leave(1, plain[0])
+        ratings.append(bank("rating4", 0))
+        for z in range(PASSES):
+            multiply(4, z)
+
+        sum_bank = {0: 4, 1: 5, 2: 6, 3: 7}
+        back_bank = {0: 1, 1: 0, 2: 2, 3: 3}
+        late = (2, 3)
+        held = {(1, 0): "gap0_1_0", (1, 1): "gap1_0_0", (2, 0): "win0_1", (2, 1): "gap1_0_0", (3, 0): "turned0", (3, 1): "gap3_0_0"}
+        sums, backs, wins, totals = {}, {}, {}, {}
         out_rows = out.rearrange("(p b) j -> p b j", b=BLOCKS)
 
         def add_turned(b, values, first, final):
@@ -167,18 +172,21 @@ def tile_picked_elo8_none_p_kernel(
             sums[b] = bank("sum%d" % b, sum_bank[b])
             add_turned(b, windows[b], True, False)
             add_turned(b, results[0, b], False, False)
-            add_turned(b, results[1, b], False, b == last)
+            add_turned(b, results[1, b], False, b in late)
+
+        def close_sum(b):
+            totals[b] = keep.tile([P, S], F32, name="turned%d" % b, tag="turned%d" % b)
+            nc.scalar.activation(out=totals[b][:], in_=sums[b][:], func=ACT.Copy, scale=STEP, bias=-2 * STEP)
 
         def turn_back(b):
-            turned = keep.tile([P, S], F32, name="turned%d" % b, tag="turned%d" % b)
-            nc.scalar.activation(out=turned[:], in_=sums[b][:], func=ACT.Copy, scale=STEP, bias=-2 * STEP)
+            turned = totals[b]
             backs[b] = bank("back%d" % b, back_bank[b])
             for c in range(CHUNKS):
                 cols = slice(c * P, (c + 1) * P)
                 nc.tensor.transpose(backs[b][:, cols], turned[:, cols], ident[:])
 
         def duel(b, g, c0=0, width=S):
-            gap = keep.tile([P, width], F32, name="gap%d_%d_%d" % (b, g, c0))
+            gap = keep.tile([P, width], F32, name="gap%d_%d_%d" % (b, g, c0), tag="gap%d_%d_%d" % (b, g, c0))
             nc.vector.tensor_tensor(
                 gap[:],
                 windows[b][:].indirect(rivals[g][:, c0 // 16 : (c0 + width) // 16]),
@@ -186,44 +194,64 @@ def tile_picked_elo8_none_p_kernel(
                 ALU.subtract,
             )
             if c0 == 0:
-                tag = "second" if g == 1 else ("turned%d" % (b - 2) if b >= 2 else "first%d" % b)
-                wins[b, g] = keep.tile([P, S], F32, name="win%d_%d" % (b, g), tag=tag)
+                name = "win%d_%d" % (b, g)
+                wins[b, g] = keep.tile([P, S], F32, name=name, tag=held.get((b, g), name))
             nc.scalar.activation(out=wins[b, g][:, c0 : c0 + width], in_=gap[:], func=ACT.Sigmoid, scale=STEP)
-            if b < last:
-                add_turned(b, wins[b, g], False, g == 1)
+
+        def count(b, g):
+            add_turned(b, wins[b, g], False, g == 1)
 
         def store(b):
             done = keep.tile([P, S], F32, name="done%d" % b)
             nc.scalar.copy(out=done[:], in_=backs[b][:])
-            nc.sync.dma_start(out=out_rows[:, b, :], in_=done[:])
+            nc.scalar.dma_start(out=out_rows[:, b, :], in_=done[:])
 
+        def settle(b, stores):
+            part = keep.tile([P, S], F32, name="part%d" % b)
+            done = keep.tile([P, S], F32, name="done%d" % b)
+            for c0 in (0, half):
+                cols = slice(c0, c0 + half)
+                nc.vector.scalar_tensor_tensor(part[:, cols], wins[b, 0][:, cols], STEP, backs[b][:, cols], ALU.mult, ALU.add)
+            for c0 in (0, half):
+                cols = slice(c0, c0 + half)
+                nc.vector.scalar_tensor_tensor(done[:, cols], wins[b, 1][:, cols], STEP, part[:, cols], ALU.mult, ALU.add)
+            for c0 in range(0, S, S // stores):
+                cols = slice(c0, c0 + S // stores)
+                nc.sync.dma_start(out=out_rows[:, b, cols], in_=done[:, cols])
+
+        leave(1 + 1, windows[1])
+        leave(1 + 1, plain[1])
+        leave(2 + 1, windows[2])
+        nc.sync.dma_start(out=plain[2][:], in_=windows[2][:, :S])
+        duel(0, 0, 0, half)
+        duel(0, 0, half, half)
+        leave(3 + 1, windows[3])
+        nc.sync.dma_start(out=plain[3][:], in_=windows[3][:, :S])
         open_sum(0)
         open_sum(1)
-        duel(0, 0)
-        duel(0, 1)
-        nc.vector.tensor_copy(out=plain[1][:], in_=windows[1][:, :S])
-        open_sum(last)
-        duel(1, 0)
-        turn_back(0)
-        duel(1, 1)
-        store(0)
+        count(0, 0)
         open_sum(2)
-        turn_back(last)
+        duel(0, 1)
+        count(0, 1)
+        duel(1, 0)
+        count(1, 0)
+        open_sum(3)
+        duel(1, 1)
+        count(1, 1)
+        close_sum(2)
+        close_sum(0)
         duel(2, 0)
+        turn_back(2)
+        turn_back(0)
+        close_sum(3)
+        close_sum(1)
+        turn_back(3)
         turn_back(1)
         duel(2, 1)
+        store(0)
+        duel(3, 0)
+        duel(3, 1, 0, half)
+        duel(3, 1, half, half)
         store(1)
-        duel(last, 0)
-        turn_back(2)
-        duel(last, 1, 0, half)
-        duel(last, 1, half, half)
-        store(2)
-
-        part = keep.tile([P, S], F32, name="part")
-        nc.vector.scalar_tensor_tensor(part[:], wins[last, 0][:], STEP, backs[last][:], ALU.mult, ALU.add)
-        for c0 in (0, half):
-            done = keep.tile([P, half], F32, name="done_last%d" % c0)
-            nc.vector.scalar_tensor_tensor(
-                done[:], wins[last, 1][:, c0 : c0 + half], STEP, part[:, c0 : c0 + half], ALU.mult, ALU.add
-            )
-            nc.sync.dma_start(out=out_rows[:, last, c0 : c0 + half], in_=done[:])
+        settle(2, 1)
+        settle(3, 2)

@@ -21,7 +21,13 @@ PACK = 4
 PASSES = K // (P * PACK)
 BLOCKS = N // P
 CHUNKS = S // P
+HALF = S // 2
+STRIPE = 16
+QUADRANTS = 4
+SCALE_ROWS = 4
+GAMES = 2
 STEP = 0.75
+EARLY, LATE = (0, 1), (2, 3)
 
 
 def tile_picked_elo8_none_p_kernel(
@@ -33,45 +39,39 @@ def tile_picked_elo8_none_p_kernel(
         keep = ctx.enter_context(tc.tile_pool(name="keep", bufs=1))
         psum = ctx.enter_context(tc.psum_pool(name="psum", bufs=1))
 
-        picks = lists.tile([P, S // 16], U16, name="picks")
-        rivals = [lists.tile([P, S // 16], U16, name="rivals%d" % g) for g in range(2)]
+        picks = lists.tile([P, S // STRIPE], U16, name="picks")
+        rivals = [lists.tile([P, S // STRIPE], U16, name="rivals%d" % g) for g in range(GAMES)]
 
         scale_table = keep.tile([P, T], U8, name="scale_table", tag="scale_table", align_bytes=64)
-        nc.gpsimd.memset(scale_table[:].bitcast(I32), 0)
+        nc.sync.dma_start(
+            out=scale_table[0:32, :].bitcast(I32), in_=x_scales.rearrange("z r c -> r z c").bitcast(I32)
+        )
+        nc.sync.dma_start(picks[:], offs)
+        nc.gpsimd.memset(scale_table[32:64, :].bitcast(I32), 0)
+        nc.gpsimd.memset(scale_table[64:128, :].bitcast(I32), 0)
+        x_planes = keep.tile([P, PASSES * S], U8, name="x_planes", align_bytes=64)
+        nc.gpsimd.memset(x_planes[:].bitcast(I32), 0)
 
         warm = keep.tile([P, 2], F32, name="warm")
         nc.vector.memset(warm[:, 0:1], 0.0)
         nc.scalar.activation(out=warm[:, 1:2], in_=warm[:, 0:1], func=ACT.Sigmoid)
 
-        w_raw = [keep.tile([P, PACK, N], F32, name="w_raw%d" % z) for z in range(PASSES)]
-        word_table = [keep.tile([P, T], I32, name="word_table%d" % z, tag="word_table%d" % z, align_bytes=64) for z in range(PASSES)]
-        w_rows = w1.rearrange("(z p j) m -> z p j m", z=PASSES, j=PACK)
+        w_raw = [
+            keep.tile([P, PACK, N], F32, name="w_raw%d" % z, tag="w_raw%d" % z, align_bytes=64)
+            for z in range(PASSES)
+        ]
+        w_rows = w1.rearrange("(z p t) m -> z p t m", z=PASSES, t=PACK)
         nc.sync.dma_start(out=w_raw[0][:], in_=w_rows[0])
-        for q in range(4):
-            nc.sync.dma_start(
-                out=scale_table[32 * q : 32 * q + 4 * PASSES, :].bitcast(I32),
-                in_=x_scales[:, 4 * q : 4 * q + 4, :].bitcast(I32),
-            )
-        nc.sync.dma_start(picks[:], offs)
-        nc.sync.dma_start(out=w_raw[1][:], in_=w_rows[1])
-        for z in range(PASSES):
-            nc.sync.dma_start(
-                out=word_table[z][:], in_=x_words[z].rearrange("p n t -> p (n t)").bitcast(I32)
-            )
         nc.sync.dma_start(rivals[0][:], opp1)
         nc.sync.dma_start(rivals[1][:], opp2)
-        results = {}
-        res_rows = [res.rearrange("(p b) j -> p b j", b=BLOCKS) for res in (res1, res2)]
-        for g in range(2):
-            both = keep.tile([P, 2, S], F32, name="res%d_early" % g)
-            nc.sync.dma_start(out=both[:], in_=res_rows[g][:, 0:2, :])
-            results[g, 0] = both[:, 0, :]
-            results[g, 1] = both[:, 1, :]
-        for b in (2, 3):
-            for g in range(2):
-                one = keep.tile([P, S], F32, name="res%d_%d" % (g, b), tag="res%d_%d" % (g, b))
-                nc.sync.dma_start(out=one[:], in_=res_rows[g][:, b, :])
-                results[g, b] = one[:]
+        nc.sync.dma_start(out=w_raw[1][:], in_=w_rows[1])
+
+        def load_words(z, tag):
+            table = keep.tile([P, T], I32, name="word_table%d" % z, tag=tag, align_bytes=64)
+            nc.sync.dma_start(out=table[:], in_=x_words[z].rearrange("p n t -> p (n t)").bitcast(I32))
+            return table
+
+        word_table = [load_words(0, "word_table0")]
 
         ident = keep.tile([P, P], F32, name="ident")
         make_identity(nc, ident[:])
@@ -80,80 +80,94 @@ def tile_picked_elo8_none_p_kernel(
         for b in range(BLOCKS):
             nc.vector.memset(windows[b][:, S:], 0.0)
 
-        half = S // 2
-        grouped = [keep.tile([P, BLOCKS, P, PACK], BF16, name="grouped%d" % z, align_bytes=64) for z in range(PASSES)]
-        dst = [grouped[z][:].rearrange("p (u e) m j -> p u m j e", e=2) for z in range(PASSES)]
-        src = [w_raw[z][:].rearrange("p j (m u e) -> p u m j e", u=2, e=2) for z in range(PASSES)]
-        nc.vector.tensor_copy(out=dst[0][:, :, P // 2 :], in_=src[0][:, :, P // 2 :])
-        nc.scalar.copy(out=dst[0][:, :, : P // 2], in_=src[0][:, :, : P // 2])
-        nc.scalar.copy(out=dst[1], in_=src[1])
-
-        x_scale = keep.tile([P, S], U8, name="x_scale", align_bytes=64)
-        nc.vector.tensor_copy(x_scale[:], scale_table[:].indirect(picks[:]))
-
-        def quantize(z, codes_tag, scale_tag):
-            codes = keep.tile([P, N], U32, name="w_codes%d" % z, tag=codes_tag, align_bytes=64)
-            scales = keep.tile([P, N], U8, name="w_scale%d" % z, tag=scale_tag, align_bytes=64)
-            nc.vector.quantize_mx(
-                out=codes[:].bitcast(FP8X4), scales=scales[:], in_=grouped[z][:].rearrange("p b m j -> p (b m j)")
+        picked_scales = keep.tile([P, S], U8, name="picked_scales", align_bytes=64)
+        nc.vector.tensor_copy(picked_scales[:], scale_table[:].indirect(picks[:]))
+        for q in range(QUADRANTS):
+            rows = PASSES * SCALE_ROWS
+            nc.sync.dma_start(
+                out=x_planes[32 * q : 32 * q + SCALE_ROWS, :].bitcast(I32),
+                in_=picked_scales[rows * q : rows * (q + 1), :].bitcast(I32),
             )
-            return codes, scales
+        word_table.append(load_words(1, "scale_table"))
+
+        grouped = [
+            keep.tile([P, BLOCKS, P, PACK], BF16, name="grouped%d" % z, tag="grouped%d" % z, align_bytes=64)
+            for z in range(PASSES)
+        ]
+        for z in range(PASSES):
+            cast_to = grouped[z][:].rearrange("p (u e) c t -> p u c t e", e=2)
+            cast_from = w_raw[z][:].rearrange("p t (c u e) -> p u c t e", u=2, e=2)
+            nc.vector.tensor_copy(out=cast_to[:, :, P // 2 :], in_=cast_from[:, :, P // 2 :])
+            nc.scalar.copy(out=cast_to[:, :, : P // 2], in_=cast_from[:, :, : P // 2])
 
         x_codes = [keep.tile([P, S], U32, name="x_codes%d" % z, align_bytes=64) for z in range(PASSES)]
-        weights = [quantize(0, "w_codes0", "scale_table")]
-        nc.vector.tensor_copy(x_codes[0][:], word_table[0][:].bitcast(U32).indirect(picks[:]))
-        weights.append(quantize(1, "word_table0", "w_scale1"))
-        for h in range(2):
-            nc.vector.tensor_copy(
-                x_codes[1][:, h * half : (h + 1) * half],
-                word_table[1][:].bitcast(U32).indirect(picks[:, h * half // 16 : (h + 1) * half // 16]),
+        w_codes, w_planes = [], []
+        for z in range(PASSES):
+            w_codes.append(keep.tile([P, N], U32, name="w_codes%d" % z, align_bytes=64))
+            w_planes.append(keep.tile([P, N], U8, name="w_plane%d" % z, align_bytes=64))
+            nc.vector.quantize_mx(
+                out=w_codes[z][:].bitcast(FP8X4),
+                scales=w_planes[z][:],
+                in_=grouped[z][:].rearrange("p b c t -> p (b c t)"),
             )
+
+        nc.vector.tensor_copy(x_codes[0][:], word_table[0][:].bitcast(U32).indirect(picks[:]))
+        for j0 in (0, HALF):
+            nc.vector.tensor_copy(
+                x_codes[1][:, j0 : j0 + HALF],
+                word_table[1][:].bitcast(U32).indirect(picks[:, j0 // STRIPE : (j0 + HALF) // STRIPE]),
+            )
+
+        results = {}
+        res_rows = [res.rearrange("(p b) j -> p b j", b=BLOCKS) for res in (res1, res2)]
+        for z, pair in enumerate((EARLY, LATE)):
+            for g, staging in enumerate(("w_raw%d" % z, "grouped%d" % z)):
+                both = keep.tile([P, 2, S], F32, name="res%d_%d" % (g, z), tag=staging, align_bytes=64)
+                nc.sync.dma_start(out=both[:], in_=res_rows[g][:, pair[0] : pair[1] + 1, :])
+                for i, b in enumerate(pair):
+                    results[g, b] = both[:, i, :]
 
         def bank(name, number, width=S):
             return psum.tile([P, width], F32, name=name, tag="bank%d" % number)
 
-        pieces = [(0, 0, half, 0), (0, half, half, 1)] + [(b, 0, S, b + 1) for b in range(1, BLOCKS)]
-        ratings = [bank("rating%d" % k, k, width) for (b, c0, width, k) in pieces[:-1]]
+        pieces = [(0, 0, HALF), (0, HALF, HALF)] + [(b, 0, S) for b in range(1, BLOCKS)]
+        piece_of = {b: i for i, (b, j0, width) in enumerate(pieces)}
+        ratings = [bank("rating%d" % i, i, pieces[i][2]) for i in range(len(pieces) - 1)]
 
-        def multiply(k, z):
-            b, c0, width, k = pieces[k]
-            cols = slice(b * P, (b + 1) * P)
-            players = slice(c0, c0 + width)
+        def multiply(i, z):
+            b, j0, width = pieces[i]
+            features = slice(b * P, (b + 1) * P)
             nc.tensor.matmul_mx(
-                out=ratings[k][:],
-                lhsT=weights[z][0][:, cols].bitcast(FP8X4),
-                lhsT_scale=weights[z][1][:, cols],
-                rhs=x_codes[z][:, players].bitcast(FP8X4),
-                rhs_scale=x_scale[4 * z :, players],
+                out=ratings[i][:],
+                lhsT=w_codes[z][:, features].bitcast(FP8X4),
+                lhsT_scale=w_planes[z][:, features],
+                rhs=x_codes[z][:, j0 : j0 + width].bitcast(FP8X4),
+                rhs_scale=x_planes[:, z * S + j0 : z * S + j0 + width],
                 start=(z == 0),
                 stop=(z == PASSES - 1),
             )
 
         for z in range(PASSES):
-            for k in range(3):
-                multiply(k, z)
+            for i in range(piece_of[1] + 1):
+                multiply(i, z)
         for z in range(PASSES):
-            multiply(3, z)
+            multiply(piece_of[2], z)
 
-        plain = [keep.tile([P, S], F32, name="plain%d" % b, tag="plain%d" % b) for b in range(BLOCKS)]
+        plain = [keep.tile([P, S], F32, name="plain%d" % b) for b in range(BLOCKS)]
 
-        def leave(k, tile):
-            b, c0, width, k = pieces[k]
-            nc.scalar.activation(out=tile[:, c0 : c0 + width], in_=ratings[k][:], func=ACT.Copy, scale=1.0 / STEP)
+        def leave(i, tile):
+            b, j0, width = pieces[i]
+            nc.scalar.activation(out=tile[:, j0 : j0 + width], in_=ratings[i][:], func=ACT.Copy, scale=1.0 / STEP)
 
-        leave(0, windows[0])
-        leave(0, plain[0])
-        leave(1, windows[0])
-        leave(1, plain[0])
-        ratings.append(bank("rating4", 0))
+        for i in range(piece_of[0] + 1):
+            leave(i, windows[0])
+            leave(i, plain[0])
+        ratings.append(bank("rating%d" % piece_of[3], 0))
         for z in range(PASSES):
-            multiply(4, z)
+            multiply(piece_of[3], z)
 
-        sum_bank = {0: 4, 1: 5, 2: 6, 3: 7}
         back_bank = {0: 1, 1: 0, 2: 2, 3: 3}
-        late = (2, 3)
-        held = {(1, 0): "gap0_1_0", (1, 1): "gap1_0_0", (2, 0): "win0_1", (2, 1): "gap1_0_0", (3, 0): "turned0", (3, 1): "gap3_0_0"}
-        sums, backs, wins, totals = {}, {}, {}, {}
+        sums, totals, backs, wins, win_tags = {}, {}, {}, {}, {}
         out_rows = out.rearrange("(p b) j -> p b j", b=BLOCKS)
 
         def add_turned(b, values, first, final):
@@ -169,89 +183,88 @@ def tile_picked_elo8_none_p_kernel(
                 )
 
         def open_sum(b):
-            sums[b] = bank("sum%d" % b, sum_bank[b])
+            sums[b] = bank("sum%d" % b, BLOCKS + b)
             add_turned(b, windows[b], True, False)
             add_turned(b, results[0, b], False, False)
-            add_turned(b, results[1, b], False, b in late)
+            add_turned(b, results[1, b], False, b in LATE)
+
+        def add_win(b, g):
+            add_turned(b, wins[b, g], False, g == GAMES - 1)
 
         def close_sum(b):
-            totals[b] = keep.tile([P, S], F32, name="turned%d" % b, tag="turned%d" % b)
-            nc.scalar.activation(out=totals[b][:], in_=sums[b][:], func=ACT.Copy, scale=STEP, bias=-2 * STEP)
+            totals[b] = keep.tile([P, S], F32, name="total%d" % b, tag="total%d" % b)
+            nc.scalar.activation(out=totals[b][:], in_=sums[b][:], func=ACT.Copy, scale=STEP, bias=-GAMES * STEP)
 
         def turn_back(b):
-            turned = totals[b]
             backs[b] = bank("back%d" % b, back_bank[b])
             for c in range(CHUNKS):
                 cols = slice(c * P, (c + 1) * P)
-                nc.tensor.transpose(backs[b][:, cols], turned[:, cols], ident[:])
+                nc.tensor.transpose(backs[b][:, cols], totals[b][:, cols], ident[:])
 
-        def duel(b, g, c0=0, width=S):
-            gap = keep.tile([P, width], F32, name="gap%d_%d_%d" % (b, g, c0), tag="gap%d_%d_%d" % (b, g, c0))
-            nc.vector.tensor_tensor(
-                gap[:],
-                windows[b][:].indirect(rivals[g][:, c0 // 16 : (c0 + width) // 16]),
-                plain[b][:, c0 : c0 + width],
-                ALU.subtract,
-            )
-            if c0 == 0:
-                name = "win%d_%d" % (b, g)
-                wins[b, g] = keep.tile([P, S], F32, name=name, tag=held.get((b, g), name))
-            nc.scalar.activation(out=wins[b, g][:, c0 : c0 + width], in_=gap[:], func=ACT.Sigmoid, scale=STEP)
+        def gap_tag(b, g, j0=0):
+            return "gap%d_%d_%d" % (b, g, j0)
 
-        def count(b, g):
-            add_turned(b, wins[b, g], False, g == 1)
+        def duel(b, g, over=None, widths=S):
+            win_tags[b, g] = over or "win%d_%d" % (b, g)
+            for j0 in range(0, S, widths):
+                gap = keep.tile([P, widths], F32, name=gap_tag(b, g, j0), tag=gap_tag(b, g, j0))
+                nc.vector.tensor_tensor(
+                    gap[:],
+                    windows[b][:].indirect(rivals[g][:, j0 // STRIPE : (j0 + widths) // STRIPE]),
+                    plain[b][:, j0 : j0 + widths],
+                    ALU.subtract,
+                )
+                if j0 == 0:
+                    wins[b, g] = keep.tile([P, S], F32, name="win%d_%d" % (b, g), tag=win_tags[b, g])
+                nc.scalar.activation(out=wins[b, g][:, j0 : j0 + widths], in_=gap[:], func=ACT.Sigmoid, scale=STEP)
 
-        def store(b):
+        def store_early(b):
             done = keep.tile([P, S], F32, name="done%d" % b)
             nc.scalar.copy(out=done[:], in_=backs[b][:])
             nc.scalar.dma_start(out=out_rows[:, b, :], in_=done[:])
 
-        def settle(b, stores):
+        def store_late(b, widths):
             part = keep.tile([P, S], F32, name="part%d" % b)
             done = keep.tile([P, S], F32, name="done%d" % b)
-            for c0 in (0, half):
-                cols = slice(c0, c0 + half)
-                nc.vector.scalar_tensor_tensor(part[:, cols], wins[b, 0][:, cols], STEP, backs[b][:, cols], ALU.mult, ALU.add)
-            for c0 in (0, half):
-                cols = slice(c0, c0 + half)
-                nc.vector.scalar_tensor_tensor(done[:, cols], wins[b, 1][:, cols], STEP, part[:, cols], ALU.mult, ALU.add)
-            for c0 in range(0, S, S // stores):
-                cols = slice(c0, c0 + S // stores)
-                nc.sync.dma_start(out=out_rows[:, b, cols], in_=done[:, cols])
+            for g, (before, after) in enumerate(((backs[b], part), (part, done))):
+                for j0 in (0, HALF):
+                    cols = slice(j0, j0 + HALF)
+                    nc.vector.scalar_tensor_tensor(
+                        after[:, cols], wins[b, g][:, cols], STEP, before[:, cols], ALU.mult, ALU.add
+                    )
+            for j0 in range(0, S, widths):
+                nc.sync.dma_start(out=out_rows[:, b, j0 : j0 + widths], in_=done[:, j0 : j0 + widths])
 
-        leave(1 + 1, windows[1])
-        leave(1 + 1, plain[1])
-        leave(2 + 1, windows[2])
+        leave(piece_of[1], windows[1])
+        leave(piece_of[1], plain[1])
+        leave(piece_of[2], windows[2])
         nc.sync.dma_start(out=plain[2][:], in_=windows[2][:, :S])
-        duel(0, 0, 0, half)
-        duel(0, 0, half, half)
-        leave(3 + 1, windows[3])
+        duel(0, 0, widths=HALF)
+        leave(piece_of[3], windows[3])
         nc.sync.dma_start(out=plain[3][:], in_=windows[3][:, :S])
+
         open_sum(0)
         open_sum(1)
-        count(0, 0)
+        add_win(0, 0)
         open_sum(2)
         duel(0, 1)
-        count(0, 1)
-        duel(1, 0)
-        count(1, 0)
+        add_win(0, 1)
+        duel(1, 0, over=gap_tag(0, 1))
+        add_win(1, 0)
         open_sum(3)
-        duel(1, 1)
-        count(1, 1)
-        close_sum(2)
-        close_sum(0)
-        duel(2, 0)
-        turn_back(2)
-        turn_back(0)
-        close_sum(3)
-        close_sum(1)
-        turn_back(3)
-        turn_back(1)
-        duel(2, 1)
-        store(0)
-        duel(3, 0)
-        duel(3, 1, 0, half)
-        duel(3, 1, half, half)
-        store(1)
-        settle(2, 1)
-        settle(3, 2)
+        duel(1, 1, over=gap_tag(1, 0))
+        add_win(1, 1)
+
+        for early, late in zip(EARLY, LATE):
+            close_sum(late)
+            close_sum(early)
+            duel(2, early, over=win_tags[early, 1])
+            turn_back(late)
+            turn_back(early)
+
+        store_early(0)
+        duel(3, 0, over="total0")
+        duel(3, 1, over=gap_tag(3, 0), widths=HALF)
+        store_early(1)
+        store_late(2, S)
+        store_late(3, HALF)

@@ -77,8 +77,7 @@ def tile_picked_elo8_none_p_kernel(
         make_identity(nc, ident[:])
 
         windows = [keep.tile([P, 2 * S], F32, name="window%d" % b) for b in range(BLOCKS)]
-        for b in range(BLOCKS):
-            nc.vector.memset(windows[b][:, S:], 0.0)
+        nc.gpsimd.memset(windows[0][:, S:], 0.0)
 
         picked_scales = keep.tile([P, S], U8, name="picked_scales", align_bytes=64)
         nc.vector.tensor_copy(picked_scales[:], scale_table[:].indirect(picks[:]))
@@ -90,38 +89,34 @@ def tile_picked_elo8_none_p_kernel(
             )
         word_table.append(load_words(1, "scale_table"))
 
-        grouped = [
-            keep.tile([P, BLOCKS, P, PACK], BF16, name="grouped%d" % z, tag="grouped%d" % z, align_bytes=64)
-            for z in range(PASSES)
-        ]
-        for z in range(PASSES):
-            cast_to = grouped[z][:].rearrange("p (u e) c t -> p u c t e", e=2)
-            cast_from = w_raw[z][:].rearrange("p t (c u e) -> p u c t e", u=2, e=2)
-            nc.vector.tensor_copy(out=cast_to[:, :, P // 2 :], in_=cast_from[:, :, P // 2 :])
-            nc.scalar.copy(out=cast_to[:, :, : P // 2], in_=cast_from[:, :, : P // 2])
-
         x_codes = [keep.tile([P, S], U32, name="x_codes%d" % z, align_bytes=64) for z in range(PASSES)]
-        w_codes, w_planes = [], []
+        w_codes = [keep.tile([P, N], U32, name="w_codes%d" % z, align_bytes=64) for z in range(PASSES)]
+        w_planes = [keep.tile([P, N], U8, name="w_plane%d" % z, align_bytes=64) for z in range(PASSES)]
         for z in range(PASSES):
-            w_codes.append(keep.tile([P, N], U32, name="w_codes%d" % z, align_bytes=64))
-            w_planes.append(keep.tile([P, N], U8, name="w_plane%d" % z, align_bytes=64))
-            nc.vector.quantize_mx(
-                out=w_codes[z][:].bitcast(FP8X4),
-                scales=w_planes[z][:],
-                in_=grouped[z][:].rearrange("p b c t -> p (b c t)"),
-            )
+            cast_from = w_raw[z][:].rearrange("p t (c u e) -> p u c t e", u=2, e=2)
+            for u, cast in enumerate((nc.vector.tensor_copy, nc.scalar.copy)):
+                grouped = keep.tile(
+                    [P, 2, P, PACK], BF16, name="grouped%d_%d" % (z, u), tag="grouped%d_%d" % (z, u), align_bytes=64
+                )
+                cast(out=grouped[:].rearrange("p e c t -> p c t e"), in_=cast_from[:, u])
+                cols = slice(2 * u * P, 2 * (u + 1) * P)
+                nc.vector.quantize_mx(
+                    out=w_codes[z][:, cols].bitcast(FP8X4),
+                    scales=w_planes[z][:, cols],
+                    in_=grouped[:].rearrange("p e c t -> p (e c t)"),
+                )
 
-        nc.vector.tensor_copy(x_codes[0][:], word_table[0][:].bitcast(U32).indirect(picks[:]))
-        for j0 in (0, HALF):
-            nc.vector.tensor_copy(
-                x_codes[1][:, j0 : j0 + HALF],
-                word_table[1][:].bitcast(U32).indirect(picks[:, j0 // STRIPE : (j0 + HALF) // STRIPE]),
-            )
+        for z in range(PASSES):
+            for j0 in (0, HALF):
+                nc.vector.tensor_copy(
+                    x_codes[z][:, j0 : j0 + HALF],
+                    word_table[z][:].bitcast(U32).indirect(picks[:, j0 // STRIPE : (j0 + HALF) // STRIPE]),
+                )
 
         results = {}
         res_rows = [res.rearrange("(p b) j -> p b j", b=BLOCKS) for res in (res1, res2)]
         for z, pair in enumerate((EARLY, LATE)):
-            for g, staging in enumerate(("w_raw%d" % z, "grouped%d" % z)):
+            for g, staging in enumerate(("w_raw%d" % z, "grouped%d_1" % z)):
                 both = keep.tile([P, 2, S], F32, name="res%d_%d" % (g, z), tag=staging, align_bytes=64)
                 nc.sync.dma_start(out=both[:], in_=res_rows[g][:, pair[0] : pair[1] + 1, :])
                 for i, b in enumerate(pair):
@@ -153,7 +148,7 @@ def tile_picked_elo8_none_p_kernel(
         for z in range(PASSES):
             multiply(piece_of[2], z)
 
-        plain = [keep.tile([P, S], F32, name="plain%d" % b) for b in range(BLOCKS)]
+        plain = [windows[b + 1][:, S:] for b in range(BLOCKS - 1)] + [keep.tile([P, S], F32, name="plain_last")]
 
         def leave(i, tile):
             b, j0, width = pieces[i]

@@ -90,52 +90,56 @@ def tile_picked_elo8_none_p_kernel(
         word_table.append(load_words(1, "scale_table"))
 
         x_codes = [keep.tile([P, S], U32, name="x_codes%d" % z, align_bytes=64) for z in range(PASSES)]
-        w_codes = [keep.tile([P, N], U32, name="w_codes%d" % z, align_bytes=64) for z in range(PASSES)]
-        w_planes = [keep.tile([P, N], U8, name="w_plane%d" % z, align_bytes=64) for z in range(PASSES)]
+        grouped, w_codes, w_planes = {}, {}, {}
+
+        def quantize(z, u, tag):
+            w_codes[z, u] = keep.tile([P, 2 * P], U32, name="w_codes%d_%d" % (z, u), tag=tag, align_bytes=64)
+            w_planes[z, u] = keep.tile([P, 2 * P], U8, name="w_plane%d_%d" % (z, u), align_bytes=64)
+            nc.vector.quantize_mx(
+                out=w_codes[z, u][:].bitcast(FP8X4),
+                scales=w_planes[z, u][:],
+                in_=grouped[z, u][:].rearrange("p e c t -> p (e c t)"),
+            )
+
         for z in range(PASSES):
             cast_from = w_raw[z][:].rearrange("p t (c u e) -> p u c t e", u=2, e=2)
             for u, cast in enumerate((nc.vector.tensor_copy, nc.scalar.copy)):
-                grouped = keep.tile(
+                grouped[z, u] = keep.tile(
                     [P, 2, P, PACK], BF16, name="grouped%d_%d" % (z, u), tag="grouped%d_%d" % (z, u), align_bytes=64
                 )
-                cast(out=grouped[:].rearrange("p e c t -> p c t e"), in_=cast_from[:, u])
-                cols = slice(2 * u * P, 2 * (u + 1) * P)
-                nc.vector.quantize_mx(
-                    out=w_codes[z][:, cols].bitcast(FP8X4),
-                    scales=w_planes[z][:, cols],
-                    in_=grouped[:].rearrange("p e c t -> p (e c t)"),
-                )
+                cast(out=grouped[z, u][:].rearrange("p e c t -> p c t e"), in_=cast_from[:, u])
+            quantize(z, 0, "w_codes%d" % z)
 
-        for z in range(PASSES):
+        for z, table_tag in enumerate(("word_table0", "scale_table")):
             for j0 in (0, HALF):
                 nc.vector.tensor_copy(
                     x_codes[z][:, j0 : j0 + HALF],
                     word_table[z][:].bitcast(U32).indirect(picks[:, j0 // STRIPE : (j0 + HALF) // STRIPE]),
                 )
+            quantize(z, 1, table_tag)
 
+        A, B, C, D = range(BLOCKS)
         results = {}
         res_rows = [res.rearrange("(p b) j -> p b j", b=BLOCKS) for res in (res1, res2)]
-        for z, pair in enumerate((EARLY, LATE)):
-            for g, staging in enumerate(("w_raw%d" % z, "grouped%d_1" % z)):
-                both = keep.tile([P, 2, S], F32, name="res%d_%d" % (g, z), tag=staging, align_bytes=64)
-                nc.sync.dma_start(out=both[:], in_=res_rows[g][:, pair[0] : pair[1] + 1, :])
-                for i, b in enumerate(pair):
-                    results[g, b] = both[:, i, :]
+        for (first, second), stagings in (((A, D), ("w_raw0", "grouped0_0")), ((B, C), ("w_raw1", "grouped1_0"))):
+            for g in range(GAMES):
+                rows = keep.tile([P, 2, S], F32, name="res%d_%d" % (g, first), tag=stagings[g], align_bytes=64)
+                nc.sync.dma_start(out=rows[:], in_=res_rows[g][:, first : second + 1 : second - first, :])
+                results[g, first], results[g, second] = rows[:, 0, :], rows[:, 1, :]
 
         def bank(name, number, width=S):
             return psum.tile([P, width], F32, name=name, tag="bank%d" % number)
 
-        pieces = [(0, 0, HALF), (0, HALF, HALF)] + [(b, 0, S) for b in range(1, BLOCKS)]
-        piece_of = {b: i for i, (b, j0, width) in enumerate(pieces)}
-        ratings = [bank("rating%d" % i, i, pieces[i][2]) for i in range(len(pieces) - 1)]
+        pieces = [(A, 0, HALF), (B, 0, HALF), (A, HALF, HALF), (B, HALF, HALF), (C, 0, S), (D, 0, S)]
+        ratings = [bank("rating%d" % i, i, pieces[i][2]) for i in range(len(pieces))]
 
         def multiply(i, z):
             b, j0, width = pieces[i]
-            features = slice(b * P, (b + 1) * P)
+            u, features = b // 2, slice(b % 2 * P, (b % 2 + 1) * P)
             nc.tensor.matmul_mx(
                 out=ratings[i][:],
-                lhsT=w_codes[z][:, features].bitcast(FP8X4),
-                lhsT_scale=w_planes[z][:, features],
+                lhsT=w_codes[z, u][:, features].bitcast(FP8X4),
+                lhsT_scale=w_planes[z, u][:, features],
                 rhs=x_codes[z][:, j0 : j0 + width].bitcast(FP8X4),
                 rhs_scale=x_planes[:, z * S + j0 : z * S + j0 + width],
                 start=(z == 0),
@@ -143,25 +147,28 @@ def tile_picked_elo8_none_p_kernel(
             )
 
         for z in range(PASSES):
-            for i in range(piece_of[1] + 1):
+            for i in range(len(pieces)):
                 multiply(i, z)
-        for z in range(PASSES):
-            multiply(piece_of[2], z)
 
-        plain = [windows[b + 1][:, S:] for b in range(BLOCKS - 1)] + [keep.tile([P, S], F32, name="plain_last")]
+        plain = {A: windows[B][:, S:], B: windows[C][:, S:], C: windows[D][:, S:], D: keep.tile([P, S], F32, name="plain_last")}
 
-        def leave(i, tile):
+        def leave(i, tile, scale=1.0 / STEP):
             b, j0, width = pieces[i]
-            nc.scalar.activation(out=tile[:, j0 : j0 + width], in_=ratings[i][:], func=ACT.Copy, scale=1.0 / STEP)
+            nc.scalar.activation(out=tile[:, j0 : j0 + width], in_=ratings[i][:], func=ACT.Copy, scale=scale)
 
-        for i in range(piece_of[0] + 1):
-            leave(i, windows[0])
-            leave(i, plain[0])
-        ratings.append(bank("rating%d" % piece_of[3], 0))
-        for z in range(PASSES):
-            multiply(piece_of[3], z)
+        def leave_by_vector(i, tile):
+            b, j0, width = pieces[i]
+            nc.vector.tensor_scalar(tile[:, j0 : j0 + width], ratings[i][:], 1.0 / STEP, None, ALU.mult)
 
-        back_bank = {0: 1, 1: 0, 2: 2, 3: 3}
+        leave(0, windows[A])
+        leave(0, plain[A])
+        leave_by_vector(1, windows[B])
+        leave(2, windows[A])
+        leave(2, plain[A])
+        leave_by_vector(3, windows[B])
+
+        sum_bank = {A: 6, D: 7, B: 0, C: 6}
+        back_bank = {A: 2, B: 3, C: 4, D: 1}
         sums, totals, backs, wins, win_tags = {}, {}, {}, {}, {}
         out_rows = out.rearrange("(p b) j -> p b j", b=BLOCKS)
 
@@ -177,17 +184,17 @@ def tile_picked_elo8_none_p_kernel(
                     is_transpose=True,
                 )
 
-        def open_sum(b):
-            sums[b] = bank("sum%d" % b, BLOCKS + b)
-            add_turned(b, windows[b], True, False)
-            add_turned(b, results[0, b], False, False)
-            add_turned(b, results[1, b], False, b in LATE)
+        def open_sum(b, final=False):
+            sums[b] = bank("sum%d" % b, sum_bank[b])
+            add_turned(b, results[0, b], True, False)
+            add_turned(b, windows[b], False, False)
+            add_turned(b, results[1, b], False, final)
 
-        def add_win(b, g):
-            add_turned(b, wins[b, g], False, g == GAMES - 1)
+        def add_win(b, g, final):
+            add_turned(b, wins[b, g], False, final)
 
         def close_sum(b):
-            totals[b] = keep.tile([P, S], F32, name="total%d" % b, tag="total%d" % b)
+            totals[b] = keep.tile([P, S], F32, name="total%d" % b, tag="total%d" % b, align_bytes=64)
             nc.scalar.activation(out=totals[b][:], in_=sums[b][:], func=ACT.Copy, scale=STEP, bias=-GAMES * STEP)
 
         def turn_back(b):
@@ -196,70 +203,89 @@ def tile_picked_elo8_none_p_kernel(
                 cols = slice(c * P, (c + 1) * P)
                 nc.tensor.transpose(backs[b][:, cols], totals[b][:, cols], ident[:])
 
-        def gap_tag(b, g, j0=0):
-            return "gap%d_%d_%d" % (b, g, j0)
+        gaps = {}
 
-        def duel(b, g, over=None, widths=S):
-            win_tags[b, g] = over or "win%d_%d" % (b, g)
-            for j0 in range(0, S, widths):
-                gap = keep.tile([P, widths], F32, name=gap_tag(b, g, j0), tag=gap_tag(b, g, j0))
+        def fetch_and_subtract(b, g, width=S):
+            gaps[b, g] = keep.tile([P, S], F32, name="gap%d_%d" % (b, g), tag="gap%d_%d" % (b, g), align_bytes=64)
+            for j0 in range(0, S, width):
                 nc.vector.tensor_tensor(
-                    gap[:],
-                    windows[b][:].indirect(rivals[g][:, j0 // STRIPE : (j0 + widths) // STRIPE]),
-                    plain[b][:, j0 : j0 + widths],
+                    gaps[b, g][:, j0 : j0 + width],
+                    windows[b][:].indirect(rivals[g][:, j0 // STRIPE : (j0 + width) // STRIPE]),
+                    plain[b][:, j0 : j0 + width],
                     ALU.subtract,
                 )
-                if j0 == 0:
-                    wins[b, g] = keep.tile([P, S], F32, name="win%d_%d" % (b, g), tag=win_tags[b, g])
-                nc.scalar.activation(out=wins[b, g][:, j0 : j0 + widths], in_=gap[:], func=ACT.Sigmoid, scale=STEP)
 
-        def store_early(b):
-            done = keep.tile([P, S], F32, name="done%d" % b)
+        fetched = {}
+
+        def fetch(b, g):
+            fetched[b, g] = keep.tile([P, S], F32, name="fetched%d_%d" % (b, g))
+            nc.scalar.activation(out=fetched[b, g][:], in_=windows[b][:].indirect(rivals[g][:]), func=ACT.Copy)
+
+        def subtract(b, g):
+            gaps[b, g] = keep.tile([P, S], F32, name="gap%d_%d" % (b, g), tag="gap%d_%d" % (b, g), align_bytes=64)
+            nc.vector.tensor_tensor(gaps[b, g][:], fetched[b, g][:], windows[b][:, :S], ALU.subtract)
+
+        def squash(b, g, scale=STEP, over=None, width=S):
+            win_tags[b, g] = over or "win%d_%d" % (b, g)
+            wins[b, g] = keep.tile([P, S], F32, name="win%d_%d" % (b, g), tag=win_tags[b, g], align_bytes=64)
+            for j0 in range(0, S, width):
+                cols = slice(j0, j0 + width)
+                nc.scalar.activation(out=wins[b, g][:, cols], in_=gaps[b, g][:, cols], func=ACT.Sigmoid, scale=scale)
+
+        def finish(b, last, factor, before, over, width=S):
+            done = keep.tile([P, S], F32, name="done%d" % b, tag=over, align_bytes=64)
+            for j0 in range(0, S, width):
+                cols = slice(j0, j0 + width)
+                nc.vector.scalar_tensor_tensor(done[:, cols], last[:, cols], factor, before[:, cols], ALU.mult, ALU.add)
+                nc.sync.dma_start(out=out_rows[:, b, cols], in_=done[:, cols])
+
+        def store_by_scalar(b, over):
+            done = keep.tile([P, S], F32, name="done%d" % b, tag=over, align_bytes=64)
             nc.scalar.copy(out=done[:], in_=backs[b][:])
-            nc.scalar.dma_start(out=out_rows[:, b, :], in_=done[:])
+            nc.sync.dma_start(out=out_rows[:, b, :], in_=done[:])
 
-        def store_late(b, widths):
-            part = keep.tile([P, S], F32, name="part%d" % b)
-            done = keep.tile([P, S], F32, name="done%d" % b)
-            for g, (before, after) in enumerate(((backs[b], part), (part, done))):
-                for j0 in (0, HALF):
-                    cols = slice(j0, j0 + HALF)
-                    nc.vector.scalar_tensor_tensor(
-                        after[:, cols], wins[b, g][:, cols], STEP, before[:, cols], ALU.mult, ALU.add
-                    )
-            for j0 in range(0, S, widths):
-                nc.sync.dma_start(out=out_rows[:, b, j0 : j0 + widths], in_=done[:, j0 : j0 + widths])
+        nc.scalar.copy(out=plain[B][:], in_=windows[B][:, :S])
+        leave(4, windows[C])
+        nc.sync.dma_start(out=plain[C][:], in_=windows[C][:, :S])
+        leave(5, windows[D])
+        nc.sync.dma_start(out=plain[D][:], in_=windows[D][:, :S])
+        fetch_and_subtract(A, 0, HALF)
+        fetch_and_subtract(A, 1)
+        for b in (B, C):
+            for g in range(GAMES):
+                fetch_and_subtract(b, g)
+        fetch_and_subtract(D, 0)
+        fetch_and_subtract(D, 1, HALF)
 
-        leave(piece_of[1], windows[1])
-        leave(piece_of[1], plain[1])
-        leave(piece_of[2], windows[2])
-        nc.sync.dma_start(out=plain[2][:], in_=windows[2][:, :S])
-        duel(0, 0, widths=HALF)
-        leave(piece_of[3], windows[3])
-        nc.sync.dma_start(out=plain[3][:], in_=windows[3][:, :S])
+        open_sum(A)
+        open_sum(D, True)
+        squash(A, 0)
+        add_win(A, 0, False)
+        squash(A, 1)
+        add_win(A, 1, True)
+        close_sum(D)
+        open_sum(B)
+        squash(B, 0, over="grouped0_0")
+        add_win(B, 0, False)
+        close_sum(A)
+        turn_back(A)
+        squash(B, 1, over=win_tags[A, 1])
+        add_win(B, 1, True)
+        store_by_scalar(A, "done_first")
+        open_sum(C)
+        squash(C, 0, over="total%d" % A)
+        add_win(C, 0, True)
+        close_sum(B)
+        turn_back(B)
+        turn_back(D)
+        squash(C, 1, over=win_tags[B, 1])
+        close_sum(C)
+        turn_back(C)
+        squash(D, 0, over=win_tags[C, 0])
+        store_by_scalar(B, "gap%d_1" % C)
+        squash(D, 1, over="total%d" % C, width=HALF)
 
-        open_sum(0)
-        open_sum(1)
-        add_win(0, 0)
-        open_sum(2)
-        duel(0, 1)
-        add_win(0, 1)
-        duel(1, 0, over=gap_tag(0, 1))
-        add_win(1, 0)
-        open_sum(3)
-        duel(1, 1, over=gap_tag(1, 0))
-        add_win(1, 1)
-
-        for early, late in zip(EARLY, LATE):
-            close_sum(late)
-            close_sum(early)
-            duel(2, early, over=win_tags[early, 1])
-            turn_back(late)
-            turn_back(early)
-
-        store_early(0)
-        duel(3, 0, over="total0")
-        duel(3, 1, over=gap_tag(3, 0), widths=HALF)
-        store_early(1)
-        store_late(2, S)
-        store_late(3, HALF)
+        finish(C, wins[C, 1], STEP, backs[C], "gap%d_0" % D)
+        part = keep.tile([P, S], F32, name="part")
+        nc.vector.scalar_tensor_tensor(part[:], wins[D, 0][:], STEP, backs[D][:], ALU.mult, ALU.add)
+        finish(D, wins[D, 1], STEP, part, "done_last", HALF)

@@ -121,7 +121,7 @@ def tile_picked_elo8_none_p_kernel(
         A, B, C, D = range(BLOCKS)
         results = {}
         res_rows = [res.rearrange("(p b) j -> p b j", b=BLOCKS) for res in (res1, res2)]
-        for (first, second), stagings in (((A, D), ("w_raw0", "grouped0_0")), ((B, C), ("w_raw1", "grouped1_0"))):
+        for (first, second), stagings in (((A, D), ("grouped0_0", "grouped1_0")), ((B, C), ("grouped0_1", "grouped1_1"))):
             for g in range(GAMES):
                 rows = keep.tile([P, 2, S], F32, name="res%d_%d" % (g, first), tag=stagings[g], align_bytes=64)
                 nc.sync.dma_start(out=rows[:], in_=res_rows[g][:, first : second + 1 : second - first, :])
@@ -167,8 +167,8 @@ def tile_picked_elo8_none_p_kernel(
         leave(2, plain[A])
         leave_by_vector(3, windows[B])
 
-        sum_bank = {A: 6, D: 7, B: 0, C: 6}
-        back_bank = {A: 2, B: 3, C: 4, D: 1}
+        sum_bank = {A: 6, D: 7, B: 0, C: 1}
+        back_bank = {A: 2, B: 3, C: 4, D: 5}
         sums, totals, backs, wins, win_tags = {}, {}, {}, {}, {}
         out_rows = out.rearrange("(p b) j -> p b j", b=BLOCKS)
 
@@ -184,11 +184,15 @@ def tile_picked_elo8_none_p_kernel(
                     is_transpose=True,
                 )
 
-        def open_sum(b, final=False):
-            sums[b] = bank("sum%d" % b, sum_bank[b])
-            add_turned(b, results[0, b], True, False)
-            add_turned(b, windows[b], False, False)
-            add_turned(b, results[1, b], False, final)
+        def add_rating(b, first=False):
+            if first:
+                sums[b] = bank("sum%d" % b, sum_bank[b])
+            add_turned(b, windows[b], first, False)
+
+        def add_result(b, g, first=False, final=False):
+            if first:
+                sums[b] = bank("sum%d" % b, sum_bank[b])
+            add_turned(b, results[g, b], first, final)
 
         def add_win(b, g, final):
             add_turned(b, wins[b, g], False, final)
@@ -257,27 +261,35 @@ def tile_picked_elo8_none_p_kernel(
         fetch_and_subtract(D, 0)
         fetch_and_subtract(D, 1, HALF)
 
-        open_sum(A)
-        open_sum(D, True)
+        add_result(A, 0, first=True)
+        add_rating(A)
+        add_result(A, 1)
+        add_result(D, 0, first=True)
+        add_rating(B, first=True)
+        add_rating(C, first=True)
+        add_rating(D)
+        add_result(D, 1, final=True)
         squash(A, 0)
         add_win(A, 0, False)
+        add_result(B, 0)
         squash(A, 1)
         add_win(A, 1, True)
         close_sum(D)
-        open_sum(B)
-        squash(B, 0, over="grouped0_0")
+        add_result(C, 0)
+        add_result(B, 1)
+        squash(B, 0, over="grouped1_0")
         add_win(B, 0, False)
         close_sum(A)
         turn_back(A)
+        add_result(C, 1)
         squash(B, 1, over=win_tags[A, 1])
         add_win(B, 1, True)
+        turn_back(D)
         store_by_scalar(A, "done_first")
-        open_sum(C)
         squash(C, 0, over="total%d" % A)
         add_win(C, 0, True)
         close_sum(B)
         turn_back(B)
-        turn_back(D)
         squash(C, 1, over=win_tags[B, 1])
         close_sum(C)
         turn_back(C)

@@ -109,19 +109,22 @@ def tile_picked_elo8_none_p_kernel(
                 )
                 cast(out=grouped[z, u][:].rearrange("p e c t -> p c t e"), in_=cast_from[:, u])
             quantize(z, 0, "w_codes%d" % z)
+            if z == 0:
+                quantize(0, 1, "w_codes_late")
 
-        for z, table_tag in enumerate(("word_table0", "scale_table")):
+        for z in range(PASSES):
             for j0 in (0, HALF):
                 nc.vector.tensor_copy(
                     x_codes[z][:, j0 : j0 + HALF],
                     word_table[z][:].bitcast(U32).indirect(picks[:, j0 // STRIPE : (j0 + HALF) // STRIPE]),
                 )
-            quantize(z, 1, table_tag)
+            if z == 0:
+                quantize(1, 1, "word_table0")
 
         A, B, C, D = range(BLOCKS)
         results = {}
         res_rows = [res.rearrange("(p b) j -> p b j", b=BLOCKS) for res in (res1, res2)]
-        for (first, second), stagings in (((A, D), ("grouped0_0", "grouped1_0")), ((B, C), ("grouped0_1", "grouped1_1"))):
+        for (first, second), stagings in (((A, D), ("grouped0_0", "grouped0_1")), ((B, C), ("grouped1_0", "grouped1_1"))):
             for g in range(GAMES):
                 rows = keep.tile([P, 2, S], F32, name="res%d_%d" % (g, first), tag=stagings[g], align_bytes=64)
                 nc.sync.dma_start(out=rows[:], in_=res_rows[g][:, first : second + 1 : second - first, :])
@@ -130,7 +133,7 @@ def tile_picked_elo8_none_p_kernel(
         def bank(name, number, width=S):
             return psum.tile([P, width], F32, name=name, tag="bank%d" % number)
 
-        pieces = [(A, 0, HALF), (B, 0, HALF), (A, HALF, HALF), (B, HALF, HALF), (C, 0, S), (D, 0, S)]
+        pieces = [(b, j0, HALF) for j0 in (0, HALF) for b in range(BLOCKS)]
         ratings = [bank("rating%d" % i, i, pieces[i][2]) for i in range(len(pieces))]
 
         def multiply(i, z):
@@ -150,7 +153,8 @@ def tile_picked_elo8_none_p_kernel(
             for i in range(len(pieces)):
                 multiply(i, z)
 
-        plain = {A: windows[B][:, S:], B: windows[C][:, S:], C: windows[D][:, S:], D: keep.tile([P, S], F32, name="plain_last")}
+        plain = {A: windows[B][:, S:], B: windows[C][:, S:], C: windows[D][:, S:]}
+        last_plain = [keep.tile([P, HALF], F32, name="last_plain%d" % h, tag=("grouped0_0", "last_plain")[h], align_bytes=64) for h in range(2)]
 
         def leave(i, tile, scale=1.0 / STEP):
             b, j0, width = pieces[i]
@@ -163,12 +167,21 @@ def tile_picked_elo8_none_p_kernel(
         leave(0, windows[A])
         leave(0, plain[A])
         leave_by_vector(1, windows[B])
-        leave(2, windows[A])
-        leave(2, plain[A])
-        leave_by_vector(3, windows[B])
+        nc.sync.dma_start(out=plain[B][:, :HALF], in_=windows[B][:, :HALF])
+        leave_by_vector(2, windows[C])
+        leave_by_vector(3, windows[D])
+        leave(4, windows[A])
+        leave(4, plain[A])
+        leave_by_vector(5, windows[B])
+        nc.sync.dma_start(out=plain[B][:, HALF:], in_=windows[B][:, HALF:S])
+        leave(6, windows[C])
+        leave(7, windows[D])
+        nc.sync.dma_start(out=plain[C][:], in_=windows[C][:, :S])
+        for h in range(2):
+            nc.sync.dma_start(out=last_plain[h][:], in_=windows[D][:, h * HALF : (h + 1) * HALF])
 
-        sum_bank = {A: 6, D: 7, B: 0, C: 1}
-        back_bank = {A: 2, B: 3, C: 4, D: 5}
+        sum_bank = {A: 1, D: 0, B: 2, C: 3}
+        back_bank = {A: 4, B: 5, C: 6, D: 7}
         sums, totals, backs, wins, win_tags = {}, {}, {}, {}, {}
         out_rows = out.rearrange("(p b) j -> p b j", b=BLOCKS)
 
@@ -215,7 +228,7 @@ def tile_picked_elo8_none_p_kernel(
                 nc.vector.tensor_tensor(
                     gaps[b, g][:, j0 : j0 + width],
                     windows[b][:].indirect(rivals[g][:, j0 // STRIPE : (j0 + width) // STRIPE]),
-                    plain[b][:, j0 : j0 + width],
+                    last_plain[j0 // HALF][:] if b == D else plain[b][:, j0 : j0 + width],
                     ALU.subtract,
                 )
 
@@ -248,56 +261,55 @@ def tile_picked_elo8_none_p_kernel(
             nc.scalar.copy(out=done[:], in_=backs[b][:])
             nc.sync.dma_start(out=out_rows[:, b, :], in_=done[:])
 
-        nc.scalar.copy(out=plain[B][:], in_=windows[B][:, :S])
-        leave(4, windows[C])
-        nc.sync.dma_start(out=plain[C][:], in_=windows[C][:, :S])
-        leave(5, windows[D])
-        nc.sync.dma_start(out=plain[D][:], in_=windows[D][:, :S])
         fetch_and_subtract(A, 0, HALF)
         fetch_and_subtract(A, 1)
-        for b in (B, C):
-            for g in range(GAMES):
-                fetch_and_subtract(b, g)
-        fetch_and_subtract(D, 0)
+        fetch(B, 1)
+        subtract(B, 1)
+        fetch_and_subtract(B, 0, HALF)
+        for g in range(GAMES):
+            fetch_and_subtract(C, g)
+        fetch_and_subtract(D, 0, HALF)
         fetch_and_subtract(D, 1, HALF)
 
         add_result(A, 0, first=True)
         add_rating(A)
-        add_result(A, 1)
         add_result(D, 0, first=True)
-        add_rating(B, first=True)
-        add_rating(C, first=True)
+        add_result(A, 1)
         add_rating(D)
         add_result(D, 1, final=True)
+        add_rating(B, first=True)
+        add_rating(C, first=True)
+        add_result(B, 0)
         squash(A, 0)
         add_win(A, 0, False)
-        add_result(B, 0)
-        squash(A, 1)
-        add_win(A, 1, True)
         close_sum(D)
         add_result(C, 0)
-        add_result(B, 1)
-        squash(B, 0, over="grouped1_0")
-        add_win(B, 0, False)
-        close_sum(A)
-        turn_back(A)
-        add_result(C, 1)
-        squash(B, 1, over=win_tags[A, 1])
-        add_win(B, 1, True)
         turn_back(D)
-        store_by_scalar(A, "done_first")
-        squash(C, 0, over="total%d" % A)
+        squash(A, 1, over="grouped0_1")
+        add_win(A, 1, True)
+        add_result(B, 1)
+        squash(B, 1, over=win_tags[A, 0])
+        add_win(B, 1, False)
+        close_sum(A)
+        add_result(C, 1)
+        turn_back(A)
+        squash(B, 0, over=win_tags[A, 1])
+        add_win(B, 0, True)
+        squash(C, 0, over=win_tags[B, 1])
         add_win(C, 0, True)
+        store_by_scalar(A, "gap%d_0" % B)
         close_sum(B)
         turn_back(B)
-        squash(C, 1, over=win_tags[B, 1])
         close_sum(C)
         turn_back(C)
-        squash(D, 0, over=win_tags[C, 0])
+        squash(C, 1, over=win_tags[C, 0])
+        squash(D, 0, over="total%d" % B)
         store_by_scalar(B, "gap%d_1" % C)
         squash(D, 1, over="total%d" % C, width=HALF)
 
-        finish(C, wins[C, 1], STEP, backs[C], "gap%d_0" % D)
+        finish(C, wins[C, 1], STEP, backs[C], "grouped0_0")
         part = keep.tile([P, S], F32, name="part")
-        nc.vector.scalar_tensor_tensor(part[:], wins[D, 0][:], STEP, backs[D][:], ALU.mult, ALU.add)
+        for j0 in (0, HALF):
+            cols = slice(j0, j0 + HALF)
+            nc.vector.scalar_tensor_tensor(part[:, cols], wins[D, 0][:, cols], STEP, backs[D][:, cols], ALU.mult, ALU.add)
         finish(D, wins[D, 1], STEP, part, "done_last", HALF)

@@ -124,7 +124,7 @@ def tile_picked_elo8_none_p_kernel(
         A, B, C, D = range(BLOCKS)
         results = {}
         res_rows = [res.rearrange("(p b) j -> p b j", b=BLOCKS) for res in (res1, res2)]
-        for (first, second), stagings in (((A, D), ("grouped0_0", "grouped0_1")), ((B, C), ("grouped1_0", "grouped1_1"))):
+        for (first, second), stagings in (((A, D), ("grouped0_0", "grouped0_1")), ((B, C), ("grouped1_0", "word_table0"))):
             for g in range(GAMES):
                 rows = keep.tile([P, 2, S], F32, name="res%d_%d" % (g, first), tag=stagings[g], align_bytes=64)
                 nc.sync.dma_start(out=rows[:], in_=res_rows[g][:, first : second + 1 : second - first, :])
@@ -133,7 +133,7 @@ def tile_picked_elo8_none_p_kernel(
         def bank(name, number, width=S):
             return psum.tile([P, width], F32, name=name, tag="bank%d" % number)
 
-        pieces = [(b, j0, HALF) for j0 in (0, HALF) for b in range(BLOCKS)]
+        pieces = [(b, 0, HALF) for b in (A, C, B, D)] + [(b, HALF, HALF) for b in range(BLOCKS)]
         ratings = [bank("rating%d" % i, i, pieces[i][2]) for i in range(len(pieces))]
 
         def multiply(i, z):
@@ -166,21 +166,21 @@ def tile_picked_elo8_none_p_kernel(
 
         leave(0, windows[A])
         leave(0, plain[A])
-        leave_by_vector(1, windows[B])
-        nc.sync.dma_start(out=plain[B][:, :HALF], in_=windows[B][:, :HALF])
-        leave_by_vector(2, windows[C])
+        leave_by_vector(1, windows[C])
+        leave_by_vector(2, windows[B])
         leave_by_vector(3, windows[D])
         leave(4, windows[A])
         leave(4, plain[A])
         leave_by_vector(5, windows[B])
-        nc.sync.dma_start(out=plain[B][:, HALF:], in_=windows[B][:, HALF:S])
         leave(6, windows[C])
+        nc.scalar.copy(out=plain[B][:], in_=windows[B][:, :S])
+        for j0 in (0, HALF):
+            nc.sync.dma_start(out=plain[C][:, j0 : j0 + HALF], in_=windows[C][:, j0 : j0 + HALF])
         leave(7, windows[D])
-        nc.sync.dma_start(out=plain[C][:], in_=windows[C][:, :S])
         for h in range(2):
             nc.sync.dma_start(out=last_plain[h][:], in_=windows[D][:, h * HALF : (h + 1) * HALF])
 
-        sum_bank = {A: 1, D: 0, B: 2, C: 3}
+        sum_bank = {A: 0, D: 1, B: 2, C: 3}
         back_bank = {A: 4, B: 5, C: 6, D: 7}
         sums, totals, backs, wins, win_tags = {}, {}, {}, {}, {}
         out_rows = out.rearrange("(p b) j -> p b j", b=BLOCKS)
@@ -197,10 +197,10 @@ def tile_picked_elo8_none_p_kernel(
                     is_transpose=True,
                 )
 
-        def add_rating(b, first=False):
+        def add_rating(b, first=False, final=False):
             if first:
                 sums[b] = bank("sum%d" % b, sum_bank[b])
-            add_turned(b, windows[b], first, False)
+            add_turned(b, windows[b], first, final)
 
         def add_result(b, g, first=False, final=False):
             if first:
@@ -210,9 +210,22 @@ def tile_picked_elo8_none_p_kernel(
         def add_win(b, g, final):
             add_turned(b, wins[b, g], False, final)
 
-        def close_sum(b):
-            totals[b] = keep.tile([P, S], F32, name="total%d" % b, tag="total%d" % b, align_bytes=64)
+        def close_sum(b, over=None):
+            totals[b] = keep.tile([P, S], F32, name="total%d" % b, tag=over or "total%d" % b, align_bytes=64)
             nc.scalar.activation(out=totals[b][:], in_=sums[b][:], func=ACT.Copy, scale=STEP, bias=-GAMES * STEP)
+
+        def close_by_halves(b, numbers):
+            totals[b] = keep.tile([P, S], F32, name="total%d" % b, tag="total%d" % b, align_bytes=64)
+            backs[b] = []
+            for h, number in enumerate(numbers):
+                cols = slice(h * HALF, (h + 1) * HALF)
+                nc.scalar.activation(
+                    out=totals[b][:, cols], in_=sums[b][:, cols], func=ACT.Copy, scale=STEP, bias=-GAMES * STEP
+                )
+                backs[b].append(bank("back%d_%d" % (b, h), number, HALF))
+                for c in range(CHUNKS // 2):
+                    chunk = slice(h * HALF + c * P, h * HALF + (c + 1) * P)
+                    nc.tensor.transpose(backs[b][h][:, c * P : (c + 1) * P], totals[b][:, chunk], ident[:])
 
         def turn_back(b):
             backs[b] = bank("back%d" % b, back_bank[b])
@@ -236,7 +249,7 @@ def tile_picked_elo8_none_p_kernel(
 
         def fetch(b, g):
             fetched[b, g] = keep.tile([P, S], F32, name="fetched%d_%d" % (b, g))
-            nc.scalar.activation(out=fetched[b, g][:], in_=windows[b][:].indirect(rivals[g][:]), func=ACT.Copy)
+            nc.scalar.activation(out=fetched[b, g][:], in_=windows[b][:].indirect(rivals[g][:]), func=ACT.Copy, scale=-1.0)
 
         def subtract(b, g):
             gaps[b, g] = keep.tile([P, S], F32, name="gap%d_%d" % (b, g), tag="gap%d_%d" % (b, g), align_bytes=64)
@@ -264,50 +277,79 @@ def tile_picked_elo8_none_p_kernel(
         fetch_and_subtract(A, 0, HALF)
         fetch_and_subtract(A, 1)
         fetch(B, 1)
-        subtract(B, 1)
-        fetch_and_subtract(B, 0, HALF)
-        for g in range(GAMES):
-            fetch_and_subtract(C, g)
-        fetch_and_subtract(D, 0, HALF)
-        fetch_and_subtract(D, 1, HALF)
+        fetch_and_subtract(B, 0)
+        half_gaps = []
+        for h in range(2):
+            half_gaps.append(keep.tile([P, HALF], F32, name="half_gap%d" % h, tag="half_gap%d" % h, align_bytes=64))
+            nc.vector.tensor_tensor(
+                half_gaps[h][:],
+                windows[C][:].indirect(rivals[0][:, h * HALF // STRIPE : (h + 1) * HALF // STRIPE]),
+                plain[C][:, h * HALF : (h + 1) * HALF],
+                ALU.subtract,
+            )
+        fetch_and_subtract(C, 1)
 
         add_result(A, 0, first=True)
         add_rating(A)
         add_result(D, 0, first=True)
         add_result(A, 1)
-        add_rating(D)
-        add_result(D, 1, final=True)
+        add_result(D, 1)
         add_rating(B, first=True)
         add_rating(C, first=True)
+        add_rating(D, final=True)
+        sums["lead"] = bank("lead", back_bank[C])
+        add_turned("lead", windows[B], True, False)
         add_result(B, 0)
+        add_turned("lead", fetched[B, 1], False, True)
         squash(A, 0)
-        add_win(A, 0, False)
-        close_sum(D)
+        add_win(A, 0, True)
+        squash(A, 1)
         add_result(C, 0)
-        turn_back(D)
-        squash(A, 1, over="grouped0_1")
-        add_win(A, 1, True)
         add_result(B, 1)
-        squash(B, 1, over=win_tags[A, 0])
-        add_win(B, 1, False)
-        close_sum(A)
         add_result(C, 1)
+        turned_win = keep.tile([P, S], F32, name="turned_win", tag="turned_win", align_bytes=64)
+        nc.scalar.activation(out=turned_win[:], in_=sums["lead"][:], func=ACT.Sigmoid, scale=-STEP)
+        sums["back"] = bank("back%d" % B, back_bank[B])
+        add_turned("back", turned_win, True, False)
+        close_sum(A)
         turn_back(A)
-        squash(B, 0, over=win_tags[A, 1])
+        squash(B, 0, over=win_tags[A, 0])
         add_win(B, 0, True)
-        squash(C, 0, over=win_tags[B, 1])
+        wins[C, 0] = keep.tile([P, S], F32, name="win%d_0" % C, tag="grouped1_0", align_bytes=64)
+        for h in range(2):
+            nc.scalar.activation(
+                out=wins[C, 0][:, h * HALF : (h + 1) * HALF], in_=half_gaps[h][:], func=ACT.Sigmoid, scale=STEP
+            )
         add_win(C, 0, True)
-        store_by_scalar(A, "gap%d_0" % B)
-        close_sum(B)
-        turn_back(B)
-        close_sum(C)
-        turn_back(C)
-        squash(C, 1, over=win_tags[C, 0])
-        squash(D, 0, over="total%d" % B)
-        store_by_scalar(B, "gap%d_1" % C)
-        squash(D, 1, over="total%d" % C, width=HALF)
+        close_sum(D, "turned_win")
+        turn_back(D)
+        totals[B] = keep.tile([P, S], F32, name="total%d" % B, tag="total%d" % B, align_bytes=64)
+        nc.scalar.copy(out=totals[B][:], in_=sums[B][:])
+        add_turned("back", totals[B], False, True)
+        squash(C, 1, over=win_tags[B, 0])
+        close_by_halves(C, (back_bank[C], sum_bank[A]))
+        done = keep.tile([P, S], F32, name="done%d" % B, tag="gap%d_0" % B, align_bytes=64)
+        nc.scalar.activation(out=done[:], in_=sums["back"][:], func=ACT.Copy, scale=STEP, bias=-GAMES * STEP)
+        nc.sync.dma_start(out=out_rows[:, B, :], in_=done[:])
 
-        finish(C, wins[C, 1], STEP, backs[C], "grouped0_0")
+        finish(A, wins[A, 1], STEP, backs[A], "half_gap0")
+        last_gaps = keep.tile([P, GAMES, S], F32, name="last_gaps", tag="total%d" % A, align_bytes=64)
+        for g in range(GAMES):
+            gaps[D, g] = last_gaps[:, g, :]
+            for h in range(2):
+                nc.vector.tensor_tensor(
+                    gaps[D, g][:, h * HALF : (h + 1) * HALF],
+                    windows[D][:].indirect(rivals[g][:, h * HALF // STRIPE : (h + 1) * HALF // STRIPE]),
+                    last_plain[h][:],
+                    ALU.subtract,
+                )
+        squash(D, 0, over="total%d" % B)
+        squash(D, 1, over="total%d" % C, width=HALF)
+        done = keep.tile([P, S], F32, name="done%d" % C, tag="grouped0_0", align_bytes=64)
+        for h in range(2):
+            cols = slice(h * HALF, (h + 1) * HALF)
+            nc.vector.scalar_tensor_tensor(done[:, cols], wins[C, 1][:, cols], STEP, backs[C][h][:], ALU.mult, ALU.add)
+            nc.sync.dma_start(out=out_rows[:, C, cols], in_=done[:, cols])
         part = keep.tile([P, S], F32, name="part")
         for j0 in (0, HALF):
             cols = slice(j0, j0 + HALF)

@@ -102,12 +102,12 @@ def tile_picked_elo8_none_p_kernel(
             )
 
         for z in range(PASSES):
-            cast_from = w_raw[z][:].rearrange("p t (c u e) -> p u c t e", u=2, e=2)
+            cast_from = w_raw[z][:].rearrange("p t (c u e) -> p u c e t", u=2, e=2)
             for u, cast in enumerate((nc.vector.tensor_copy, nc.scalar.copy)):
                 grouped[z, u] = keep.tile(
                     [P, 2, P, PACK], BF16, name="grouped%d_%d" % (z, u), tag="grouped%d_%d" % (z, u), align_bytes=64
                 )
-                cast(out=grouped[z, u][:].rearrange("p e c t -> p c t e"), in_=cast_from[:, u])
+                cast(out=grouped[z, u][:].rearrange("p e c t -> p c e t"), in_=cast_from[:, u])
             quantize(z, 0, "w_codes%d" % z)
             if z == 0:
                 quantize(0, 1, "w_codes_late")

@@ -77,7 +77,8 @@ def tile_picked_elo8_none_p_kernel(
         make_identity(nc, ident[:])
 
         windows = [keep.tile([P, 2 * S], F32, name="window%d" % b) for b in range(BLOCKS)]
-        nc.gpsimd.memset(windows[0][:, S:], 0.0)
+        for window in windows:
+            nc.gpsimd.memset(window[:, S:], 0.0)
 
         picked_scales = keep.tile([P, S], U8, name="picked_scales", align_bytes=64)
         nc.vector.tensor_copy(picked_scales[:], scale_table[:].indirect(picks[:]))
@@ -122,74 +123,82 @@ def tile_picked_elo8_none_p_kernel(
                 quantize(1, 1, "word_table0")
 
         A, B, C, D = range(BLOCKS)
-        results = {}
         res_rows = [res.rearrange("(p b) j -> p b j", b=BLOCKS) for res in (res1, res2)]
-        for (first, second), stagings in (((A, D), ("grouped0_0", "grouped0_1")), ((B, C), ("grouped1_0", "word_table0"))):
-            for g in range(GAMES):
-                rows = keep.tile([P, 2, S], F32, name="res%d_%d" % (g, first), tag=stagings[g], align_bytes=64)
-                nc.sync.dma_start(out=rows[:], in_=res_rows[g][:, first : second + 1 : second - first, :])
-                results[g, first], results[g, second] = rows[:, 0, :], rows[:, 1, :]
+        out_rows = out.rearrange("(p b) j -> p b j", b=BLOCKS)
+        results = {}
+
+        def wide(name, tag=None, width=S):
+            return keep.tile([P, width], F32, name=name, tag=tag or name, align_bytes=64)
+
+        def load_result(b, g, tag):
+            results[b, g] = wide("res%d_%d" % (b, g), tag)
+            nc.sync.dma_start(out=results[b, g][:], in_=res_rows[g][:, b, :])
+
+        staged = ("grouped0_0", "w_raw0", "grouped0_1", "grouped1_0", "w_raw1", "grouped1_1")
+        for i, tag in enumerate(staged):
+            load_result(i // GAMES, i % GAMES, tag)
 
         def bank(name, number, width=S):
             return psum.tile([P, width], F32, name=name, tag="bank%d" % number)
 
-        pieces = [(b, 0, HALF) for b in (A, C, B, D)] + [(b, HALF, HALF) for b in range(BLOCKS)]
-        ratings = [bank("rating%d" % i, i, pieces[i][2]) for i in range(len(pieces))]
+        pieces = [(b, h) for h in range(2) for b in range(BLOCKS)]
+        ratings = {piece: bank("rating%d_%d" % piece, i, HALF) for i, piece in enumerate(pieces)}
+        for z in range(PASSES):
+            for b, h in pieces:
+                u, features = b // 2, slice(b % 2 * P, (b % 2 + 1) * P)
+                nc.tensor.matmul_mx(
+                    out=ratings[b, h][:],
+                    lhsT=w_codes[z, u][:, features].bitcast(FP8X4),
+                    lhsT_scale=w_planes[z, u][:, features],
+                    rhs=x_codes[z][:, h * HALF : (h + 1) * HALF].bitcast(FP8X4),
+                    rhs_scale=x_planes[:, z * S + h * HALF : z * S + (h + 1) * HALF],
+                    start=(z == 0),
+                    stop=(z == PASSES - 1),
+                )
 
-        def multiply(i, z):
-            b, j0, width = pieces[i]
-            u, features = b // 2, slice(b % 2 * P, (b % 2 + 1) * P)
-            nc.tensor.matmul_mx(
-                out=ratings[i][:],
-                lhsT=w_codes[z, u][:, features].bitcast(FP8X4),
-                lhsT_scale=w_planes[z, u][:, features],
-                rhs=x_codes[z][:, j0 : j0 + width].bitcast(FP8X4),
-                rhs_scale=x_planes[:, z * S + j0 : z * S + j0 + width],
-                start=(z == 0),
-                stop=(z == PASSES - 1),
+        def half(h):
+            return slice(h * HALF, (h + 1) * HALF)
+
+        def entries(g, j0, width):
+            return rivals[g][:, j0 // STRIPE : (j0 + width) // STRIPE]
+
+        window_scale = {A: 1.0, B: 1.0, C: 1.0, D: 1.0 / STEP}
+
+        def leave_by_scalar(b, h):
+            nc.scalar.activation(
+                out=windows[b][:, half(h)], in_=ratings[b, h][:], func=ACT.Copy, scale=window_scale[b]
             )
 
-        for z in range(PASSES):
-            for i in range(len(pieces)):
-                multiply(i, z)
+        def leave_by_vector(b, h):
+            nc.vector.tensor_scalar(windows[b][:, half(h)], ratings[b, h][:], window_scale[b], None, ALU.mult)
 
-        plain = {A: windows[B][:, S:], B: windows[C][:, S:], C: windows[D][:, S:]}
-        last_plain = [keep.tile([P, HALF], F32, name="last_plain%d" % h, tag=("grouped0_0", "last_plain")[h], align_bytes=64) for h in range(2)]
+        plain = {b: wide("plain%d" % b) for b in (B, C, D)}
 
-        def leave(i, tile, scale=1.0 / STEP):
-            b, j0, width = pieces[i]
-            nc.scalar.activation(out=tile[:, j0 : j0 + width], in_=ratings[i][:], func=ACT.Copy, scale=scale)
+        leave_by_scalar(A, 0)
+        leave_by_vector(B, 0)
+        nc.sync.dma_start(out=plain[B][:, half(0)], in_=windows[B][:, half(0)])
+        leave_by_scalar(C, 0)
+        leave_by_vector(D, 0)
+        leave_by_scalar(A, 1)
+        leave_by_vector(B, 1)
+        nc.sync.dma_start(out=plain[B][:, half(1)], in_=windows[B][:, half(1)])
+        leave_by_scalar(C, 1)
+        nc.sync.dma_start(out=plain[C][:], in_=windows[C][:, :S])
+        leave_by_scalar(D, 1)
+        nc.sync.dma_start(out=plain[D][:], in_=windows[D][:, :S])
 
-        def leave_by_vector(i, tile):
-            b, j0, width = pieces[i]
-            nc.vector.tensor_scalar(tile[:, j0 : j0 + width], ratings[i][:], 1.0 / STEP, None, ALU.mult)
+        both = wide("both")
+        nc.gpsimd.tensor_tensor(both[:], results[A, 0][:], results[A, 1][:], ALU.add)
+        scaled = wide("scaled")
+        nc.gpsimd.tensor_scalar(scaled[:], both[:], STEP, 0.0, ALU.mult, ALU.add)
+        base = wide("base")
+        nc.gpsimd.tensor_tensor(base[:], scaled[:], windows[A][:, :S], ALU.add)
 
-        leave(0, windows[A])
-        leave(0, plain[A])
-        leave_by_vector(1, windows[C])
-        leave_by_vector(2, windows[B])
-        leave_by_vector(3, windows[D])
-        leave(4, windows[A])
-        leave(4, plain[A])
-        leave_by_vector(5, windows[B])
-        leave(6, windows[C])
-        nc.scalar.copy(out=plain[B][:], in_=windows[B][:, :S])
-        for j0 in (0, HALF):
-            nc.sync.dma_start(out=plain[C][:, j0 : j0 + HALF], in_=windows[C][:, j0 : j0 + HALF])
-        leave(7, windows[D])
-        for h in range(2):
-            nc.sync.dma_start(out=last_plain[h][:], in_=windows[D][:, h * HALF : (h + 1) * HALF])
-
-        sum_bank = {A: 0, D: 1, B: 2, C: 3}
-        back_bank = {A: 4, B: 5, C: 6, D: 7}
-        sums, totals, backs, wins, win_tags = {}, {}, {}, {}, {}
-        out_rows = out.rearrange("(p b) j -> p b j", b=BLOCKS)
-
-        def add_turned(b, values, first, final):
+        def add_turned(target, values, first=False, final=False):
             for c in range(CHUNKS):
                 cols = slice(c * P, (c + 1) * P)
                 nc.tensor.matmul(
-                    sums[b][:, cols],
+                    target[:, cols],
                     values[:, cols],
                     ident[:],
                     start=(first and c == 0),
@@ -197,161 +206,111 @@ def tile_picked_elo8_none_p_kernel(
                     is_transpose=True,
                 )
 
-        def add_rating(b, first=False, final=False):
-            if first:
-                sums[b] = bank("sum%d" % b, sum_bank[b])
-            add_turned(b, windows[b], first, final)
+        def squash(name, gap, scale, tag=None, width=S):
+            win = wide(name, tag)
+            for j0 in range(0, S, width):
+                nc.scalar.activation(out=win[:, j0 : j0 + width], in_=gap[:, j0 : j0 + width], func=ACT.Sigmoid, scale=scale)
+            return win
 
-        def add_result(b, g, first=False, final=False):
-            if first:
-                sums[b] = bank("sum%d" % b, sum_bank[b])
-            add_turned(b, results[g, b], first, final)
-
-        def add_win(b, g, final):
-            add_turned(b, wins[b, g], False, final)
-
-        def close_sum(b, over=None):
-            totals[b] = keep.tile([P, S], F32, name="total%d" % b, tag=over or "total%d" % b, align_bytes=64)
-            nc.scalar.activation(out=totals[b][:], in_=sums[b][:], func=ACT.Copy, scale=STEP, bias=-GAMES * STEP)
-
-        def close_by_halves(b, numbers):
-            totals[b] = keep.tile([P, S], F32, name="total%d" % b, tag="total%d" % b, align_bytes=64)
-            backs[b] = []
-            for h, number in enumerate(numbers):
-                cols = slice(h * HALF, (h + 1) * HALF)
-                nc.scalar.activation(
-                    out=totals[b][:, cols], in_=sums[b][:, cols], func=ACT.Copy, scale=STEP, bias=-GAMES * STEP
-                )
-                backs[b].append(bank("back%d_%d" % (b, h), number, HALF))
-                for c in range(CHUNKS // 2):
-                    chunk = slice(h * HALF + c * P, h * HALF + (c + 1) * P)
-                    nc.tensor.transpose(backs[b][h][:, c * P : (c + 1) * P], totals[b][:, chunk], ident[:])
-
-        def turn_back(b):
-            backs[b] = bank("back%d" % b, back_bank[b])
-            for c in range(CHUNKS):
-                cols = slice(c * P, (c + 1) * P)
-                nc.tensor.transpose(backs[b][:, cols], totals[b][:, cols], ident[:])
-
-        gaps = {}
-
-        def fetch_and_subtract(b, g, width=S):
-            gaps[b, g] = keep.tile([P, S], F32, name="gap%d_%d" % (b, g), tag="gap%d_%d" % (b, g), align_bytes=64)
+        def fetch_and_subtract(b, g, width=S, tag=None):
+            gap = wide("gap%d_%d" % (b, g), tag)
             for j0 in range(0, S, width):
                 nc.vector.tensor_tensor(
-                    gaps[b, g][:, j0 : j0 + width],
-                    windows[b][:].indirect(rivals[g][:, j0 // STRIPE : (j0 + width) // STRIPE]),
-                    last_plain[j0 // HALF][:] if b == D else plain[b][:, j0 : j0 + width],
+                    gap[:, j0 : j0 + width],
+                    windows[b][:].indirect(entries(g, j0, width)),
+                    plain[b][:, j0 : j0 + width],
                     ALU.subtract,
                 )
+            return gap
 
-        fetched = {}
+        def close(name, total, scale, tag=None):
+            closed = wide(name, tag)
+            nc.scalar.activation(out=closed[:], in_=total[:], func=ACT.Copy, scale=scale, bias=-GAMES * scale)
+            return closed
 
-        def fetch(b, g):
-            fetched[b, g] = keep.tile([P, S], F32, name="fetched%d_%d" % (b, g))
-            nc.scalar.activation(out=fetched[b, g][:], in_=windows[b][:].indirect(rivals[g][:]), func=ACT.Copy, scale=-1.0)
-
-        def subtract(b, g):
-            gaps[b, g] = keep.tile([P, S], F32, name="gap%d_%d" % (b, g), tag="gap%d_%d" % (b, g), align_bytes=64)
-            nc.vector.tensor_tensor(gaps[b, g][:], fetched[b, g][:], windows[b][:, :S], ALU.subtract)
-
-        def squash(b, g, scale=STEP, over=None, width=S):
-            win_tags[b, g] = over or "win%d_%d" % (b, g)
-            wins[b, g] = keep.tile([P, S], F32, name="win%d_%d" % (b, g), tag=win_tags[b, g], align_bytes=64)
-            for j0 in range(0, S, width):
-                cols = slice(j0, j0 + width)
-                nc.scalar.activation(out=wins[b, g][:, cols], in_=gaps[b, g][:, cols], func=ACT.Sigmoid, scale=scale)
-
-        def finish(b, last, factor, before, over, width=S):
-            done = keep.tile([P, S], F32, name="done%d" % b, tag=over, align_bytes=64)
+        def finish(b, last, factor, before, tag=None, width=S):
+            done = wide("done%d" % b, tag)
             for j0 in range(0, S, width):
                 cols = slice(j0, j0 + width)
                 nc.vector.scalar_tensor_tensor(done[:, cols], last[:, cols], factor, before[:, cols], ALU.mult, ALU.add)
                 nc.sync.dma_start(out=out_rows[:, b, cols], in_=done[:, cols])
 
-        def store_by_scalar(b, over):
-            done = keep.tile([P, S], F32, name="done%d" % b, tag=over, align_bytes=64)
-            nc.scalar.copy(out=done[:], in_=backs[b][:])
-            nc.sync.dma_start(out=out_rows[:, b, :], in_=done[:])
-
-        fetch_and_subtract(A, 0, HALF)
-        fetch_and_subtract(A, 1)
-        fetch(B, 1)
-        fetch_and_subtract(B, 0)
-        half_gaps = []
-        for h in range(2):
-            half_gaps.append(keep.tile([P, HALF], F32, name="half_gap%d" % h, tag="half_gap%d" % h, align_bytes=64))
-            nc.vector.tensor_tensor(
-                half_gaps[h][:],
-                windows[C][:].indirect(rivals[0][:, h * HALF // STRIPE : (h + 1) * HALF // STRIPE]),
-                plain[C][:, h * HALF : (h + 1) * HALF],
-                ALU.subtract,
-            )
-        fetch_and_subtract(C, 1)
-
-        add_result(A, 0, first=True)
-        add_rating(A)
-        add_result(D, 0, first=True)
-        add_result(A, 1)
-        add_result(D, 1)
-        add_rating(B, first=True)
-        add_rating(C, first=True)
-        add_rating(D, final=True)
-        sums["lead"] = bank("lead", back_bank[C])
-        add_turned("lead", windows[B], True, False)
-        add_result(B, 0)
-        add_turned("lead", fetched[B, 1], False, True)
-        squash(A, 0)
-        add_win(A, 0, True)
-        squash(A, 1)
-        add_result(C, 0)
-        add_result(B, 1)
-        add_result(C, 1)
-        turned_win = keep.tile([P, S], F32, name="turned_win", tag="turned_win", align_bytes=64)
-        nc.scalar.activation(out=turned_win[:], in_=sums["lead"][:], func=ACT.Sigmoid, scale=-STEP)
-        sums["back"] = bank("back%d" % B, back_bank[B])
-        add_turned("back", turned_win, True, False)
-        close_sum(A)
-        turn_back(A)
-        squash(B, 0, over=win_tags[A, 0])
-        add_win(B, 0, True)
-        wins[C, 0] = keep.tile([P, S], F32, name="win%d_0" % C, tag="grouped1_0", align_bytes=64)
-        for h in range(2):
-            nc.scalar.activation(
-                out=wins[C, 0][:, h * HALF : (h + 1) * HALF], in_=half_gaps[h][:], func=ACT.Sigmoid, scale=STEP
-            )
-        add_win(C, 0, True)
-        close_sum(D, "turned_win")
-        turn_back(D)
-        totals[B] = keep.tile([P, S], F32, name="total%d" % B, tag="total%d" % B, align_bytes=64)
-        nc.scalar.copy(out=totals[B][:], in_=sums[B][:])
-        add_turned("back", totals[B], False, True)
-        squash(C, 1, over=win_tags[B, 0])
-        close_by_halves(C, (back_bank[C], sum_bank[A]))
-        done = keep.tile([P, S], F32, name="done%d" % B, tag="gap%d_0" % B, align_bytes=64)
-        nc.scalar.activation(out=done[:], in_=sums["back"][:], func=ACT.Copy, scale=STEP, bias=-GAMES * STEP)
-        nc.sync.dma_start(out=out_rows[:, B, :], in_=done[:])
-
-        finish(A, wins[A, 1], STEP, backs[A], "half_gap0")
-        last_gaps = keep.tile([P, GAMES, S], F32, name="last_gaps", tag="total%d" % A, align_bytes=64)
+        fetched = {}
         for g in range(GAMES):
-            gaps[D, g] = last_gaps[:, g, :]
-            for h in range(2):
-                nc.vector.tensor_tensor(
-                    gaps[D, g][:, h * HALF : (h + 1) * HALF],
-                    windows[D][:].indirect(rivals[g][:, h * HALF // STRIPE : (h + 1) * HALF // STRIPE]),
-                    last_plain[h][:],
-                    ALU.subtract,
-                )
-        squash(D, 0, over="total%d" % B)
-        squash(D, 1, over="total%d" % C, width=HALF)
-        done = keep.tile([P, S], F32, name="done%d" % C, tag="grouped0_0", align_bytes=64)
+            fetched[A, g] = wide("fetched0_%d" % g)
+            nc.vector.tensor_scalar(fetched[A, g][:], windows[A][:].indirect(rivals[g][:]), -1.0, 0.0, ALU.mult, ALU.add)
+        for b, g in ((B, 1), (C, 0)):
+            fetched[b, g] = wide("fetched%d_%d" % (b, g))
+            nc.scalar.activation(out=fetched[b, g][:], in_=windows[b][:].indirect(rivals[g][:]), func=ACT.Copy, scale=-1.0)
+        gap_b0 = fetch_and_subtract(B, 0, HALF)
+        gap_c1 = fetch_and_subtract(C, 1)
+        gap_d0 = fetch_and_subtract(D, 0)
+
+        lead_a0, lead_a1, lead_b1 = bank("lead_a0", 0), bank("lead_a1", 1), bank("lead_b1", 2)
+        sum_b, back_a, lead_c0 = bank("sum_b", 3), bank("back_a", 4), bank("lead_c0", 5)
+        sum_c, sum_d = bank("sum_c", 6), bank("sum_d", 7)
+        add_turned(lead_a0, windows[A], first=True)
+        add_turned(lead_a1, windows[A], first=True)
+        add_turned(lead_b1, windows[B], first=True)
+        add_turned(lead_c0, windows[C], first=True)
+        add_turned(sum_b, results[B, 0], first=True)
+        add_turned(lead_a0, fetched[A, 0], final=True)
+        add_turned(lead_b1, fetched[B, 1], final=True)
+        load_result(D, 0, "fetched0_0")
+        load_result(D, 1, "fetched1_1")
+        add_turned(sum_b, results[B, 1])
+        add_turned(lead_a1, fetched[A, 1], final=True)
+        add_turned(lead_c0, fetched[C, 0], final=True)
+        win_a0 = squash("win_a0", lead_a0, 1.0)
+        add_turned(sum_c, results[C, 0], first=True)
+        add_turned(back_a, win_a0, first=True)
+        win_b1 = squash("win_b1", lead_b1, -1.0)
+        add_turned(sum_c, results[C, 1])
+        back_b = bank("back_b", 0)
+        add_turned(back_b, win_b1, first=True)
+        win_b0 = squash("win_b0", gap_b0, 1.0, "fetched2_0")
+        add_turned(sum_b, win_b0, final=True)
+        win_a1 = squash("win_a1", lead_a1, 1.0, "win_a0")
+        add_turned(sum_d, windows[D], first=True)
+        add_turned(back_a, win_a1, final=True)
+        win_c1 = squash("win_c1", gap_c1, 1.0, "win_b1")
+        add_turned(sum_d, results[D, 0])
+        add_turned(sum_c, win_c1, final=True)
+        total_b = close("total_b", sum_b, 1.0)
+        add_turned(sum_d, results[D, 1])
+        add_turned(back_b, total_b, final=True)
+        win_d0 = squash("win_d0", gap_d0, STEP, "win_a0")
+        add_turned(sum_d, win_d0, final=True)
+        total_c = close("total_c", sum_c, 1.0)
+        back_c = bank("back_c", 2)
+        add_turned(back_c, total_c, first=True)
+        win_c0 = squash("win_c0", lead_c0, -1.0, "win_b1")
+        add_turned(back_c, win_c0, final=True)
+
+        def last_gap(h, tag):
+            gap = wide("last_gap%d" % h, tag, HALF)
+            nc.vector.tensor_tensor(
+                gap[:], windows[D][:].indirect(entries(1, h * HALF, HALF)), plain[D][:, half(h)], ALU.subtract
+            )
+            return gap
+
+        def close_half(h, number):
+            closed = wide("total_d%d" % h, None, HALF)
+            nc.scalar.activation(out=closed[:], in_=sum_d[:, half(h)], func=ACT.Copy, scale=STEP, bias=-GAMES * STEP)
+            back = bank("back_d%d" % h, number, HALF)
+            for c in range(CHUNKS // 2):
+                nc.tensor.transpose(back[:, c * P : (c + 1) * P], closed[:, c * P : (c + 1) * P], ident[:])
+            return back
+
+        gaps = [last_gap(0, "fetched2_0")]
+        finish(A, back_a, -STEP, base)
+        finish(B, back_b, STEP, windows[B])
+        gaps.append(last_gap(1, "total_b"))
+        finish(C, back_c, STEP, windows[C])
         for h in range(2):
-            cols = slice(h * HALF, (h + 1) * HALF)
-            nc.vector.scalar_tensor_tensor(done[:, cols], wins[C, 1][:, cols], STEP, backs[C][h][:], ALU.mult, ALU.add)
-            nc.sync.dma_start(out=out_rows[:, C, cols], in_=done[:, cols])
-        part = keep.tile([P, S], F32, name="part")
-        for j0 in (0, HALF):
-            cols = slice(j0, j0 + HALF)
-            nc.vector.scalar_tensor_tensor(part[:, cols], wins[D, 0][:, cols], STEP, backs[D][:, cols], ALU.mult, ALU.add)
-        finish(D, wins[D, 1], STEP, part, "done_last", HALF)
+            back = close_half(h, (1, 3)[h])
+            win = wide("win_d1_%d" % h, ("win_a0", "total_c")[h], HALF)
+            nc.scalar.activation(out=win[:], in_=gaps[h][:], func=ACT.Sigmoid, scale=STEP)
+            done = wide("done3_%d" % h, None, HALF)
+            nc.vector.scalar_tensor_tensor(done[:], win[:], STEP, back[:], ALU.mult, ALU.add)
+            nc.sync.dma_start(out=out_rows[:, D, half(h)], in_=done[:])

@@ -76,9 +76,10 @@ def tile_picked_elo8_none_p_kernel(
         ident = keep.tile([P, P], F32, name="ident")
         make_identity(nc, ident[:])
 
-        windows = [keep.tile([P, 2 * S], F32, name="window%d" % b) for b in range(BLOCKS)]
-        for window in windows:
-            nc.gpsimd.memset(window[:, S:], 0.0)
+        spare = (S, S, 0, S)
+        windows = [keep.tile([P, S + spare[b]], F32, name="window%d" % b) for b in range(BLOCKS)]
+        for b in (0, 1, 3):
+            nc.gpsimd.memset(windows[b][:, S:], 0.0)
 
         picked_scales = keep.tile([P, S], U8, name="picked_scales", align_bytes=64)
         nc.vector.tensor_copy(picked_scales[:], scale_table[:].indirect(picks[:]))
@@ -241,9 +242,19 @@ def tile_picked_elo8_none_p_kernel(
             nc.vector.tensor_scalar(fetched[A, g][:], windows[A][:].indirect(rivals[g][:]), -1.0, 0.0, ALU.mult, ALU.add)
         for b, g in ((B, 1), (C, 0)):
             fetched[b, g] = wide("fetched%d_%d" % (b, g))
-            nc.scalar.activation(out=fetched[b, g][:], in_=windows[b][:].indirect(rivals[g][:]), func=ACT.Copy, scale=-1.0)
+        nc.scalar.activation(out=fetched[B, 1][:], in_=windows[B][:].indirect(rivals[1][:]), func=ACT.Copy, scale=-1.0)
+        nc.vector.tensor_scalar(
+            fetched[C, 0][:, S - P :], windows[C][:].indirect(entries(0, S - P, P)), -1.0, 0.0, ALU.mult, ALU.add
+        )
+        for j0, width in ((0, HALF), (HALF, P)):
+            nc.scalar.activation(
+                out=fetched[C, 0][:, j0 : j0 + width],
+                in_=windows[C][:].indirect(entries(0, j0, width)),
+                func=ACT.Copy,
+                scale=-1.0,
+            )
         gap_b0 = fetch_and_subtract(B, 0, HALF)
-        gap_c1 = fetch_and_subtract(C, 1)
+        gap_c1 = fetch_and_subtract(C, 1, HALF)
         gap_d0 = fetch_and_subtract(D, 0)
 
         lead_a0, lead_a1, lead_b1 = bank("lead_a0", 0), bank("lead_a1", 1), bank("lead_b1", 2)
@@ -262,30 +273,30 @@ def tile_picked_elo8_none_p_kernel(
         add_turned(lead_a1, fetched[A, 1], final=True)
         add_turned(lead_c0, fetched[C, 0], final=True)
         win_a0 = squash("win_a0", lead_a0, 1.0)
-        add_turned(sum_c, results[C, 0], first=True)
         add_turned(back_a, win_a0, first=True)
+        add_turned(sum_c, results[C, 0], first=True)
         win_b1 = squash("win_b1", lead_b1, -1.0)
-        add_turned(sum_c, results[C, 1])
         back_b = bank("back_b", 0)
         add_turned(back_b, win_b1, first=True)
+        add_turned(sum_c, results[C, 1])
+        win_a1 = squash("win_a1", lead_a1, 1.0)
+        add_turned(back_a, win_a1, final=True)
         win_b0 = squash("win_b0", gap_b0, 1.0, "fetched2_0")
         add_turned(sum_b, win_b0, final=True)
-        win_a1 = squash("win_a1", lead_a1, 1.0, "win_a0")
         add_turned(sum_d, windows[D], first=True)
-        add_turned(back_a, win_a1, final=True)
-        win_c1 = squash("win_c1", gap_c1, 1.0, "win_b1")
+        win_c0 = squash("win_c0", lead_c0, -1.0, "win_b1")
+        back_c = bank("back_c", 2)
+        add_turned(back_c, win_c0, first=True)
         add_turned(sum_d, results[D, 0])
+        win_c1 = squash("win_c1", gap_c1, 1.0, "win_a1")
         add_turned(sum_c, win_c1, final=True)
         total_b = close("total_b", sum_b, 1.0)
-        add_turned(sum_d, results[D, 1])
         add_turned(back_b, total_b, final=True)
-        win_d0 = squash("win_d0", gap_d0, STEP, "win_a0")
+        add_turned(sum_d, results[D, 1])
+        win_d0 = squash("win_d0", gap_d0, STEP, "fetched2_0")
         add_turned(sum_d, win_d0, final=True)
         total_c = close("total_c", sum_c, 1.0)
-        back_c = bank("back_c", 2)
-        add_turned(back_c, total_c, first=True)
-        win_c0 = squash("win_c0", lead_c0, -1.0, "win_b1")
-        add_turned(back_c, win_c0, final=True)
+        add_turned(back_c, total_c, final=True)
 
         def last_gap(h, tag):
             gap = wide("last_gap%d" % h, tag, HALF)
@@ -302,14 +313,14 @@ def tile_picked_elo8_none_p_kernel(
                 nc.tensor.transpose(back[:, c * P : (c + 1) * P], closed[:, c * P : (c + 1) * P], ident[:])
             return back
 
-        gaps = [last_gap(0, "fetched2_0")]
+        gaps = [last_gap(0, "win_a0")]
         finish(A, back_a, -STEP, base)
         finish(B, back_b, STEP, windows[B])
         gaps.append(last_gap(1, "total_b"))
-        finish(C, back_c, STEP, windows[C])
+        finish(C, back_c, STEP, windows[C], width=HALF)
         for h in range(2):
             back = close_half(h, (1, 3)[h])
-            win = wide("win_d1_%d" % h, ("win_a0", "total_c")[h], HALF)
+            win = wide("win_d1_%d" % h, ("fetched2_0", "total_c")[h], HALF)
             nc.scalar.activation(out=win[:], in_=gaps[h][:], func=ACT.Sigmoid, scale=STEP)
             done = wide("done3_%d" % h, None, HALF)
             nc.vector.scalar_tensor_tensor(done[:], win[:], STEP, back[:], ALU.mult, ALU.add)

@@ -196,21 +196,21 @@ def tile_picked_elo8_none_p_kernel(
         nc.gpsimd.tensor_tensor(base[:], scaled[:], windows[A][:, :S], ALU.add)
 
         def add_turned(target, values, first=False, final=False):
-            for c in range(CHUNKS):
+            chunks = target.shape[1] // P
+            for c in range(chunks):
                 cols = slice(c * P, (c + 1) * P)
                 nc.tensor.matmul(
                     target[:, cols],
                     values[:, cols],
                     ident[:],
                     start=(first and c == 0),
-                    stop=(final and c == CHUNKS - 1),
+                    stop=(final and c == chunks - 1),
                     is_transpose=True,
                 )
 
-        def squash(name, gap, scale, tag=None, width=S):
-            win = wide(name, tag)
-            for j0 in range(0, S, width):
-                nc.scalar.activation(out=win[:, j0 : j0 + width], in_=gap[:, j0 : j0 + width], func=ACT.Sigmoid, scale=scale)
+        def squash(name, gap, scale, tag=None):
+            win = wide(name, tag, gap.shape[1])
+            nc.scalar.activation(out=win[:], in_=gap[:], func=ACT.Sigmoid, scale=scale)
             return win
 
         def fetch_and_subtract(b, g, width=S, tag=None):
@@ -225,7 +225,7 @@ def tile_picked_elo8_none_p_kernel(
             return gap
 
         def close(name, total, scale, tag=None):
-            closed = wide(name, tag)
+            closed = wide(name, tag, total.shape[1])
             nc.scalar.activation(out=closed[:], in_=total[:], func=ACT.Copy, scale=scale, bias=-GAMES * scale)
             return closed
 
@@ -265,6 +265,7 @@ def tile_picked_elo8_none_p_kernel(
         add_turned(lead_b1, windows[B], first=True)
         add_turned(lead_c0, windows[C], first=True)
         add_turned(sum_b, results[B, 0], first=True)
+        add_turned(sum_d[:, half(0)], windows[D][:, half(0)], first=True)
         add_turned(lead_a0, fetched[A, 0], final=True)
         add_turned(lead_b1, fetched[B, 1], final=True)
         load_result(D, 0, "fetched0_0")
@@ -283,10 +284,11 @@ def tile_picked_elo8_none_p_kernel(
         add_turned(back_a, win_a1, final=True)
         win_b0 = squash("win_b0", gap_b0, 1.0, "fetched2_0")
         add_turned(sum_b, win_b0, final=True)
-        add_turned(sum_d, windows[D], first=True)
+        add_turned(sum_d[:, half(1)], windows[D][:, half(1)])
         win_c0 = squash("win_c0", lead_c0, -1.0, "win_b1")
-        back_c = bank("back_c", 2)
-        add_turned(back_c, win_c0, first=True)
+        back_c = [bank("back_c%d" % h, number, HALF) for h, number in enumerate((2, 1))]
+        for h in range(2):
+            add_turned(back_c[h], win_c0[:, half(h)], first=True)
         add_turned(sum_d, results[D, 0])
         win_c1 = squash("win_c1", gap_c1, 1.0, "win_a1")
         add_turned(sum_c, win_c1, final=True)
@@ -295,8 +297,9 @@ def tile_picked_elo8_none_p_kernel(
         add_turned(sum_d, results[D, 1])
         win_d0 = squash("win_d0", gap_d0, STEP, "fetched2_0")
         add_turned(sum_d, win_d0, final=True)
-        total_c = close("total_c", sum_c, 1.0)
-        add_turned(back_c, total_c, final=True)
+        for h in range(2):
+            total_c = close("total_c%d" % h, sum_c[:, half(h)], 1.0)
+            add_turned(back_c[h], total_c, final=True)
 
         def last_gap(h, tag):
             gap = wide("last_gap%d" % h, tag, HALF)
@@ -305,23 +308,22 @@ def tile_picked_elo8_none_p_kernel(
             )
             return gap
 
-        def close_half(h, number):
-            closed = wide("total_d%d" % h, None, HALF)
-            nc.scalar.activation(out=closed[:], in_=sum_d[:, half(h)], func=ACT.Copy, scale=STEP, bias=-GAMES * STEP)
-            back = bank("back_d%d" % h, number, HALF)
-            for c in range(CHUNKS // 2):
-                nc.tensor.transpose(back[:, c * P : (c + 1) * P], closed[:, c * P : (c + 1) * P], ident[:])
-            return back
+        def finish_half(b, h, last, before):
+            done = wide("done%d_%d" % (b, h), None, HALF)
+            nc.vector.scalar_tensor_tensor(done[:], last, STEP, before, ALU.mult, ALU.add)
+            nc.sync.dma_start(out=out_rows[:, b, half(h)], in_=done[:])
 
         gaps = [last_gap(0, "win_a0")]
         finish(A, back_a, -STEP, base)
         finish(B, back_b, STEP, windows[B])
         gaps.append(last_gap(1, "total_b"))
-        finish(C, back_c, STEP, windows[C], width=HALF)
         for h in range(2):
-            back = close_half(h, (1, 3)[h])
-            win = wide("win_d1_%d" % h, ("fetched2_0", "total_c")[h], HALF)
-            nc.scalar.activation(out=win[:], in_=gaps[h][:], func=ACT.Sigmoid, scale=STEP)
-            done = wide("done3_%d" % h, None, HALF)
-            nc.vector.scalar_tensor_tensor(done[:], win[:], STEP, back[:], ALU.mult, ALU.add)
-            nc.sync.dma_start(out=out_rows[:, D, half(h)], in_=done[:])
+            finish_half(C, h, back_c[h][:], windows[C][:, half(h)])
+        wins = [squash("win_d1_0", gaps[0], STEP, "win_a1")]
+        back_d = [bank("back_d%d" % h, number, HALF) for h, number in enumerate((5, 3))]
+        for h in range(2):
+            total_d = close("total_d%d" % h, sum_d[:, half(h)], STEP)
+            add_turned(back_d[h], total_d, first=True, final=True)
+        wins.append(squash("win_d1_1", gaps[1], STEP, "fetched2_0"))
+        for h in range(2):
+            finish_half(D, h, wins[h][:], back_d[h][:])

@@ -76,12 +76,11 @@ def tile_picked_elo8_none_p_kernel(
         ident = keep.tile([P, P], F32, name="ident")
         make_identity(nc, ident[:])
 
-        spare = (S, S, 0, S)
-        windows = [keep.tile([P, S + spare[b]], F32, name="window%d" % b) for b in range(BLOCKS)]
-        for b in (0, 1, 3):
-            nc.gpsimd.memset(windows[b][:, S:], 0.0)
+        windows = [keep.tile([P, 2 * S], F32, name="window%d" % b) for b in range(BLOCKS)]
+        for window in windows:
+            nc.gpsimd.memset(window[:, S:], 0.0)
 
-        picked_scales = keep.tile([P, S], U8, name="picked_scales", align_bytes=64)
+        picked_scales = keep.tile([P, S], U8, name="picked_scales", tag="picked_scales", align_bytes=64)
         nc.vector.tensor_copy(picked_scales[:], scale_table[:].indirect(picks[:]))
         for q in range(QUADRANTS):
             rows = PASSES * SCALE_ROWS
@@ -91,7 +90,7 @@ def tile_picked_elo8_none_p_kernel(
             )
         word_table.append(load_words(1, "scale_table"))
 
-        x_codes = [keep.tile([P, S], U32, name="x_codes%d" % z, align_bytes=64) for z in range(PASSES)]
+        x_codes = [keep.tile([P, S], U32, name="x_codes%d" % z, tag="x_codes%d" % z, align_bytes=64) for z in range(PASSES)]
         grouped, w_codes, w_planes = {}, {}, {}
 
         def quantize(z, u, tag):
@@ -135,9 +134,15 @@ def tile_picked_elo8_none_p_kernel(
             results[b, g] = wide("res%d_%d" % (b, g), tag)
             nc.sync.dma_start(out=results[b, g][:], in_=res_rows[g][:, b, :])
 
-        staged = ("grouped0_0", "w_raw0", "grouped0_1", "grouped1_0", "w_raw1", "grouped1_1")
-        for i, tag in enumerate(staged):
-            load_result(i // GAMES, i % GAMES, tag)
+        def half(h):
+            return slice(h * HALF, (h + 1) * HALF)
+
+        first_results = {}
+        for h, g, tag in ((0, 0, "grouped0_0"), (0, 1, "w_raw0"), (1, 0, "grouped0_1"), (1, 1, "grouped1_0")):
+            first_results[g, h] = wide("res0_%d_%d" % (g, h), tag, HALF)
+            nc.sync.dma_start(out=first_results[g, h][:], in_=res_rows[g][:, A, half(h)])
+        for b, g, tag in ((B, 0, "w_raw1"), (B, 1, "picked_scales"), (C, 0, "grouped1_1")):
+            load_result(b, g, tag)
 
         def bank(name, number, width=S):
             return psum.tile([P, width], F32, name=name, tag="bank%d" % number)
@@ -157,9 +162,6 @@ def tile_picked_elo8_none_p_kernel(
                     stop=(z == PASSES - 1),
                 )
 
-        def half(h):
-            return slice(h * HALF, (h + 1) * HALF)
-
         def entries(g, j0, width):
             return rivals[g][:, j0 // STRIPE : (j0 + width) // STRIPE]
 
@@ -175,21 +177,22 @@ def tile_picked_elo8_none_p_kernel(
 
         plain = {b: wide("plain%d" % b) for b in (B, C, D)}
 
-        leave_by_scalar(A, 0)
-        leave_by_vector(B, 0)
+        leave_by_vector(A, 0)
+        leave_by_scalar(B, 0)
         nc.sync.dma_start(out=plain[B][:, half(0)], in_=windows[B][:, half(0)])
-        leave_by_scalar(C, 0)
-        leave_by_vector(D, 0)
-        leave_by_scalar(A, 1)
-        leave_by_vector(B, 1)
+        leave_by_vector(C, 0)
+        leave_by_scalar(D, 0)
+        leave_by_vector(A, 1)
+        leave_by_scalar(B, 1)
         nc.sync.dma_start(out=plain[B][:, half(1)], in_=windows[B][:, half(1)])
-        leave_by_scalar(C, 1)
+        leave_by_vector(C, 1)
         nc.sync.dma_start(out=plain[C][:], in_=windows[C][:, :S])
         leave_by_scalar(D, 1)
         nc.sync.dma_start(out=plain[D][:], in_=windows[D][:, :S])
 
         both = wide("both")
-        nc.gpsimd.tensor_tensor(both[:], results[A, 0][:], results[A, 1][:], ALU.add)
+        for h in range(2):
+            nc.gpsimd.tensor_tensor(both[:, half(h)], first_results[0, h][:], first_results[1, h][:], ALU.add)
         scaled = wide("scaled")
         nc.gpsimd.tensor_scalar(scaled[:], both[:], STEP, 0.0, ALU.mult, ALU.add)
         base = wide("base")
@@ -243,18 +246,9 @@ def tile_picked_elo8_none_p_kernel(
         for b, g in ((B, 1), (C, 0)):
             fetched[b, g] = wide("fetched%d_%d" % (b, g))
         nc.scalar.activation(out=fetched[B, 1][:], in_=windows[B][:].indirect(rivals[1][:]), func=ACT.Copy, scale=-1.0)
-        nc.vector.tensor_scalar(
-            fetched[C, 0][:, S - P :], windows[C][:].indirect(entries(0, S - P, P)), -1.0, 0.0, ALU.mult, ALU.add
-        )
-        for j0, width in ((0, HALF), (HALF, P)):
-            nc.scalar.activation(
-                out=fetched[C, 0][:, j0 : j0 + width],
-                in_=windows[C][:].indirect(entries(0, j0, width)),
-                func=ACT.Copy,
-                scale=-1.0,
-            )
+        nc.scalar.activation(out=fetched[C, 0][:], in_=windows[C][:].indirect(rivals[0][:]), func=ACT.Copy, scale=-1.0)
         gap_b0 = fetch_and_subtract(B, 0, HALF)
-        gap_c1 = fetch_and_subtract(C, 1, HALF)
+        gap_c1 = fetch_and_subtract(C, 1)
         gap_d0 = fetch_and_subtract(D, 0)
 
         lead_a0, lead_a1, lead_b1 = bank("lead_a0", 0), bank("lead_a1", 1), bank("lead_b1", 2)
@@ -268,6 +262,7 @@ def tile_picked_elo8_none_p_kernel(
         add_turned(sum_d[:, half(0)], windows[D][:, half(0)], first=True)
         add_turned(lead_a0, fetched[A, 0], final=True)
         add_turned(lead_b1, fetched[B, 1], final=True)
+        load_result(C, 1, "both")
         load_result(D, 0, "fetched0_0")
         load_result(D, 1, "fetched1_1")
         add_turned(sum_b, results[B, 1])
@@ -292,9 +287,9 @@ def tile_picked_elo8_none_p_kernel(
         add_turned(sum_d, results[D, 0])
         win_c1 = squash("win_c1", gap_c1, 1.0, "win_a1")
         add_turned(sum_c, win_c1, final=True)
+        add_turned(sum_d, results[D, 1])
         total_b = close("total_b", sum_b, 1.0)
         add_turned(back_b, total_b, final=True)
-        add_turned(sum_d, results[D, 1])
         win_d0 = squash("win_d0", gap_d0, STEP, "fetched2_0")
         add_turned(sum_d, win_d0, final=True)
         for h in range(2):
@@ -315,8 +310,8 @@ def tile_picked_elo8_none_p_kernel(
 
         gaps = [last_gap(0, "win_a0")]
         finish(A, back_a, -STEP, base)
-        finish(B, back_b, STEP, windows[B])
-        gaps.append(last_gap(1, "total_b"))
+        gaps.append(last_gap(1, "win_b1"))
+        finish(B, back_b, STEP, windows[B], width=HALF)
         for h in range(2):
             finish_half(C, h, back_c[h][:], windows[C][:, half(h)])
         wins = [squash("win_d1_0", gaps[0], STEP, "win_a1")]

@@ -141,8 +141,10 @@ def tile_picked_elo8_none_p_kernel(
         for h, g, tag in ((0, 0, "grouped0_0"), (0, 1, "w_raw0"), (1, 0, "grouped0_1"), (1, 1, "grouped1_0")):
             first_results[g, h] = wide("res0_%d_%d" % (g, h), tag, HALF)
             nc.sync.dma_start(out=first_results[g, h][:], in_=res_rows[g][:, A, half(h)])
-        for b, g, tag in ((B, 0, "w_raw1"), (B, 1, "picked_scales"), (C, 0, "grouped1_1")):
-            load_result(b, g, tag)
+        for g, tag in enumerate(("w_raw1", "grouped1_1")):
+            rows = wide("res12_%d" % g, tag, 2 * S)
+            nc.sync.dma_start(out=rows[:].rearrange("p (b j) -> p b j", b=2), in_=res_rows[g][:, B : C + 1, :])
+            results[B, g], results[C, g] = rows[:, :S], rows[:, S:]
 
         def bank(name, number, width=S):
             return psum.tile([P, width], F32, name=name, tag="bank%d" % number)
@@ -262,7 +264,6 @@ def tile_picked_elo8_none_p_kernel(
         add_turned(sum_d[:, half(0)], windows[D][:, half(0)], first=True)
         add_turned(lead_a0, fetched[A, 0], final=True)
         add_turned(lead_b1, fetched[B, 1], final=True)
-        load_result(C, 1, "both")
         load_result(D, 0, "fetched0_0")
         load_result(D, 1, "fetched1_1")
         add_turned(sum_b, results[B, 1])

@@ -19,15 +19,14 @@ ACT = mybir.ActivationFunctionType
 P = 128
 PACK = 4
 PASSES = K // (P * PACK)
-BLOCKS = N // P
-CHUNKS = S // P
+PARTS = N // P
 HALF = S // 2
 STRIPE = 16
-QUADRANTS = 4
+QUADRANT = 32
 SCALE_ROWS = 4
 GAMES = 2
 STEP = 0.75
-EARLY, LATE = (0, 1), (2, 3)
+A, B, C, D = range(PARTS)
 
 
 def tile_picked_elo8_none_p_kernel(
@@ -44,11 +43,11 @@ def tile_picked_elo8_none_p_kernel(
 
         scale_table = keep.tile([P, T], U8, name="scale_table", tag="scale_table", align_bytes=64)
         nc.sync.dma_start(
-            out=scale_table[0:32, :].bitcast(I32), in_=x_scales.rearrange("z r c -> r z c").bitcast(I32)
+            out=scale_table[:QUADRANT, :].bitcast(I32), in_=x_scales.rearrange("z r c -> r z c").bitcast(I32)
         )
         nc.sync.dma_start(picks[:], offs)
-        nc.gpsimd.memset(scale_table[32:64, :].bitcast(I32), 0)
-        nc.gpsimd.memset(scale_table[64:128, :].bitcast(I32), 0)
+        nc.gpsimd.memset(scale_table[QUADRANT : 2 * QUADRANT, :].bitcast(I32), 0)
+        nc.gpsimd.memset(scale_table[2 * QUADRANT :, :].bitcast(I32), 0)
         x_planes = keep.tile([P, PASSES * S], U8, name="x_planes", align_bytes=64)
         nc.gpsimd.memset(x_planes[:].bitcast(I32), 0)
 
@@ -76,21 +75,23 @@ def tile_picked_elo8_none_p_kernel(
         ident = keep.tile([P, P], F32, name="ident")
         make_identity(nc, ident[:])
 
-        windows = [keep.tile([P, 2 * S], F32, name="window%d" % b) for b in range(BLOCKS)]
+        windows = [keep.tile([P, 2 * S], F32, name="window%d" % b) for b in range(PARTS)]
         for window in windows:
             nc.gpsimd.memset(window[:, S:], 0.0)
 
         picked_scales = keep.tile([P, S], U8, name="picked_scales", tag="picked_scales", align_bytes=64)
         nc.vector.tensor_copy(picked_scales[:], scale_table[:].indirect(picks[:]))
-        for q in range(QUADRANTS):
-            rows = PASSES * SCALE_ROWS
+        moved = PASSES * SCALE_ROWS
+        for q in range(P // QUADRANT):
             nc.sync.dma_start(
-                out=x_planes[32 * q : 32 * q + SCALE_ROWS, :].bitcast(I32),
-                in_=picked_scales[rows * q : rows * (q + 1), :].bitcast(I32),
+                out=x_planes[QUADRANT * q : QUADRANT * q + SCALE_ROWS, :].bitcast(I32),
+                in_=picked_scales[moved * q : moved * (q + 1), :].bitcast(I32),
             )
         word_table.append(load_words(1, "scale_table"))
 
-        x_codes = [keep.tile([P, S], U32, name="x_codes%d" % z, tag="x_codes%d" % z, align_bytes=64) for z in range(PASSES)]
+        x_codes = [
+            keep.tile([P, S], U32, name="x_codes%d" % z, tag="x_codes%d" % z, align_bytes=64) for z in range(PASSES)
+        ]
         grouped, w_codes, w_planes = {}, {}, {}
 
         def quantize(z, u, tag):
@@ -102,54 +103,53 @@ def tile_picked_elo8_none_p_kernel(
                 in_=grouped[z, u][:].rearrange("p e c t -> p (e c t)"),
             )
 
-        for z in range(PASSES):
+        def cast_weights(z):
             cast_from = w_raw[z][:].rearrange("p t (c u e) -> p u c e t", u=2, e=2)
             for u, cast in enumerate((nc.vector.tensor_copy, nc.scalar.copy)):
                 grouped[z, u] = keep.tile(
                     [P, 2, P, PACK], BF16, name="grouped%d_%d" % (z, u), tag="grouped%d_%d" % (z, u), align_bytes=64
                 )
                 cast(out=grouped[z, u][:].rearrange("p e c t -> p c e t"), in_=cast_from[:, u])
-            quantize(z, 0, "w_codes%d" % z)
-            if z == 0:
-                quantize(0, 1, "w_codes_late")
 
-        for z in range(PASSES):
+        def gather_words(z):
             for j0 in (0, HALF):
                 nc.vector.tensor_copy(
                     x_codes[z][:, j0 : j0 + HALF],
                     word_table[z][:].bitcast(U32).indirect(picks[:, j0 // STRIPE : (j0 + HALF) // STRIPE]),
                 )
-            if z == 0:
-                quantize(1, 1, "word_table0")
 
-        A, B, C, D = range(BLOCKS)
-        res_rows = [res.rearrange("(p b) j -> p b j", b=BLOCKS) for res in (res1, res2)]
-        out_rows = out.rearrange("(p b) j -> p b j", b=BLOCKS)
+        cast_weights(0)
+        quantize(0, 0, "w_codes0_0")
+        quantize(0, 1, "w_codes0_1")
+        cast_weights(1)
+        quantize(1, 0, "w_codes1_0")
+        gather_words(0)
+        quantize(1, 1, "word_table0")
+        gather_words(1)
+
+        res_rows = [res.rearrange("(p b) j -> p b j", b=PARTS) for res in (res1, res2)]
+        out_rows = out.rearrange("(p b) j -> p b j", b=PARTS)
         results = {}
 
         def wide(name, tag=None, width=S):
             return keep.tile([P, width], F32, name=name, tag=tag or name, align_bytes=64)
 
-        def load_result(b, g, tag):
-            results[b, g] = wide("res%d_%d" % (b, g), tag)
-            nc.sync.dma_start(out=results[b, g][:], in_=res_rows[g][:, b, :])
-
         def half(h):
             return slice(h * HALF, (h + 1) * HALF)
 
-        first_results = {}
+        a_results = {}
         for h, g, tag in ((0, 0, "grouped0_0"), (0, 1, "w_raw0"), (1, 0, "grouped0_1"), (1, 1, "grouped1_0")):
-            first_results[g, h] = wide("res0_%d_%d" % (g, h), tag, HALF)
-            nc.sync.dma_start(out=first_results[g, h][:], in_=res_rows[g][:, A, half(h)])
+            a_results[g, h] = wide("res0_%d_%d" % (g, h), tag, HALF)
+            nc.sync.dma_start(out=a_results[g, h][:], in_=res_rows[g][:, A, half(h)])
         for g, tag in enumerate(("w_raw1", "grouped1_1")):
-            rows = wide("res12_%d" % g, tag, 2 * S)
-            nc.sync.dma_start(out=rows[:].rearrange("p (b j) -> p b j", b=2), in_=res_rows[g][:, B : C + 1, :])
-            results[B, g], results[C, g] = rows[:, :S], rows[:, S:]
+            pair = wide("res12_%d" % g, tag, 2 * S)
+            nc.sync.dma_start(out=pair[:].rearrange("p (b j) -> p b j", b=2), in_=res_rows[g][:, B : C + 1, :])
+            results[B, g], results[C, g] = pair[:, :S], pair[:, S:]
 
         def bank(name, number, width=S):
             return psum.tile([P, width], F32, name=name, tag="bank%d" % number)
 
-        pieces = [(b, h) for h in range(2) for b in range(BLOCKS)]
+        pieces = [(b, h) for h in range(2) for b in range(PARTS)]
         ratings = {piece: bank("rating%d_%d" % piece, i, HALF) for i, piece in enumerate(pieces)}
         for z in range(PASSES):
             for b, h in pieces:
@@ -158,43 +158,28 @@ def tile_picked_elo8_none_p_kernel(
                     out=ratings[b, h][:],
                     lhsT=w_codes[z, u][:, features].bitcast(FP8X4),
                     lhsT_scale=w_planes[z, u][:, features],
-                    rhs=x_codes[z][:, h * HALF : (h + 1) * HALF].bitcast(FP8X4),
+                    rhs=x_codes[z][:, half(h)].bitcast(FP8X4),
                     rhs_scale=x_planes[:, z * S + h * HALF : z * S + (h + 1) * HALF],
                     start=(z == 0),
                     stop=(z == PASSES - 1),
                 )
 
-        def entries(g, j0, width):
-            return rivals[g][:, j0 // STRIPE : (j0 + width) // STRIPE]
-
         window_scale = {A: 1.0, B: 1.0, C: 1.0, D: 1.0 / STEP}
-
-        def leave_by_scalar(b, h):
-            nc.scalar.activation(
-                out=windows[b][:, half(h)], in_=ratings[b, h][:], func=ACT.Copy, scale=window_scale[b]
-            )
-
-        def leave_by_vector(b, h):
-            nc.vector.tensor_scalar(windows[b][:, half(h)], ratings[b, h][:], window_scale[b], None, ALU.mult)
-
-        plain = {b: wide("plain%d" % b) for b in (B, C, D)}
-
-        leave_by_vector(A, 0)
-        leave_by_scalar(B, 0)
-        nc.sync.dma_start(out=plain[B][:, half(0)], in_=windows[B][:, half(0)])
-        leave_by_vector(C, 0)
-        leave_by_scalar(D, 0)
-        leave_by_vector(A, 1)
-        leave_by_scalar(B, 1)
-        nc.sync.dma_start(out=plain[B][:, half(1)], in_=windows[B][:, half(1)])
-        leave_by_vector(C, 1)
-        nc.sync.dma_start(out=plain[C][:], in_=windows[C][:, :S])
-        leave_by_scalar(D, 1)
-        nc.sync.dma_start(out=plain[D][:], in_=windows[D][:, :S])
+        second = {b: wide("second%d" % b) for b in (B, C, D)}
+        for b, h in pieces:
+            into = windows[b][:, half(h)]
+            if b in (A, C):
+                nc.vector.tensor_scalar(into, ratings[b, h][:], window_scale[b], None, ALU.mult)
+            else:
+                nc.scalar.activation(out=into, in_=ratings[b, h][:], func=ACT.Copy, scale=window_scale[b])
+            if b == B:
+                nc.sync.dma_start(out=second[B][:, half(h)], in_=into)
+            elif b != A and h == 1:
+                nc.sync.dma_start(out=second[b][:], in_=windows[b][:, :S])
 
         both = wide("both")
         for h in range(2):
-            nc.gpsimd.tensor_tensor(both[:, half(h)], first_results[0, h][:], first_results[1, h][:], ALU.add)
+            nc.gpsimd.tensor_tensor(both[:, half(h)], a_results[0, h][:], a_results[1, h][:], ALU.add)
         scaled = wide("scaled")
         nc.gpsimd.tensor_scalar(scaled[:], both[:], STEP, 0.0, ALU.mult, ALU.add)
         base = wide("base")
@@ -218,28 +203,23 @@ def tile_picked_elo8_none_p_kernel(
             nc.scalar.activation(out=win[:], in_=gap[:], func=ACT.Sigmoid, scale=scale)
             return win
 
-        def fetch_and_subtract(b, g, width=S, tag=None):
-            gap = wide("gap%d_%d" % (b, g), tag)
-            for j0 in range(0, S, width):
-                nc.vector.tensor_tensor(
-                    gap[:, j0 : j0 + width],
-                    windows[b][:].indirect(entries(g, j0, width)),
-                    plain[b][:, j0 : j0 + width],
-                    ALU.subtract,
-                )
-            return gap
+        def fetch_and_subtract(gap, b, g, j0):
+            width = gap.shape[1]
+            offsets = rivals[g][:, j0 // STRIPE : (j0 + width) // STRIPE]
+            nc.vector.tensor_tensor(gap, windows[b][:].indirect(offsets), second[b][:, j0 : j0 + width], ALU.subtract)
 
-        def close(name, total, scale, tag=None):
-            closed = wide(name, tag, total.shape[1])
+        def close(name, total, scale):
+            closed = wide(name, None, total.shape[1])
             nc.scalar.activation(out=closed[:], in_=total[:], func=ACT.Copy, scale=scale, bias=-GAMES * scale)
             return closed
 
-        def finish(b, last, factor, before, tag=None, width=S):
-            done = wide("done%d" % b, tag)
-            for j0 in range(0, S, width):
-                cols = slice(j0, j0 + width)
-                nc.vector.scalar_tensor_tensor(done[:, cols], last[:, cols], factor, before[:, cols], ALU.mult, ALU.add)
-                nc.sync.dma_start(out=out_rows[:, b, cols], in_=done[:, cols])
+        def finish(done, b, cols, scaled_term, factor, other_term):
+            nc.vector.scalar_tensor_tensor(done, scaled_term, factor, other_term, ALU.mult, ALU.add)
+            nc.sync.dma_start(out=out_rows[:, b, cols], in_=done)
+
+        def load_d_result(g, tag):
+            results[D, g] = wide("res3_%d" % g, tag)
+            nc.sync.dma_start(out=results[D, g][:], in_=res_rows[g][:, D, :])
 
         fetched = {}
         for g in range(GAMES):
@@ -247,11 +227,14 @@ def tile_picked_elo8_none_p_kernel(
             nc.vector.tensor_scalar(fetched[A, g][:], windows[A][:].indirect(rivals[g][:]), -1.0, 0.0, ALU.mult, ALU.add)
         for b, g in ((B, 1), (C, 0)):
             fetched[b, g] = wide("fetched%d_%d" % (b, g))
-        nc.scalar.activation(out=fetched[B, 1][:], in_=windows[B][:].indirect(rivals[1][:]), func=ACT.Copy, scale=-1.0)
-        nc.scalar.activation(out=fetched[C, 0][:], in_=windows[C][:].indirect(rivals[0][:]), func=ACT.Copy, scale=-1.0)
-        gap_b0 = fetch_and_subtract(B, 0, HALF)
-        gap_c1 = fetch_and_subtract(C, 1)
-        gap_d0 = fetch_and_subtract(D, 0)
+            nc.scalar.activation(out=fetched[b, g][:], in_=windows[b][:].indirect(rivals[g][:]), func=ACT.Copy, scale=-1.0)
+        gap_b0 = wide("gap_b0")
+        for h in range(2):
+            fetch_and_subtract(gap_b0[:, half(h)], B, 0, h * HALF)
+        gap_c1 = wide("gap_c1")
+        fetch_and_subtract(gap_c1[:], C, 1, 0)
+        gap_d0 = wide("gap_d0")
+        fetch_and_subtract(gap_d0[:], D, 0, 0)
 
         lead_a0, lead_a1, lead_b1 = bank("lead_a0", 0), bank("lead_a1", 1), bank("lead_b1", 2)
         sum_b, back_a, lead_c0 = bank("sum_b", 3), bank("back_a", 4), bank("lead_c0", 5)
@@ -264,8 +247,8 @@ def tile_picked_elo8_none_p_kernel(
         add_turned(sum_d[:, half(0)], windows[D][:, half(0)], first=True)
         add_turned(lead_a0, fetched[A, 0], final=True)
         add_turned(lead_b1, fetched[B, 1], final=True)
-        load_result(D, 0, "fetched0_0")
-        load_result(D, 1, "fetched1_1")
+        load_d_result(0, "fetched0_0")
+        load_d_result(1, "fetched1_1")
         add_turned(sum_b, results[B, 1])
         add_turned(lead_a1, fetched[A, 1], final=True)
         add_turned(lead_c0, fetched[C, 0], final=True)
@@ -281,12 +264,12 @@ def tile_picked_elo8_none_p_kernel(
         win_b0 = squash("win_b0", gap_b0, 1.0, "fetched2_0")
         add_turned(sum_b, win_b0, final=True)
         add_turned(sum_d[:, half(1)], windows[D][:, half(1)])
-        win_c0 = squash("win_c0", lead_c0, -1.0, "win_b1")
+        win_c0 = squash("win_c0", lead_c0, -1.0, "win_a0")
         back_c = [bank("back_c%d" % h, number, HALF) for h, number in enumerate((2, 1))]
         for h in range(2):
             add_turned(back_c[h], win_c0[:, half(h)], first=True)
         add_turned(sum_d, results[D, 0])
-        win_c1 = squash("win_c1", gap_c1, 1.0, "win_a1")
+        win_c1 = squash("win_c1", gap_c1, 1.0, "win_b1")
         add_turned(sum_c, win_c1, final=True)
         add_turned(sum_d, results[D, 1])
         total_b = close("total_b", sum_b, 1.0)
@@ -297,29 +280,24 @@ def tile_picked_elo8_none_p_kernel(
             total_c = close("total_c%d" % h, sum_c[:, half(h)], 1.0)
             add_turned(back_c[h], total_c, final=True)
 
-        def last_gap(h, tag):
-            gap = wide("last_gap%d" % h, tag, HALF)
-            nc.vector.tensor_tensor(
-                gap[:], windows[D][:].indirect(entries(1, h * HALF, HALF)), plain[D][:, half(h)], ALU.subtract
-            )
-            return gap
-
-        def finish_half(b, h, last, before):
-            done = wide("done%d_%d" % (b, h), None, HALF)
-            nc.vector.scalar_tensor_tensor(done[:], last, STEP, before, ALU.mult, ALU.add)
-            nc.sync.dma_start(out=out_rows[:, b, half(h)], in_=done[:])
-
-        gaps = [last_gap(0, "win_a0")]
-        finish(A, back_a, -STEP, base)
-        gaps.append(last_gap(1, "win_b1"))
-        finish(B, back_b, STEP, windows[B], width=HALF)
+        last_gaps = [wide("last_gap0", "win_a1", HALF)]
+        fetch_and_subtract(last_gaps[0][:], D, 1, 0)
+        done_a = wide("done_a")
+        finish(done_a[:], A, slice(0, S), back_a[:], -STEP, base[:])
+        last_gaps.append(wide("last_gap1", "win_a0", HALF))
+        fetch_and_subtract(last_gaps[1][:], D, 1, HALF)
+        done_b = wide("done_b")
         for h in range(2):
-            finish_half(C, h, back_c[h][:], windows[C][:, half(h)])
-        wins = [squash("win_d1_0", gaps[0], STEP, "win_a1")]
+            finish(done_b[:, half(h)], B, half(h), back_b[:, half(h)], STEP, windows[B][:, half(h)])
+        for h in range(2):
+            done_c = wide("done_c%d" % h, None, HALF)
+            finish(done_c[:], C, half(h), back_c[h][:], STEP, windows[C][:, half(h)])
+        last_wins = [squash("last_win0", last_gaps[0], STEP, "win_b1")]
         back_d = [bank("back_d%d" % h, number, HALF) for h, number in enumerate((5, 3))]
         for h in range(2):
             total_d = close("total_d%d" % h, sum_d[:, half(h)], STEP)
             add_turned(back_d[h], total_d, first=True, final=True)
-        wins.append(squash("win_d1_1", gaps[1], STEP, "fetched2_0"))
+        last_wins.append(squash("last_win1", last_gaps[1], STEP, "fetched2_0"))
         for h in range(2):
-            finish_half(D, h, wins[h][:], back_d[h][:])
+            done_d = wide("done_d%d" % h, None, HALF)
+            finish(done_d[:], D, half(h), last_wins[h][:], STEP, back_d[h][:])

@@ -129,7 +129,6 @@ def tile_picked_elo8_none_p_kernel(
 
         res_rows = [res.rearrange("(p b) j -> p b j", b=PARTS) for res in (res1, res2)]
         out_rows = out.rearrange("(p b) j -> p b j", b=PARTS)
-        results = {}
 
         def wide(name, tag=None, width=S):
             return keep.tile([P, width], F32, name=name, tag=tag or name, align_bytes=64)
@@ -137,14 +136,21 @@ def tile_picked_elo8_none_p_kernel(
         def half(h):
             return slice(h * HALF, (h + 1) * HALF)
 
-        a_results = {}
-        for h, g, tag in ((0, 0, "grouped0_0"), (0, 1, "w_raw0"), (1, 0, "grouped0_1"), (1, 1, "grouped1_0")):
-            a_results[g, h] = wide("res0_%d_%d" % (g, h), tag, HALF)
-            nc.sync.dma_start(out=a_results[g, h][:], in_=res_rows[g][:, A, half(h)])
-        for g, tag in enumerate(("w_raw1", "grouped1_1")):
-            pair = wide("res12_%d" % g, tag, 2 * S)
-            nc.sync.dma_start(out=pair[:].rearrange("p (b j) -> p b j", b=2), in_=res_rows[g][:, B : C + 1, :])
-            results[B, g], results[C, g] = pair[:, :S], pair[:, S:]
+        results = {}
+
+        def load_results(b, tag, pieces):
+            both_games = wide("results%d" % b, tag, GAMES * S)
+            for g in range(GAMES):
+                results[b, g] = both_games[:, g * S : (g + 1) * S]
+            for cols in pieces:
+                for g in range(GAMES):
+                    nc.sync.dma_start(out=results[b, g][:, cols], in_=res_rows[g][:, b, cols])
+
+        whole = slice(0, S)
+        load_results(B, "w_raw0", [half(0), half(1)])
+        load_results(A, "grouped0_1", [whole])
+        load_results(C, "w_raw1", [whole])
+        load_results(D, "grouped1_1", [whole])
 
         def bank(name, number, width=S):
             return psum.tile([P, width], F32, name=name, tag="bank%d" % number)
@@ -164,26 +170,39 @@ def tile_picked_elo8_none_p_kernel(
                     stop=(z == PASSES - 1),
                 )
 
-        window_scale = {A: 1.0, B: 1.0, C: 1.0, D: 1.0 / STEP}
-        second = {b: wide("second%d" % b) for b in (B, C, D)}
         for b, h in pieces:
-            into = windows[b][:, half(h)]
             if b in (A, C):
-                nc.vector.tensor_scalar(into, ratings[b, h][:], window_scale[b], None, ALU.mult)
+                nc.vector.tensor_copy(windows[b][:, half(h)], ratings[b, h][:])
             else:
-                nc.scalar.activation(out=into, in_=ratings[b, h][:], func=ACT.Copy, scale=window_scale[b])
-            if b == B:
-                nc.sync.dma_start(out=second[B][:, half(h)], in_=into)
-            elif b != A and h == 1:
-                nc.sync.dma_start(out=second[b][:], in_=windows[b][:, :S])
+                nc.scalar.copy(out=windows[b][:, half(h)], in_=ratings[b, h][:])
 
-        both = wide("both")
+        summed = [[wide("summed%d_%d" % (b, h), None, HALF) for h in range(2)] if b == A else wide("summed%d" % b) for b in range(PARTS)]
+        scaled = {b: wide("scaled%d" % b) for b in (B, C, D)}
+        bases = [wide("base%d" % b) for b in range(PARTS)]
+
+        def add_results(b, cols):
+            nc.gpsimd.tensor_tensor(summed[b][:, cols], results[b, 0][:, cols], results[b, 1][:, cols], ALU.add)
+
+        def scale_results(b, cols):
+            nc.gpsimd.tensor_scalar(scaled[b][:, cols], summed[b][:, cols], STEP, 0.0, ALU.mult, ALU.add)
+
+        def add_ratings(b, cols):
+            nc.gpsimd.tensor_tensor(bases[b][:, cols], scaled[b][:, cols], windows[b][:, cols], ALU.add)
+
         for h in range(2):
-            nc.gpsimd.tensor_tensor(both[:, half(h)], a_results[0, h][:], a_results[1, h][:], ALU.add)
-        scaled = wide("scaled")
-        nc.gpsimd.tensor_scalar(scaled[:], both[:], STEP, 0.0, ALU.mult, ALU.add)
-        base = wide("base")
-        nc.gpsimd.tensor_tensor(base[:], scaled[:], windows[A][:, :S], ALU.add)
+            add_results(B, half(h))
+        for h in range(2):
+            scale_results(B, half(h))
+        for h in range(2):
+            nc.gpsimd.tensor_tensor(summed[A][h][:], results[A, 0][:, half(h)], results[A, 1][:, half(h)], ALU.add)
+        add_ratings(B, whole)
+        add_results(C, whole)
+        add_results(D, whole)
+        scale_results(C, whole)
+        scale_results(D, whole)
+        add_ratings(C, whole)
+        for h in range(2):
+            add_ratings(D, half(h))
 
         def add_turned(target, values, first=False, final=False):
             chunks = target.shape[1] // P
@@ -198,106 +217,99 @@ def tile_picked_elo8_none_p_kernel(
                     is_transpose=True,
                 )
 
-        def squash(name, gap, scale, tag=None):
+        def fetch(engine, name, b, g, j0=0, j1=S, tag=None):
+            into = wide(name, tag, j1 - j0)
+            picked = windows[b][:].indirect(rivals[g][:, j0 // STRIPE : j1 // STRIPE])
+            if engine is nc.vector:
+                nc.vector.tensor_scalar(into[:], picked, -1.0, 0.0, ALU.mult, ALU.add)
+            else:
+                nc.scalar.activation(out=into[:], in_=picked, func=ACT.Copy, scale=-1.0)
+            return into
+
+        def open_lead(name, number, b, cols=whole):
+            lead = bank(name, number, cols.stop - cols.start)
+            add_turned(lead, windows[b][:, cols], first=True)
+            return lead
+
+        def squash(name, gap, tag=None):
             win = wide(name, tag, gap.shape[1])
-            nc.scalar.activation(out=win[:], in_=gap[:], func=ACT.Sigmoid, scale=scale)
+            nc.scalar.activation(out=win[:], in_=gap, func=ACT.Sigmoid)
             return win
 
-        def fetch_and_subtract(gap, b, g, j0):
-            width = gap.shape[1]
-            offsets = rivals[g][:, j0 // STRIPE : (j0 + width) // STRIPE]
-            nc.vector.tensor_tensor(gap, windows[b][:].indirect(offsets), second[b][:, j0 : j0 + width], ALU.subtract)
-
-        def close(name, total, scale):
-            closed = wide(name, None, total.shape[1])
-            nc.scalar.activation(out=closed[:], in_=total[:], func=ACT.Copy, scale=scale, bias=-GAMES * scale)
-            return closed
-
-        def finish(done, b, cols, scaled_term, factor, other_term):
-            nc.vector.scalar_tensor_tensor(done, scaled_term, factor, other_term, ALU.mult, ALU.add)
+        def finish(done, b, cols, back, base):
+            nc.vector.scalar_tensor_tensor(done, back, -STEP, base, ALU.mult, ALU.add)
             nc.sync.dma_start(out=out_rows[:, b, cols], in_=done)
 
-        def load_d_result(g, tag):
-            results[D, g] = wide("res3_%d" % g, tag)
-            nc.sync.dma_start(out=results[D, g][:], in_=res_rows[g][:, D, :])
+        got_a0 = fetch(nc.vector, "got_a0", A, 0)
+        got_b0 = fetch(nc.scalar, "got_b0", B, 0)
+        got_a1 = fetch(nc.vector, "got_a1", A, 1)
+        got_b1 = fetch(nc.scalar, "got_b1", B, 1)
+        got_c0 = fetch(nc.vector, "got_c0", C, 0)
 
-        fetched = {}
-        for g in range(GAMES):
-            fetched[A, g] = wide("fetched0_%d" % g)
-            nc.vector.tensor_scalar(fetched[A, g][:], windows[A][:].indirect(rivals[g][:]), -1.0, 0.0, ALU.mult, ALU.add)
-        for b, g in ((B, 1), (C, 0)):
-            fetched[b, g] = wide("fetched%d_%d" % (b, g))
-            nc.scalar.activation(out=fetched[b, g][:], in_=windows[b][:].indirect(rivals[g][:]), func=ACT.Copy, scale=-1.0)
-        gap_b0 = wide("gap_b0")
-        for h in range(2):
-            fetch_and_subtract(gap_b0[:, half(h)], B, 0, h * HALF)
-        gap_c1 = wide("gap_c1")
-        fetch_and_subtract(gap_c1[:], C, 1, 0)
-        gap_d0 = wide("gap_d0")
-        fetch_and_subtract(gap_d0[:], D, 0, 0)
-
-        lead_a0, lead_a1, lead_b1 = bank("lead_a0", 0), bank("lead_a1", 1), bank("lead_b1", 2)
-        sum_b, back_a, lead_c0 = bank("sum_b", 3), bank("back_a", 4), bank("lead_c0", 5)
-        sum_c, sum_d = bank("sum_c", 6), bank("sum_d", 7)
-        add_turned(lead_a0, windows[A], first=True)
-        add_turned(lead_a1, windows[A], first=True)
-        add_turned(lead_b1, windows[B], first=True)
-        add_turned(lead_c0, windows[C], first=True)
-        add_turned(sum_b, results[B, 0], first=True)
-        add_turned(sum_d[:, half(0)], windows[D][:, half(0)], first=True)
-        add_turned(lead_a0, fetched[A, 0], final=True)
-        add_turned(lead_b1, fetched[B, 1], final=True)
-        load_d_result(0, "fetched0_0")
-        load_d_result(1, "fetched1_1")
-        add_turned(sum_b, results[B, 1])
-        add_turned(lead_a1, fetched[A, 1], final=True)
-        add_turned(lead_c0, fetched[C, 0], final=True)
-        win_a0 = squash("win_a0", lead_a0, 1.0)
-        add_turned(back_a, win_a0, first=True)
-        add_turned(sum_c, results[C, 0], first=True)
-        win_b1 = squash("win_b1", lead_b1, -1.0)
-        back_b = bank("back_b", 0)
-        add_turned(back_b, win_b1, first=True)
-        add_turned(sum_c, results[C, 1])
-        win_a1 = squash("win_a1", lead_a1, 1.0)
-        add_turned(back_a, win_a1, final=True)
-        win_b0 = squash("win_b0", gap_b0, 1.0, "fetched2_0")
-        add_turned(sum_b, win_b0, final=True)
-        add_turned(sum_d[:, half(1)], windows[D][:, half(1)])
-        win_c0 = squash("win_c0", lead_c0, -1.0, "win_a0")
-        back_c = [bank("back_c%d" % h, number, HALF) for h, number in enumerate((2, 1))]
+        lead_a0 = open_lead("lead_a0", 1, A)
+        lead_a1 = open_lead("lead_a1", 2, A)
+        lead_b0 = open_lead("lead_b0", 3, B)
+        lead_b1 = open_lead("lead_b1", 5, B)
+        lead_d0 = open_lead("lead_d0", 7, D)
+        add_turned(lead_a0, got_a0, final=True)
+        add_turned(lead_b0, got_b0, final=True)
+        lead_c0 = open_lead("lead_c0", 6, C)
+        sum_a = bank("sum_a", 4, HALF)
+        add_turned(sum_a, summed[A][1], first=True, final=True)
+        add_turned(lead_a1, got_a1, final=True)
+        add_turned(lead_b1, got_b1, final=True)
+        nc.vector.scalar_tensor_tensor(
+            bases[A][:, half(0)], summed[A][0][:], STEP, ratings[A, 0][:], ALU.mult, ALU.add
+        )
+        owed = wide("owed", None, HALF)
+        nc.vector.tensor_scalar(owed[:], sum_a[:], -1.0, None, ALU.mult)
+        got_c1 = fetch(nc.vector, "got_c1", C, 1, tag="summed0_1")
+        back_a = bank("back_a", 1)
+        add_turned(back_a, squash("win_a0", lead_a0[:]), first=True)
+        add_turned(lead_c0, got_c0, final=True)
+        back_b = bank("back_b", 3)
+        add_turned(back_b, squash("win_b0", lead_b0[:]), first=True)
+        add_turned(back_a[:, half(1)], owed)
+        add_turned(back_a, squash("win_a1", lead_a1[:]), final=True)
+        lead_c1 = open_lead("lead_c1", 0, C)
+        lead_d1 = [open_lead("lead_d1_%d" % h, number, D, half(h)) for h, number in enumerate((4, 2))]
+        add_turned(lead_c1, got_c1, final=True)
+        win_b1 = squash("win_b1", lead_b1[:])
+        got_d0 = fetch(nc.scalar, "got_d0", D, 0, tag="win_a0")
+        done_a = wide("done_a")
+        nc.vector.scalar_tensor_tensor(done_a[:, half(0)], back_a[:, half(0)], -STEP, bases[A][:, half(0)], ALU.mult, ALU.add)
+        nc.vector.scalar_tensor_tensor(done_a[:, half(1)], back_a[:, half(1)], -STEP, windows[A][:, half(1)], ALU.mult, ALU.add)
+        nc.sync.dma_start(out=out_rows[:, A, :], in_=done_a[:])
+        got_d1 = [fetch(nc.vector, "got_d1_%d" % h, D, 1, h * HALF, (h + 1) * HALF, tag) for h, tag in enumerate(("owed", "win_a1"))]
+        add_turned(back_b, win_b1, final=True)
+        add_turned(lead_d0, got_d0, final=True)
+        add_turned(lead_d1[0], got_d1[0], final=True)
+        back_c = [bank("back_c%d" % h, number, HALF) for h, number in enumerate((5, 1))]
+        win_c0 = squash("win_c0", lead_c0[:], "win_b0")
         for h in range(2):
             add_turned(back_c[h], win_c0[:, half(h)], first=True)
-        add_turned(sum_d, results[D, 0])
-        win_c1 = squash("win_c1", gap_c1, 1.0, "win_b1")
-        add_turned(sum_c, win_c1, final=True)
-        add_turned(sum_d, results[D, 1])
-        total_b = close("total_b", sum_b, 1.0)
-        add_turned(back_b, total_b, final=True)
-        win_d0 = squash("win_d0", gap_d0, STEP, "fetched2_0")
-        add_turned(sum_d, win_d0, final=True)
-        for h in range(2):
-            total_c = close("total_c%d" % h, sum_c[:, half(h)], 1.0)
-            add_turned(back_c[h], total_c, final=True)
+        win_c1 = [squash("win_c1_%d" % h, lead_c1[:, half(h)]) for h in range(2)]
+        add_turned(back_c[0], win_c1[0], final=True)
+        add_turned(lead_d1[1], got_d1[1], final=True)
+        add_turned(back_c[1], win_c1[1], final=True)
+        finish(wide("done_b")[:], B, whole, back_b[:], bases[B][:])
 
-        last_gaps = [wide("last_gap0", "win_a1", HALF)]
-        fetch_and_subtract(last_gaps[0][:], D, 1, 0)
-        done_a = wide("done_a")
-        finish(done_a[:], A, slice(0, S), back_a[:], -STEP, base[:])
-        last_gaps.append(wide("last_gap1", "win_a0", HALF))
-        fetch_and_subtract(last_gaps[1][:], D, 1, HALF)
-        done_b = wide("done_b")
+        back_d = [bank("back_d0", 6, HALF), bank("back_d1", 0, P), bank("back_d2", 3, P)]
+        add_turned(back_d[0], squash("win_d0_0", lead_d0[:, half(0)]), first=True)
+        add_turned(back_d[0], squash("win_d1_0", lead_d1[0][:]), final=True)
+        win_d0 = squash("win_d0_1", lead_d0[:, half(1)])
+        for q in range(2):
+            add_turned(back_d[1 + q], win_d0[:, q * P : (q + 1) * P], first=True)
+        for q in range(2):
+            add_turned(back_d[1 + q], squash("win_d1_%d" % (1 + q), lead_d1[1][:, q * P : (q + 1) * P]), final=True)
+
+        done_c = wide("done_c")
         for h in range(2):
-            finish(done_b[:, half(h)], B, half(h), back_b[:, half(h)], STEP, windows[B][:, half(h)])
-        for h in range(2):
-            done_c = wide("done_c%d" % h, None, HALF)
-            finish(done_c[:], C, half(h), back_c[h][:], STEP, windows[C][:, half(h)])
-        last_wins = [squash("last_win0", last_gaps[0], STEP, "win_b1")]
-        back_d = [bank("back_d%d" % h, number, HALF) for h, number in enumerate((5, 3))]
-        for h in range(2):
-            total_d = close("total_d%d" % h, sum_d[:, half(h)], STEP)
-            add_turned(back_d[h], total_d, first=True, final=True)
-        last_wins.append(squash("last_win1", last_gaps[1], STEP, "fetched2_0"))
-        for h in range(2):
-            done_d = wide("done_d%d" % h, None, HALF)
-            finish(done_d[:], D, half(h), last_wins[h][:], STEP, back_d[h][:])
+            nc.vector.scalar_tensor_tensor(done_c[:, half(h)], back_c[h][:], -STEP, bases[C][:, half(h)], ALU.mult, ALU.add)
+        nc.sync.dma_start(out=out_rows[:, C, :], in_=done_c[:])
+        finish(wide("done_d0", None, HALF)[:], D, half(0), back_d[0][:], bases[D][:, half(0)])
+        done_d = wide("done_d1", None, HALF)
+        for q in range(2):
+            cols = slice(HALF + q * P, HALF + (q + 1) * P)
+            nc.vector.scalar_tensor_tensor(done_d[:, q * P : (q + 1) * P], back_d[1 + q][:], -STEP, bases[D][:, cols], ALU.mult, ALU.add)
+        nc.sync.dma_start(out=out_rows[:, D, half(1)], in_=done_d[:])

@@ -147,62 +147,61 @@ def tile_picked_elo8_none_p_kernel(
                     nc.sync.dma_start(out=results[b, g][:, cols], in_=res_rows[g][:, b, cols])
 
         whole = slice(0, S)
-        load_results(B, "w_raw0", [half(0), half(1)])
-        load_results(A, "grouped0_1", [whole])
-        load_results(C, "w_raw1", [whole])
-        load_results(D, "grouped1_1", [whole])
+        load_results(A, "w_raw0", [half(0), half(1)])
+        load_results(B, "grouped0_1", [whole])
+        load_results(D, "w_raw1", [whole])
+        load_results(C, "grouped1_1", [whole])
 
         def bank(name, number, width=S):
             return psum.tile([P, width], F32, name=name, tag="bank%d" % number)
+
+        def multiply(target, z, b, cols):
+            u, features = b // 2, slice(b % 2 * P, (b % 2 + 1) * P)
+            nc.tensor.matmul_mx(
+                out=target,
+                lhsT=w_codes[z, u][:, features].bitcast(FP8X4),
+                lhsT_scale=w_planes[z, u][:, features],
+                rhs=x_codes[z][:, cols].bitcast(FP8X4),
+                rhs_scale=x_planes[:, z * S + cols.start : z * S + cols.stop],
+                start=(z == 0),
+                stop=(z == PASSES - 1),
+            )
 
         pieces = [(b, h) for h in range(2) for b in range(PARTS)]
         ratings = {piece: bank("rating%d_%d" % piece, i, HALF) for i, piece in enumerate(pieces)}
         for z in range(PASSES):
             for b, h in pieces:
-                u, features = b // 2, slice(b % 2 * P, (b % 2 + 1) * P)
-                nc.tensor.matmul_mx(
-                    out=ratings[b, h][:],
-                    lhsT=w_codes[z, u][:, features].bitcast(FP8X4),
-                    lhsT_scale=w_planes[z, u][:, features],
-                    rhs=x_codes[z][:, half(h)].bitcast(FP8X4),
-                    rhs_scale=x_planes[:, z * S + h * HALF : z * S + (h + 1) * HALF],
-                    start=(z == 0),
-                    stop=(z == PASSES - 1),
-                )
+                multiply(ratings[b, h][:], z, b, half(h))
 
-        for b, h in pieces:
-            if b in (A, C):
-                nc.vector.tensor_copy(windows[b][:, half(h)], ratings[b, h][:])
-            else:
-                nc.scalar.copy(out=windows[b][:, half(h)], in_=ratings[b, h][:])
-
-        summed = [[wide("summed%d_%d" % (b, h), None, HALF) for h in range(2)] if b == A else wide("summed%d" % b) for b in range(PARTS)]
-        scaled = {b: wide("scaled%d" % b) for b in (B, C, D)}
-        bases = [wide("base%d" % b) for b in range(PARTS)]
+        summed = {b: wide("summed%d" % b) for b in (A, B, D)}
+        scaled = {}
+        bases = {b: wide("base%d" % b) for b in (A, B, D)}
 
         def add_results(b, cols):
             nc.gpsimd.tensor_tensor(summed[b][:, cols], results[b, 0][:, cols], results[b, 1][:, cols], ALU.add)
 
-        def scale_results(b, cols):
-            nc.gpsimd.tensor_scalar(scaled[b][:, cols], summed[b][:, cols], STEP, 0.0, ALU.mult, ALU.add)
+        def scale_results(b):
+            nc.gpsimd.tensor_scalar(scaled[b], summed[b][:], STEP, 0.0, ALU.mult, ALU.add)
 
-        def add_ratings(b, cols):
-            nc.gpsimd.tensor_tensor(bases[b][:, cols], scaled[b][:, cols], windows[b][:, cols], ALU.add)
+        def add_ratings(b):
+            nc.gpsimd.tensor_tensor(bases[b][:], scaled[b], windows[b][:, :S], ALU.add)
+
+        def base_from_bank(b, cols, product):
+            nc.vector.scalar_tensor_tensor(bases[b][:, cols], summed[b][:, cols], STEP, product, ALU.mult, ALU.add)
 
         for h in range(2):
-            add_results(B, half(h))
-        for h in range(2):
-            scale_results(B, half(h))
-        for h in range(2):
-            nc.gpsimd.tensor_tensor(summed[A][h][:], results[A, 0][:, half(h)], results[A, 1][:, half(h)], ALU.add)
-        add_ratings(B, whole)
-        add_results(C, whole)
+            add_results(A, half(h))
+
+        for b, h in pieces:
+            if (b, h) in ((B, 0), (A, 1), (C, 1)):
+                nc.vector.tensor_copy(windows[b][:, half(h)], ratings[b, h][:])
+            else:
+                nc.scalar.copy(out=windows[b][:, half(h)], in_=ratings[b, h][:])
+            if (b, h) == (B, 0):
+                base_from_bank(A, half(0), ratings[A, 0][:])
+
+        add_results(B, whole)
         add_results(D, whole)
-        scale_results(C, whole)
-        scale_results(D, whole)
-        add_ratings(C, whole)
-        for h in range(2):
-            add_ratings(D, half(h))
 
         def add_turned(target, values, first=False, final=False):
             chunks = target.shape[1] // P
@@ -242,71 +241,73 @@ def tile_picked_elo8_none_p_kernel(
 
         got_a0 = fetch(nc.vector, "got_a0", A, 0)
         got_b0 = fetch(nc.scalar, "got_b0", B, 0)
+        base_from_bank(A, half(1), ratings[A, 1][:])
         got_a1 = fetch(nc.vector, "got_a1", A, 1)
         got_b1 = fetch(nc.scalar, "got_b1", B, 1)
-        got_c0 = fetch(nc.vector, "got_c0", C, 0)
 
-        lead_a0 = open_lead("lead_a0", 1, A)
-        lead_a1 = open_lead("lead_a1", 2, A)
-        lead_b0 = open_lead("lead_b0", 3, B)
-        lead_b1 = open_lead("lead_b1", 5, B)
-        lead_d0 = open_lead("lead_d0", 7, D)
+        lead_a0, lead_a1, lead_b0 = bank("lead_a0", 1), bank("lead_a1", 2), bank("lead_b0", 3)
+        for h in range(2):
+            for lead, b in ((lead_a0, A), (lead_a1, A), (lead_b0, B)):
+                add_turned(lead[:, half(h)], windows[b][:, half(h)], first=(h == 0))
+        lead_b1 = open_lead("lead_b1", 0, B)
+        again_c = bank("again_c", 5)
+        for z in range(PASSES):
+            multiply(again_c[:], z, C, whole)
         add_turned(lead_a0, got_a0, final=True)
+        later = wide("later", "got_a0", 3 * S)
+        scaled[B], scaled[D], summed[C] = later[:, :S], later[:, S : 2 * S], later[:, 2 * S :]
+        scale_results(B)
+        scale_results(D)
+        add_ratings(B)
+        add_results(C, whole)
+        add_ratings(D)
         add_turned(lead_b0, got_b0, final=True)
+        got_c0 = fetch(nc.vector, "got_c0", C, 0, tag="got_b0")
         lead_c0 = open_lead("lead_c0", 6, C)
-        sum_a = bank("sum_a", 4, HALF)
-        add_turned(sum_a, summed[A][1], first=True, final=True)
-        add_turned(lead_a1, got_a1, final=True)
         add_turned(lead_b1, got_b1, final=True)
-        nc.vector.scalar_tensor_tensor(
-            bases[A][:, half(0)], summed[A][0][:], STEP, ratings[A, 0][:], ALU.mult, ALU.add
-        )
-        owed = wide("owed", None, HALF)
-        nc.vector.tensor_scalar(owed[:], sum_a[:], -1.0, None, ALU.mult)
-        got_c1 = fetch(nc.vector, "got_c1", C, 1, tag="summed0_1")
-        back_a = bank("back_a", 1)
+        got_c1 = fetch(nc.vector, "got_c1", C, 1, tag="got_b1")
+        add_turned(lead_a1, got_a1, final=True)
+        got_d1 = fetch(nc.vector, "got_d1", D, 1, tag="got_a1")
+        back_a = bank("back_a", 4)
         add_turned(back_a, squash("win_a0", lead_a0[:]), first=True)
-        add_turned(lead_c0, got_c0, final=True)
-        back_b = bank("back_b", 3)
+        lead_d0 = open_lead("lead_d0", 7, D)
+        back_b = bank("back_b", 1)
         add_turned(back_b, squash("win_b0", lead_b0[:]), first=True)
-        add_turned(back_a[:, half(1)], owed)
-        add_turned(back_a, squash("win_a1", lead_a1[:]), final=True)
+        add_turned(lead_c0, got_c0, final=True)
+        add_turned(back_b, squash("win_b1", lead_b1[:]), final=True)
         lead_c1 = open_lead("lead_c1", 0, C)
-        lead_d1 = [open_lead("lead_d1_%d" % h, number, D, half(h)) for h, number in enumerate((4, 2))]
+        add_turned(back_a, squash("win_a1", lead_a1[:]), final=True)
         add_turned(lead_c1, got_c1, final=True)
-        win_b1 = squash("win_b1", lead_b1[:])
+        lead_d1 = open_lead("lead_d1", 2, D)
         got_d0 = fetch(nc.scalar, "got_d0", D, 0, tag="win_a0")
-        done_a = wide("done_a")
-        nc.vector.scalar_tensor_tensor(done_a[:, half(0)], back_a[:, half(0)], -STEP, bases[A][:, half(0)], ALU.mult, ALU.add)
-        nc.vector.scalar_tensor_tensor(done_a[:, half(1)], back_a[:, half(1)], -STEP, windows[A][:, half(1)], ALU.mult, ALU.add)
-        nc.sync.dma_start(out=out_rows[:, A, :], in_=done_a[:])
-        got_d1 = [fetch(nc.vector, "got_d1_%d" % h, D, 1, h * HALF, (h + 1) * HALF, tag) for h, tag in enumerate(("owed", "win_a1"))]
-        add_turned(back_b, win_b1, final=True)
         add_turned(lead_d0, got_d0, final=True)
-        add_turned(lead_d1[0], got_d1[0], final=True)
-        back_c = [bank("back_c%d" % h, number, HALF) for h, number in enumerate((5, 1))]
-        win_c0 = squash("win_c0", lead_c0[:], "win_b0")
+        add_turned(lead_d1, got_d1, final=True)
+        finish(wide("done_a")[:], A, whole, back_a[:], bases[A][:])
+        after_a = wide("after_a", "win_a1", 2 * S)
+        bases[C] = after_a[:, S:]
+        finish(after_a[:, :S], B, whole, back_b[:], bases[B][:])
+        for h in range(2):
+            base_from_bank(C, half(h), again_c[:, half(h)])
+
+        back_c = [bank("back_c%d" % h, number, HALF) for h, number in enumerate((3, 6))]
+        win_c0 = squash("win_c0", lead_c0[:])
+        win_c1 = [squash("win_c1_%d" % h, lead_c1[:, half(h)]) for h in range(2)]
         for h in range(2):
             add_turned(back_c[h], win_c0[:, half(h)], first=True)
-        win_c1 = [squash("win_c1_%d" % h, lead_c1[:, half(h)]) for h in range(2)]
-        add_turned(back_c[0], win_c1[0], final=True)
-        add_turned(lead_d1[1], got_d1[1], final=True)
-        add_turned(back_c[1], win_c1[1], final=True)
-        finish(wide("done_b")[:], B, whole, back_b[:], bases[B][:])
+            add_turned(back_c[h], win_c1[h], final=True)
 
-        back_d = [bank("back_d0", 6, HALF), bank("back_d1", 0, P), bank("back_d2", 3, P)]
+        back_d = [bank("back_d0", 0, HALF), bank("back_d1", 4, P), bank("back_d2", 1, P)]
         add_turned(back_d[0], squash("win_d0_0", lead_d0[:, half(0)]), first=True)
-        add_turned(back_d[0], squash("win_d1_0", lead_d1[0][:]), final=True)
-        win_d0 = squash("win_d0_1", lead_d0[:, half(1)])
+        add_turned(back_d[0], squash("win_d1_0", lead_d1[:, half(0)]), final=True)
+        win_d0 = squash("win_d0_1", lead_d0[:, half(1)], "got_a1")
         for q in range(2):
             add_turned(back_d[1 + q], win_d0[:, q * P : (q + 1) * P], first=True)
         for q in range(2):
-            add_turned(back_d[1 + q], squash("win_d1_%d" % (1 + q), lead_d1[1][:, q * P : (q + 1) * P]), final=True)
+            cols = slice(HALF + q * P, HALF + (q + 1) * P)
+            add_turned(back_d[1 + q], squash("win_d1_%d" % (1 + q), lead_d1[:, cols]), final=True)
 
-        done_c = wide("done_c")
         for h in range(2):
-            nc.vector.scalar_tensor_tensor(done_c[:, half(h)], back_c[h][:], -STEP, bases[C][:, half(h)], ALU.mult, ALU.add)
-        nc.sync.dma_start(out=out_rows[:, C, :], in_=done_c[:])
+            finish(wide("done_c%d" % h, None, HALF)[:], C, half(h), back_c[h][:], bases[C][:, half(h)])
         finish(wide("done_d0", None, HALF)[:], D, half(0), back_d[0][:], bases[D][:, half(0)])
         done_d = wide("done_d1", None, HALF)
         for q in range(2):

@@ -111,11 +111,13 @@ def tile_picked_elo8_none_p_kernel(
                 )
                 cast(out=grouped[z, u][:].rearrange("p e c t -> p c e t"), in_=cast_from[:, u])
 
+        spans = [slice(0, P), slice(P, HALF), slice(HALF, S)]
+
         def gather_words(z):
-            for j0 in (0, HALF):
+            for cols in spans:
                 nc.vector.tensor_copy(
-                    x_codes[z][:, j0 : j0 + HALF],
-                    word_table[z][:].bitcast(U32).indirect(picks[:, j0 // STRIPE : (j0 + HALF) // STRIPE]),
+                    x_codes[z][:, cols],
+                    word_table[z][:].bitcast(U32).indirect(picks[:, cols.start // STRIPE : cols.stop // STRIPE]),
                 )
 
         cast_weights(0)
@@ -155,7 +157,7 @@ def tile_picked_elo8_none_p_kernel(
         def bank(name, number, width=S):
             return psum.tile([P, width], F32, name=name, tag="bank%d" % number)
 
-        def multiply(target, z, b, cols):
+        def multiply(target, z, b, cols, first=True, final=True):
             u, features = b // 2, slice(b % 2 * P, (b % 2 + 1) * P)
             nc.tensor.matmul_mx(
                 out=target,
@@ -163,15 +165,22 @@ def tile_picked_elo8_none_p_kernel(
                 lhsT_scale=w_planes[z, u][:, features],
                 rhs=x_codes[z][:, cols].bitcast(FP8X4),
                 rhs_scale=x_planes[:, z * S + cols.start : z * S + cols.stop],
-                start=(z == 0),
-                stop=(z == PASSES - 1),
+                start=(first and z == 0),
+                stop=(final and z == PASSES - 1),
             )
 
-        pieces = [(b, h) for h in range(2) for b in range(PARTS)]
-        ratings = {piece: bank("rating%d_%d" % piece, i, HALF) for i, piece in enumerate(pieces)}
+        sharing = [[(B, C, D), (A,)], [(A, C), (B, D)], [(B,), (A,), (D,), (C,)]]
+        pieces = [(i, parts) for i in range(len(spans)) for parts in sharing[i]]
+        ratings = {}
+        for number, (i, parts) in enumerate(pieces):
+            width = spans[i].stop - spans[i].start
+            shared = bank("rating%d" % number, number, width * len(parts))
+            for n, b in enumerate(parts):
+                ratings[b, i] = shared[:, n * width : (n + 1) * width]
         for z in range(PASSES):
-            for b, h in pieces:
-                multiply(ratings[b, h][:], z, b, half(h))
+            for i, parts in pieces:
+                for b in parts:
+                    multiply(ratings[b, i], z, b, spans[i], b == parts[0], b == parts[-1])
 
         summed = {b: wide("summed%d" % b) for b in (A, B, D)}
         scaled = {}
@@ -192,13 +201,15 @@ def tile_picked_elo8_none_p_kernel(
         for h in range(2):
             add_results(A, half(h))
 
-        for b, h in pieces:
-            if (b, h) in ((B, 0), (A, 1), (C, 1)):
-                nc.vector.tensor_copy(windows[b][:, half(h)], ratings[b, h][:])
-            else:
-                nc.scalar.copy(out=windows[b][:, half(h)], in_=ratings[b, h][:])
-            if (b, h) == (B, 0):
-                base_from_bank(A, half(0), ratings[A, 0][:])
+        for i, parts in pieces:
+            for b in parts:
+                if b == A or (b == C and i > 0):
+                    nc.vector.tensor_copy(windows[b][:, spans[i]], ratings[b, i])
+                else:
+                    nc.scalar.copy(out=windows[b][:, spans[i]], in_=ratings[b, i])
+            if (i, parts) == (1, (A, C)):
+                for early in range(2):
+                    base_from_bank(A, spans[early], ratings[A, early])
 
         add_results(B, whole)
         add_results(D, whole)
@@ -241,44 +252,44 @@ def tile_picked_elo8_none_p_kernel(
 
         got_a0 = fetch(nc.vector, "got_a0", A, 0)
         got_b0 = fetch(nc.scalar, "got_b0", B, 0)
-        base_from_bank(A, half(1), ratings[A, 1][:])
+        base_from_bank(A, half(1), ratings[A, 2])
         got_a1 = fetch(nc.vector, "got_a1", A, 1)
         got_b1 = fetch(nc.scalar, "got_b1", B, 1)
 
-        lead_a0, lead_a1, lead_b0 = bank("lead_a0", 1), bank("lead_a1", 2), bank("lead_b0", 3)
+        lead_a0, lead_a1, lead_b0 = bank("lead_a0", 0), bank("lead_a1", 1), bank("lead_b0", 2)
         for h in range(2):
             for lead, b in ((lead_a0, A), (lead_a1, A), (lead_b0, B)):
                 add_turned(lead[:, half(h)], windows[b][:, half(h)], first=(h == 0))
-        lead_b1 = open_lead("lead_b1", 0, B)
-        again_c = bank("again_c", 5)
+        lead_b1 = open_lead("lead_b1", 3, B)
+        again_c = bank("again_c", 4)
         for z in range(PASSES):
             multiply(again_c[:], z, C, whole)
         add_turned(lead_a0, got_a0, final=True)
-        later = wide("later", "got_a0", 3 * S)
+        add_turned(lead_b0, got_b0, final=True)
+        later = wide("later", "got_b0", 3 * S)
         scaled[B], scaled[D], summed[C] = later[:, :S], later[:, S : 2 * S], later[:, 2 * S :]
         scale_results(B)
         scale_results(D)
         add_ratings(B)
         add_results(C, whole)
         add_ratings(D)
-        add_turned(lead_b0, got_b0, final=True)
-        got_c0 = fetch(nc.vector, "got_c0", C, 0, tag="got_b0")
+        got_c0 = fetch(nc.vector, "got_c0", C, 0, tag="got_a0")
         lead_c0 = open_lead("lead_c0", 6, C)
         add_turned(lead_b1, got_b1, final=True)
         got_c1 = fetch(nc.vector, "got_c1", C, 1, tag="got_b1")
         add_turned(lead_a1, got_a1, final=True)
         got_d1 = fetch(nc.vector, "got_d1", D, 1, tag="got_a1")
-        back_a = bank("back_a", 4)
+        back_a = bank("back_a", 0)
         add_turned(back_a, squash("win_a0", lead_a0[:]), first=True)
         lead_d0 = open_lead("lead_d0", 7, D)
-        back_b = bank("back_b", 1)
+        back_b = bank("back_b", 2)
         add_turned(back_b, squash("win_b0", lead_b0[:]), first=True)
         add_turned(lead_c0, got_c0, final=True)
         add_turned(back_b, squash("win_b1", lead_b1[:]), final=True)
-        lead_c1 = open_lead("lead_c1", 0, C)
+        lead_c1 = open_lead("lead_c1", 3, C)
         add_turned(back_a, squash("win_a1", lead_a1[:]), final=True)
         add_turned(lead_c1, got_c1, final=True)
-        lead_d1 = open_lead("lead_d1", 2, D)
+        lead_d1 = open_lead("lead_d1", 1, D)
         got_d0 = fetch(nc.scalar, "got_d0", D, 0, tag="win_a0")
         add_turned(lead_d0, got_d0, final=True)
         add_turned(lead_d1, got_d1, final=True)
@@ -289,14 +300,14 @@ def tile_picked_elo8_none_p_kernel(
         for h in range(2):
             base_from_bank(C, half(h), again_c[:, half(h)])
 
-        back_c = [bank("back_c%d" % h, number, HALF) for h, number in enumerate((3, 6))]
+        back_c = [bank("back_c%d" % h, number, HALF) for h, number in enumerate((6, 0))]
         win_c0 = squash("win_c0", lead_c0[:])
         win_c1 = [squash("win_c1_%d" % h, lead_c1[:, half(h)]) for h in range(2)]
         for h in range(2):
             add_turned(back_c[h], win_c0[:, half(h)], first=True)
             add_turned(back_c[h], win_c1[h], final=True)
 
-        back_d = [bank("back_d0", 0, HALF), bank("back_d1", 4, P), bank("back_d2", 1, P)]
+        back_d = [bank("back_d0", 3, HALF), bank("back_d1", 2, P), bank("back_d2", 4, P)]
         add_turned(back_d[0], squash("win_d0_0", lead_d0[:, half(0)]), first=True)
         add_turned(back_d[0], squash("win_d1_0", lead_d1[:, half(0)]), final=True)
         win_d0 = squash("win_d0_1", lead_d0[:, half(1)], "got_a1")

@@ -227,13 +227,12 @@ def tile_picked_elo8_none_p_kernel(
                     is_transpose=True,
                 )
 
-        def fetch(engine, name, b, g, j0=0, j1=S, tag=None):
-            into = wide(name, tag, j1 - j0)
-            picked = windows[b][:].indirect(rivals[g][:, j0 // STRIPE : j1 // STRIPE])
+        def fetch(engine, into, b, g):
+            picked = windows[b][:].indirect(rivals[g][:])
             if engine is nc.vector:
-                nc.vector.tensor_scalar(into[:], picked, -1.0, 0.0, ALU.mult, ALU.add)
+                nc.vector.tensor_scalar(into, picked, -1.0, 0.0, ALU.mult, ALU.add)
             else:
-                nc.scalar.activation(out=into[:], in_=picked, func=ACT.Copy, scale=-1.0)
+                nc.scalar.activation(out=into, in_=picked, func=ACT.Copy, scale=-1.0)
             return into
 
         def open_lead(name, number, b, cols=whole):
@@ -250,11 +249,11 @@ def tile_picked_elo8_none_p_kernel(
             nc.vector.scalar_tensor_tensor(done, back, -STEP, base, ALU.mult, ALU.add)
             nc.sync.dma_start(out=out_rows[:, b, cols], in_=done)
 
-        got_a0 = fetch(nc.vector, "got_a0", A, 0)
-        got_b0 = fetch(nc.scalar, "got_b0", B, 0)
+        got_a0 = fetch(nc.vector, wide("got_a0")[:], A, 0)
+        got_b0 = fetch(nc.scalar, wide("got_b0")[:], B, 0)
         base_from_bank(A, half(1), ratings[A, 2])
-        got_a1 = fetch(nc.vector, "got_a1", A, 1)
-        got_b1 = fetch(nc.scalar, "got_b1", B, 1)
+        got_a1 = fetch(nc.vector, wide("got_a1")[:], A, 1)
+        got_b1 = fetch(nc.scalar, wide("got_b1")[:], B, 1)
 
         lead_a0, lead_a1, lead_b0 = bank("lead_a0", 0), bank("lead_a1", 1), bank("lead_b0", 2)
         for h in range(2):
@@ -266,19 +265,19 @@ def tile_picked_elo8_none_p_kernel(
             multiply(again_c[:], z, C, whole)
         add_turned(lead_a0, got_a0, final=True)
         add_turned(lead_b0, got_b0, final=True)
-        later = wide("later", "got_b0", 3 * S)
-        scaled[B], scaled[D], summed[C] = later[:, :S], later[:, S : 2 * S], later[:, 2 * S :]
+        later = wide("later", "got_a0", 4 * S)
+        scaled[B], scaled[D], summed[C] = later[:, :S], later[:, S : 2 * S], later[:, 2 * S : 3 * S]
         scale_results(B)
         scale_results(D)
         add_ratings(B)
         add_results(C, whole)
         add_ratings(D)
-        got_c0 = fetch(nc.vector, "got_c0", C, 0, tag="got_a0")
+        got_c0 = fetch(nc.vector, later[:, 3 * S :], C, 0)
         lead_c0 = open_lead("lead_c0", 6, C)
         add_turned(lead_b1, got_b1, final=True)
-        got_c1 = fetch(nc.vector, "got_c1", C, 1, tag="got_b1")
+        got_c1 = fetch(nc.vector, wide("got_c1", "got_b1")[:], C, 1)
         add_turned(lead_a1, got_a1, final=True)
-        got_d1 = fetch(nc.vector, "got_d1", D, 1, tag="got_a1")
+        got_d1 = fetch(nc.vector, wide("got_d1", "got_a1")[:], D, 1)
         back_a = bank("back_a", 0)
         add_turned(back_a, squash("win_a0", lead_a0[:]), first=True)
         lead_d0 = open_lead("lead_d0", 7, D)
@@ -290,7 +289,7 @@ def tile_picked_elo8_none_p_kernel(
         add_turned(back_a, squash("win_a1", lead_a1[:]), final=True)
         add_turned(lead_c1, got_c1, final=True)
         lead_d1 = open_lead("lead_d1", 1, D)
-        got_d0 = fetch(nc.scalar, "got_d0", D, 0, tag="win_a0")
+        got_d0 = fetch(nc.scalar, wide("got_d0", "win_a0")[:], D, 0)
         add_turned(lead_d0, got_d0, final=True)
         add_turned(lead_d1, got_d1, final=True)
         finish(wide("done_a")[:], A, whole, back_a[:], bases[A][:])

@@ -203,7 +203,7 @@ def tile_picked_elo8_none_p_kernel(
 
         for i, parts in pieces:
             for b in parts:
-                if b == A or (b == C and i > 0):
+                if b == A or (b, i) == (C, 1):
                     nc.vector.tensor_copy(windows[b][:, spans[i]], ratings[b, i])
                 else:
                     nc.scalar.copy(out=windows[b][:, spans[i]], in_=ratings[b, i])
@@ -249,9 +249,9 @@ def tile_picked_elo8_none_p_kernel(
             nc.vector.scalar_tensor_tensor(done, back, -STEP, base, ALU.mult, ALU.add)
             nc.sync.dma_start(out=out_rows[:, b, cols], in_=done)
 
+        base_from_bank(A, half(1), ratings[A, 2])
         got_a0 = fetch(nc.vector, wide("got_a0")[:], A, 0)
         got_b0 = fetch(nc.scalar, wide("got_b0")[:], B, 0)
-        base_from_bank(A, half(1), ratings[A, 2])
         got_a1 = fetch(nc.vector, wide("got_a1")[:], A, 1)
         got_b1 = fetch(nc.scalar, wide("got_b1")[:], B, 1)
 
@@ -260,9 +260,10 @@ def tile_picked_elo8_none_p_kernel(
             for lead, b in ((lead_a0, A), (lead_a1, A), (lead_b0, B)):
                 add_turned(lead[:, half(h)], windows[b][:, half(h)], first=(h == 0))
         lead_b1 = open_lead("lead_b1", 3, B)
-        again_c = bank("again_c", 4)
+        again_c = bank("again_c", 4, HALF)
         for z in range(PASSES):
-            multiply(again_c[:], z, C, whole)
+            multiply(again_c[:], z, C, half(0))
+        lead_c0 = open_lead("lead_c0", 6, C)
         add_turned(lead_a0, got_a0, final=True)
         add_turned(lead_b0, got_b0, final=True)
         later = wide("later", "got_a0", 4 * S)
@@ -273,14 +274,13 @@ def tile_picked_elo8_none_p_kernel(
         add_results(C, whole)
         add_ratings(D)
         got_c0 = fetch(nc.vector, later[:, 3 * S :], C, 0)
-        lead_c0 = open_lead("lead_c0", 6, C)
+        lead_d0 = open_lead("lead_d0", 5, D)
         add_turned(lead_b1, got_b1, final=True)
         got_c1 = fetch(nc.vector, wide("got_c1", "got_b1")[:], C, 1)
         add_turned(lead_a1, got_a1, final=True)
         got_d1 = fetch(nc.vector, wide("got_d1", "got_a1")[:], D, 1)
         back_a = bank("back_a", 0)
         add_turned(back_a, squash("win_a0", lead_a0[:]), first=True)
-        lead_d0 = open_lead("lead_d0", 7, D)
         back_b = bank("back_b", 2)
         add_turned(back_b, squash("win_b0", lead_b0[:]), first=True)
         add_turned(lead_c0, got_c0, final=True)
@@ -296,8 +296,8 @@ def tile_picked_elo8_none_p_kernel(
         after_a = wide("after_a", "win_a1", 2 * S)
         bases[C] = after_a[:, S:]
         finish(after_a[:, :S], B, whole, back_b[:], bases[B][:])
-        for h in range(2):
-            base_from_bank(C, half(h), again_c[:, half(h)])
+        base_from_bank(C, half(0), again_c[:])
+        base_from_bank(C, half(1), ratings[C, 2])
 
         back_c = [bank("back_c%d" % h, number, HALF) for h, number in enumerate((6, 0))]
         win_c0 = squash("win_c0", lead_c0[:])

@@ -46,10 +46,12 @@ def tile_picked_elo8_none_p_kernel(
             out=scale_table[:QUADRANT, :].bitcast(I32), in_=x_scales.rearrange("z r c -> r z c").bitcast(I32)
         )
         nc.sync.dma_start(picks[:], offs)
+        x_planes = keep.tile([P, PASSES * S], U8, name="x_planes", align_bytes=64)
+        windows = [keep.tile([P, 2 * S], F32, name="window%d" % b) for b in range(PARTS)]
+        nc.gpsimd.memset(x_planes[:].bitcast(I32), 0)
+        nc.gpsimd.memset(windows[B][:, S:], 0.0)
         nc.gpsimd.memset(scale_table[QUADRANT : 2 * QUADRANT, :].bitcast(I32), 0)
         nc.gpsimd.memset(scale_table[2 * QUADRANT :, :].bitcast(I32), 0)
-        x_planes = keep.tile([P, PASSES * S], U8, name="x_planes", align_bytes=64)
-        nc.gpsimd.memset(x_planes[:].bitcast(I32), 0)
 
         warm = keep.tile([P, 2], F32, name="warm")
         nc.vector.memset(warm[:, 0:1], 0.0)
@@ -75,9 +77,8 @@ def tile_picked_elo8_none_p_kernel(
         ident = keep.tile([P, P], F32, name="ident")
         make_identity(nc, ident[:])
 
-        windows = [keep.tile([P, 2 * S], F32, name="window%d" % b) for b in range(PARTS)]
-        for window in windows:
-            nc.gpsimd.memset(window[:, S:], 0.0)
+        for b in (A, C, D):
+            nc.gpsimd.memset(windows[b][:, S:], 0.0)
 
         picked_scales = keep.tile([P, S], U8, name="picked_scales", tag="picked_scales", align_bytes=64)
         nc.vector.tensor_copy(picked_scales[:], scale_table[:].indirect(picks[:]))
@@ -297,7 +298,6 @@ def tile_picked_elo8_none_p_kernel(
         bases[C] = after_a[:, S:]
         finish(after_a[:, :S], B, whole, back_b[:], bases[B][:])
         base_from_bank(C, half(0), again_c[:])
-        base_from_bank(C, half(1), ratings[C, 2])
 
         back_c = [bank("back_c%d" % h, number, HALF) for h, number in enumerate((6, 0))]
         win_c0 = squash("win_c0", lead_c0[:])
@@ -305,11 +305,14 @@ def tile_picked_elo8_none_p_kernel(
         for h in range(2):
             add_turned(back_c[h], win_c0[:, half(h)], first=True)
             add_turned(back_c[h], win_c1[h], final=True)
+        base_c = [bases[C][:, half(0)], wide("base_c1", "win_c1_0", HALF)[:]]
+        nc.vector.scalar_tensor_tensor(base_c[1], summed[C][:, half(1)], STEP, ratings[C, 2], ALU.mult, ALU.add)
 
-        back_d = [bank("back_d0", 3, HALF), bank("back_d1", 2, P), bank("back_d2", 4, P)]
+        back_d = [bank("back_d0", 3, HALF)]
         add_turned(back_d[0], squash("win_d0_0", lead_d0[:, half(0)]), first=True)
         add_turned(back_d[0], squash("win_d1_0", lead_d1[:, half(0)]), final=True)
         win_d0 = squash("win_d0_1", lead_d0[:, half(1)], "got_a1")
+        back_d.extend([bank("back_d1", 5, P), bank("back_d2", 4, P)])
         for q in range(2):
             add_turned(back_d[1 + q], win_d0[:, q * P : (q + 1) * P], first=True)
         for q in range(2):
@@ -317,7 +320,7 @@ def tile_picked_elo8_none_p_kernel(
             add_turned(back_d[1 + q], squash("win_d1_%d" % (1 + q), lead_d1[:, cols]), final=True)
 
         for h in range(2):
-            finish(wide("done_c%d" % h, None, HALF)[:], C, half(h), back_c[h][:], bases[C][:, half(h)])
+            finish(wide("done_c%d" % h, None, HALF)[:], C, half(h), back_c[h][:], base_c[h])
         finish(wide("done_d0", None, HALF)[:], D, half(0), back_d[0][:], bases[D][:, half(0)])
         done_d = wide("done_d1", None, HALF)
         for q in range(2):

from contextlib import ExitStack

import concourse.mybir as mybir
from concourse.masks import make_identity

K, T, S, N = 1024, 2048, 512, 512
FLOPS = 2 * K * N * S

F32 = mybir.dt.float32
BF16 = mybir.dt.bfloat16
I32 = mybir.dt.int32
U32 = mybir.dt.uint32
U16 = mybir.dt.uint16
U8 = mybir.dt.uint8
FP8X4 = mybir.dt.float8_e4m3fn_x4
ALU = mybir.AluOpType
ACT = mybir.ActivationFunctionType

P = 128
PACK = 4
PASSES = K // (P * PACK)
PARTS = N // P
HALF = S // 2
STRIPE = 16
QUADRANT = 32
SCALE_ROWS = 4
GAMES = 2
STEP = 0.75
A, B, C, D = range(PARTS)


def tile_picked_elo8_none_p_kernel(
    tc, x_words, x_scales, w1, res1, res2, offs, opp1, opp2, out
):
    nc = tc.nc
    with ExitStack() as ctx:
        lists = ctx.enter_context(tc.tile_pool(name="lists", bufs=1))
        keep = ctx.enter_context(tc.tile_pool(name="keep", bufs=1))
        psum = ctx.enter_context(tc.psum_pool(name="psum", bufs=1))

        picks = lists.tile([P, S // STRIPE], U16, name="picks")
        rivals = [lists.tile([P, S // STRIPE], U16, name="rivals%d" % g) for g in range(GAMES)]

        scale_table = keep.tile([P, T], U8, name="scale_table", tag="scale_table", align_bytes=64)
        nc.sync.dma_start(
            out=scale_table[:QUADRANT, :].bitcast(I32), in_=x_scales.rearrange("z r c -> r z c").bitcast(I32)
        )
        nc.sync.dma_start(picks[:], offs)
        x_planes = keep.tile([P, PASSES * S], U8, name="x_planes", align_bytes=64)
        windows = [keep.tile([P, 2 * S], F32, name="window%d" % b) for b in range(PARTS)]
        nc.gpsimd.memset(x_planes[:].bitcast(I32), 0)
        nc.gpsimd.memset(windows[B][:, S:], 0.0)
        nc.gpsimd.memset(scale_table[QUADRANT : 2 * QUADRANT, :].bitcast(I32), 0)
        nc.gpsimd.memset(scale_table[2 * QUADRANT :, :].bitcast(I32), 0)

        warm = keep.tile([P, 2], F32, name="warm")
        nc.vector.memset(warm[:, 0:1], 0.0)
        nc.scalar.activation(out=warm[:, 1:2], in_=warm[:, 0:1], func=ACT.Sigmoid)

        w_raw = [
            keep.tile([P, PACK, N], F32, name="w_raw%d" % z, tag="w_raw%d" % z, align_bytes=64)
            for z in range(PASSES)
        ]
        w_rows = w1.rearrange("(z p t) m -> z p t m", z=PASSES, t=PACK)
        nc.sync.dma_start(out=w_raw[0][:], in_=w_rows[0])
        nc.sync.dma_start(rivals[0][:], opp1)
        nc.sync.dma_start(rivals[1][:], opp2)
        nc.sync.dma_start(out=w_raw[1][:], in_=w_rows[1])

        def load_words(z, tag):
            table = keep.tile([P, T], I32, name="word_table%d" % z, tag=tag, align_bytes=64)
            nc.sync.dma_start(out=table[:], in_=x_words[z].rearrange("p n t -> p (n t)").bitcast(I32))
            return table

        word_table = [load_words(0, "word_table0")]

        ident = keep.tile([P, P], F32, name="ident")
        make_identity(nc, ident[:])

        for b in (A, C, D):
            nc.gpsimd.memset(windows[b][:, S:], 0.0)

        picked_scales = keep.tile([P, S], U8, name="picked_scales", tag="picked_scales", align_bytes=64)
        nc.vector.tensor_copy(picked_scales[:], scale_table[:].indirect(picks[:]))
        moved = PASSES * SCALE_ROWS
        for q in range(P // QUADRANT):
            nc.sync.dma_start(
                out=x_planes[QUADRANT * q : QUADRANT * q + SCALE_ROWS, :].bitcast(I32),
                in_=picked_scales[moved * q : moved * (q + 1), :].bitcast(I32),
            )
        word_table.append(load_words(1, "scale_table"))

        x_codes = [
            keep.tile([P, S], U32, name="x_codes%d" % z, tag="x_codes%d" % z, align_bytes=64) for z in range(PASSES)
        ]
        grouped, w_codes, w_planes = {}, {}, {}

        def quantize(z, u, tag):
            w_codes[z, u] = keep.tile([P, 2 * P], U32, name="w_codes%d_%d" % (z, u), tag=tag, align_bytes=64)
            w_planes[z, u] = keep.tile([P, 2 * P], U8, name="w_plane%d_%d" % (z, u), align_bytes=64)
            nc.vector.quantize_mx(
                out=w_codes[z, u][:].bitcast(FP8X4),
                scales=w_planes[z, u][:],
                in_=grouped[z, u][:].rearrange("p e c t -> p (e c t)"),
            )

        def cast_weights(z):
            cast_from = w_raw[z][:].rearrange("p t (c u e) -> p u c e t", u=2, e=2)
            for u, cast in enumerate((nc.vector.tensor_copy, nc.scalar.copy)):
                grouped[z, u] = keep.tile(
                    [P, 2, P, PACK], BF16, name="grouped%d_%d" % (z, u), tag="grouped%d_%d" % (z, u), align_bytes=64
                )
                cast(out=grouped[z, u][:].rearrange("p e c t -> p c e t"), in_=cast_from[:, u])

        spans = [slice(0, P), slice(P, HALF), slice(HALF, S)]

        def gather_words(z):
            for cols in spans:
                nc.vector.tensor_copy(
                    x_codes[z][:, cols],
                    word_table[z][:].bitcast(U32).indirect(picks[:, cols.start // STRIPE : cols.stop // STRIPE]),
                )

        cast_weights(0)
        quantize(0, 0, "w_codes0_0")
        quantize(0, 1, "w_codes0_1")
        cast_weights(1)
        quantize(1, 0, "w_codes1_0")
        gather_words(0)
        quantize(1, 1, "word_table0")
        gather_words(1)

        res_rows = [res.rearrange("(p b) j -> p b j", b=PARTS) for res in (res1, res2)]
        out_rows = out.rearrange("(p b) j -> p b j", b=PARTS)

        def wide(name, tag=None, width=S):
            return keep.tile([P, width], F32, name=name, tag=tag or name, align_bytes=64)

        def half(h):
            return slice(h * HALF, (h + 1) * HALF)

        results = {}

        def load_results(b, tag, pieces):
            both_games = wide("results%d" % b, tag, GAMES * S)
            for g in range(GAMES):
                results[b, g] = both_games[:, g * S : (g + 1) * S]
            for cols in pieces:
                for g in range(GAMES):
                    nc.sync.dma_start(out=results[b, g][:, cols], in_=res_rows[g][:, b, cols])

        whole = slice(0, S)
        load_results(A, "w_raw0", [half(0), half(1)])
        load_results(B, "grouped0_1", [whole])
        load_results(D, "w_raw1", [whole])
        load_results(C, "grouped1_1", [whole])

        def bank(name, number, width=S):
            return psum.tile([P, width], F32, name=name, tag="bank%d" % number)

        def multiply(target, z, b, cols, first=True, final=True):
            u, features = b // 2, slice(b % 2 * P, (b % 2 + 1) * P)
            nc.tensor.matmul_mx(
                out=target,
                lhsT=w_codes[z, u][:, features].bitcast(FP8X4),
                lhsT_scale=w_planes[z, u][:, features],
                rhs=x_codes[z][:, cols].bitcast(FP8X4),
                rhs_scale=x_planes[:, z * S + cols.start : z * S + cols.stop],
                start=(first and z == 0),
                stop=(final and z == PASSES - 1),
            )

        sharing = [[(B, C, D), (A,)], [(A, C), (B, D)], [(B,), (A,), (D,), (C,)]]
        pieces = [(i, parts) for i in range(len(spans)) for parts in sharing[i]]
        ratings = {}
        for number, (i, parts) in enumerate(pieces):
            width = spans[i].stop - spans[i].start
            shared = bank("rating%d" % number, number, width * len(parts))
            for n, b in enumerate(parts):
                ratings[b, i] = shared[:, n * width : (n + 1) * width]
        for z in range(PASSES):
            for i, parts in pieces:
                for b in parts:
                    multiply(ratings[b, i], z, b, spans[i], b == parts[0], b == parts[-1])

        summed = {b: wide("summed%d" % b) for b in (A, B, D)}
        scaled = {}
        bases = {b: wide("base%d" % b) for b in (A, B, D)}

        def add_results(b, cols):
            nc.gpsimd.tensor_tensor(summed[b][:, cols], results[b, 0][:, cols], results[b, 1][:, cols], ALU.add)

        def scale_results(b):
            nc.gpsimd.tensor_scalar(scaled[b], summed[b][:], STEP, 0.0, ALU.mult, ALU.add)

        def add_ratings(b):
            nc.gpsimd.tensor_tensor(bases[b][:], scaled[b], windows[b][:, :S], ALU.add)

        def base_from_bank(b, cols, product):
            nc.vector.scalar_tensor_tensor(bases[b][:, cols], summed[b][:, cols], STEP, product, ALU.mult, ALU.add)

        for h in range(2):
            add_results(A, half(h))

        for i, parts in pieces:
            for b in parts:
                if b == A or (b, i) == (C, 1):
                    nc.vector.tensor_copy(windows[b][:, spans[i]], ratings[b, i])
                else:
                    nc.scalar.copy(out=windows[b][:, spans[i]], in_=ratings[b, i])
            if (i, parts) == (1, (A, C)):
                for early in range(2):
                    base_from_bank(A, spans[early], ratings[A, early])

        add_results(B, whole)
        add_results(D, whole)

        def add_turned(target, values, first=False, final=False):
            chunks = target.shape[1] // P
            for c in range(chunks):
                cols = slice(c * P, (c + 1) * P)
                nc.tensor.matmul(
                    target[:, cols],
                    values[:, cols],
                    ident[:],
                    start=(first and c == 0),
                    stop=(final and c == chunks - 1),
                    is_transpose=True,
                )

        def fetch(engine, into, b, g):
            picked = windows[b][:].indirect(rivals[g][:])
            if engine is nc.vector:
                nc.vector.tensor_scalar(into, picked, -1.0, 0.0, ALU.mult, ALU.add)
            else:
                nc.scalar.activation(out=into, in_=picked, func=ACT.Copy, scale=-1.0)
            return into

        def open_lead(name, number, b, cols=whole):
            lead = bank(name, number, cols.stop - cols.start)
            add_turned(lead, windows[b][:, cols], first=True)
            return lead

        def squash(name, gap, tag=None):
            win = wide(name, tag, gap.shape[1])
            nc.scalar.activation(out=win[:], in_=gap, func=ACT.Sigmoid)
            return win

        def finish(done, b, cols, back, base):
            nc.vector.scalar_tensor_tensor(done, back, -STEP, base, ALU.mult, ALU.add)
            nc.sync.dma_start(out=out_rows[:, b, cols], in_=done)

        base_from_bank(A, half(1), ratings[A, 2])
        got_a0 = fetch(nc.vector, wide("got_a0")[:], A, 0)
        got_b0 = fetch(nc.scalar, wide("got_b0")[:], B, 0)
        got_a1 = fetch(nc.vector, wide("got_a1")[:], A, 1)
        got_b1 = fetch(nc.scalar, wide("got_b1")[:], B, 1)

        lead_a0, lead_a1, lead_b0 = bank("lead_a0", 0), bank("lead_a1", 1), bank("lead_b0", 2)
        for h in range(2):
            for lead, b in ((lead_a0, A), (lead_a1, A), (lead_b0, B)):
                add_turned(lead[:, half(h)], windows[b][:, half(h)], first=(h == 0))
        lead_b1 = open_lead("lead_b1", 3, B)
        again_c = bank("again_c", 4, HALF)
        for z in range(PASSES):
            multiply(again_c[:], z, C, half(0))
        lead_c0 = open_lead("lead_c0", 6, C)
        add_turned(lead_a0, got_a0, final=True)
        add_turned(lead_b0, got_b0, final=True)
        later = wide("later", "got_a0", 4 * S)
        scaled[B], scaled[D], summed[C] = later[:, :S], later[:, S : 2 * S], later[:, 2 * S : 3 * S]
        scale_results(B)
        scale_results(D)
        add_ratings(B)
        add_results(C, whole)
        add_ratings(D)
        got_c0 = fetch(nc.vector, later[:, 3 * S :], C, 0)
        lead_d0 = open_lead("lead_d0", 5, D)
        add_turned(lead_b1, got_b1, final=True)
        got_c1 = fetch(nc.vector, wide("got_c1", "got_b1")[:], C, 1)
        add_turned(lead_a1, got_a1, final=True)
        got_d1 = fetch(nc.vector, wide("got_d1", "got_a1")[:], D, 1)
        back_a = bank("back_a", 0)
        add_turned(back_a, squash("win_a0", lead_a0[:]), first=True)
        back_b = bank("back_b", 2)
        add_turned(back_b, squash("win_b0", lead_b0[:]), first=True)
        add_turned(lead_c0, got_c0, final=True)
        add_turned(back_b, squash("win_b1", lead_b1[:]), final=True)
        lead_c1 = open_lead("lead_c1", 3, C)
        add_turned(back_a, squash("win_a1", lead_a1[:]), final=True)
        add_turned(lead_c1, got_c1, final=True)
        lead_d1 = open_lead("lead_d1", 1, D)
        got_d0 = fetch(nc.scalar, wide("got_d0", "win_a0")[:], D, 0)
        add_turned(lead_d0, got_d0, final=True)
        add_turned(lead_d1, got_d1, final=True)
        finish(wide("done_a")[:], A, whole, back_a[:], bases[A][:])
        after_a = wide("after_a", "win_a1", 2 * S)
        bases[C] = after_a[:, S:]
        finish(after_a[:, :S], B, whole, back_b[:], bases[B][:])
        base_from_bank(C, half(0), again_c[:])

        back_c = [bank("back_c%d" % h, number, HALF) for h, number in enumerate((6, 0))]
        win_c0 = squash("win_c0", lead_c0[:])
        win_c1 = [squash("win_c1_%d" % h, lead_c1[:, half(h)]) for h in range(2)]
        for h in range(2):
            add_turned(back_c[h], win_c0[:, half(h)], first=True)
            add_turned(back_c[h], win_c1[h], final=True)
        base_c = [bases[C][:, half(0)], wide("base_c1", "win_c1_0", HALF)[:]]
        nc.vector.scalar_tensor_tensor(base_c[1], summed[C][:, half(1)], STEP, ratings[C, 2], ALU.mult, ALU.add)

        back_d = [bank("back_d0", 3, HALF)]
        add_turned(back_d[0], squash("win_d0_0", lead_d0[:, half(0)]), first=True)
        add_turned(back_d[0], squash("win_d1_0", lead_d1[:, half(0)]), final=True)
        win_d0 = squash("win_d0_1", lead_d0[:, half(1)], "got_a1")
        back_d.extend([bank("back_d1", 5, P), bank("back_d2", 4, P)])
        for q in range(2):
            add_turned(back_d[1 + q], win_d0[:, q * P : (q + 1) * P], first=True)
        for q in range(2):
            cols = slice(HALF + q * P, HALF + (q + 1) * P)
            add_turned(back_d[1 + q], squash("win_d1_%d" % (1 + q), lead_d1[:, cols]), final=True)

        for h in range(2):
            finish(wide("done_c%d" % h, None, HALF)[:], C, half(h), back_c[h][:], base_c[h])
        finish(wide("done_d0", None, HALF)[:], D, half(0), back_d[0][:], bases[D][:, half(0)])
        done_d = wide("done_d1", None, HALF)
        for q in range(2):
            cols = slice(HALF + q * P, HALF + (q + 1) * P)
            nc.vector.scalar_tensor_tensor(done_d[:, q * P : (q + 1) * P], back_d[1 + q][:], -STEP, bases[D][:, cols], ALU.mult, ALU.add)
        nc.sync.dma_start(out=out_rows[:, D, half(1)], in_=done_d[:])
